import numpy as np, ml_dtypes
CORES = [83,85,87,115,117,119]
N = 6
BF = ml_dtypes.bfloat16
W, SV, M, HOPS = 4096, 512, 192, [1, 2, 3]
RO = len(HOPS) + 1
def names(rng, power, *shape):
    return np.minimum((W * rng.random(shape) ** power).astype(np.int64), W - 1)
def pairs(rng, C, power):
    a = names(rng, power, N, 8, 16, C); b = np.take_along_axis(a, np.argsort(rng.random((N, 8, 16, C)), axis=2), 2)
    share = rng.choice(np.array([0.0, 0.15, 0.5, 1.0]), (N, 8, 1, C)); b = np.where(rng.random(b.shape) < share, b, names(rng, power, N, 8, 16, C))
    fa = rng.choice(np.array([0.05, 0.12, 0.3, 0.7, 1.0]), (N, 8, 1, C), p=[0.2, 0.25, 0.2, 0.2, 0.15])
    fb = rng.choice(np.array([0.0, 0.3, 0.7, 1.0]), (N, 8, 1, C), p=[0.05, 0.25, 0.3, 0.4])
    return np.where(rng.random(a.shape) < fa, a, -1), np.where(rng.random(b.shape) < fb, b, -1)
def parts(rng, power):
    clk = rng.integers(0, 256, (N, 8, 16, W)); z = rng.integers(0, 256, (N, 8, 16, M)); th = rng.integers(1200, 1600, (N, 8))
    sc, st = pairs(rng, SV, power); d, t = pairs(rng, M, power)
    return clk, sc, st, d, t, z, th
def pack(clk, sc, st, d, t, z, th):
    return {"clk": clk.reshape(N, 128, W).astype(np.float32).astype(BF), "sc": sc.reshape(N, 128, SV).astype(np.int32), "st": st.reshape(N, 128, SV).astype(np.int32),
            "dl": d.reshape(N, 128, M).astype(np.int32), "tl": t.reshape(N, 128, M).astype(np.int32), "z0": z.reshape(N, 128, M).astype(np.float32).astype(BF),
            "th": np.repeat(th.reshape(N, 8), 16, axis=1).reshape(N, 128, 1).astype(np.int32)}
def setup_inputs(rng):
    return pack(*parts(rng, 1))
def setup_inputs_spread(rng):
    clk, sc, st, d, t, z, th = parts(rng, 4)
    clk = np.floor(np.exp2(8 * rng.random((N, 8, 1, W))) * rng.random((N, 8, 16, W))).astype(np.int64)
    z = np.floor(np.exp2(8 * rng.random((N, 8, 1, M))) * rng.random((N, 8, 16, M))).astype(np.int64)
    th = np.minimum(np.floor(np.exp2(12 * rng.random((N, 8)))).astype(np.int64), 4080)
    return pack(np.minimum(clk, 255), sc, st, d, t, np.minimum(z, 255), th)
def setup_inputs_ends(rng):
    def rec(C):
        p = rng.choice(np.array([0.0, 0.06, 0.5, 1.0]), (N, 8, 1, C)); s = (N, 8, 16, C)
        a = np.where(rng.random(s) < p, W - 1, -1)
        o = np.where(rng.random(s) < 0.3, -1, np.where(rng.random(s) < 0.15, W - 1, rng.integers(0, W, s)))
        return np.where(rng.random((N, 8, 1, C)) < 0.6, a, o)
    def half(C):
        k = rng.integers(0, 3, (N, 8, 1, C))
        return np.where(k == 0, 0, np.where(k == 1, 255, 255 * rng.integers(0, 2, (N, 8, 16, C))))
    clk = half(W); z = half(M); sc = rec(SV); st = rec(SV); d = rec(M); t = rec(M)
    g = np.arange(8)[None, :]; q = np.arange(N)[:, None]
    clk[..., 0] = 255; clk[..., W - 1] = np.where(((g + q + N) & 1) == 0, 255, 0)[:, :, None]
    clk[..., W - 2] = 255; clk[:, :, 15, W - 2] = 254
    z[..., 0] = 255; z[..., M - 1] = 255; z[..., M - 2] = 0
    th = 4080 * ((g // 2 + q + rng.integers(0, 2, (N, 1))) & 1); th[:, 5] = 4080
    for m, lo, hi in ((M - 1, 0, W - 1), (0, W - 1, 0)):
        d[..., m] = -1; d[:, :, 15, m] = W - 1; d[:, :, 4, m] = 5; t[..., m] = -1; t[:, :, 2, m] = lo; t[:, :, 15, m] = hi
    s = slice(M - 6, M - 2); z[..., s] = 255; d[:, :, 15, s] = W - 1; t[..., s] = -1; t[:, :, 2, s] = W - 2; t[:, :, 15, s] = 0
    d[:, 5] = W - 1; t[:, 5] = W - 1; sc[:, 5] = W - 1; st[:, 5] = W - 1; z[:, 5] = z[:, 5, :1]
    return pack(clk, sc, st, d, t, z, th)
def setup_inputs_corners(rng):
    clk, sc, st, d, t, z, th = parts(rng, 1)
    clk[:, 1::2, :, 1::2] = clk[:, 1::2, :, 0::2]
    th = rng.choice(np.array([0, 1, 126, 128, 1000, 1999, 4080]), (N, 8)); th[:, 0] = 1000; th[:, 7] = 1999; th[:, 3] = 0
    th[:, 5] = 2051 + 4 * rng.integers(0, 100, N); th[:, 6] = 2052 + 4 * rng.integers(0, 100, N)
    lanes = np.array([0, 1, SV - 1, SV, W - 2, W - 1])
    for q in range(N):
        for g in range(8):
            kind = rng.permutation(M) % 10; n = np.where(rng.random(M) < 0.5, rng.choice(lanes, M), rng.integers(0, W, M)); full = rng.integers(0, W, (16, M))
            D = d[q, g]; T = t[q, g]; x = clk[q, g][:, n]; room = np.maximum(x, 255 - x)
            gap = np.maximum(int(th[q, g]) + rng.integers(-1, 2, M), 0); step = np.clip(gap[None, :] - (np.add.accumulate(room, axis=0) - room), 0, room)
            near = np.where(x < 128, x + step, x - step)
            s = kind == 0; D[:, s] = -1; T[:, s] = -1; T[15, s] = n[s]
            s = kind == 1; D[:, s] = -1; T[:, s] = -1
            s = kind == 2; D[:, s] = full[:, s]; T[:, s] = -1
            s = kind == 3; D[:, s] = full[:, s]; T[:, s] = full[::-1][:, s]
            s = kind == 4; D[:, s] = n[s]; T[:, s] = -1; T[15, s] = n[s]
            s = kind == 5; D[:, s] = full[:, s] & ~1; T[:, s] = full[::-1][:, s] | 1
            s = kind == 6; D[:, s] = -1; D[15, s] = n[s]; T[:, s] = -1; T[0, s] = n[s]
            s = kind == 7; D[:, s] = -1; D[0, s] = n[s]; T[:, s] = -1; T[15, s] = n[s] ^ 1
            s = kind == 8; D[:, s] = -1; D[7, s] = n[s]; D[8, s] = (n[s] + 5) % W; T[:, s] = -1; T[15, s] = n[s]; T[3, s] = n[s] ^ 1
            s = kind == 9; D[:, s] = n[s]; D[0, s] = n[s] ^ 1; T[:, s] = n[s]
            s = (kind == 4) | (kind == 6) | (kind == 8) | (kind == 9); z[q, g][:, s] = near[:, s]
    k = rng.integers(0, 6, (N, 8, 1, SV)); more = rng.integers(0, W, (2, N, 8, 16, SV))
    st = np.where(k == 4, sc[:, :, ::-1], st)
    sc = np.where((k == 0) | (k == 2), -1, np.where(k == 1, more[0], sc)); st = np.where((k == 0) | (k == 3), -1, np.where(k == 1, more[1], st))
    return pack(clk, sc, st, d, t, z, th)
def setup_inputs_crowd(rng):
    clk, sc, st, d, t, z, th = parts(rng, 1); h = SV >> 1
    def high(*shape):
        return h + rng.integers(0, h - 1, shape) + SV * rng.integers(0, W // SV, shape)
    for q in range(N):
        for g in (0, 1):
            keep = d[q, g, :, M - 1].copy(), z[q, g, :, M - 1].copy()
            z[q, g] = rng.permuted(np.repeat(rng.integers(0, 256, (16, 1)), M, axis=1), axis=0); t[q, g] = -1
            if g == 1: d[q, g, :, M - 1], z[q, g, :, M - 1] = keep; t[q, g, 15, M - 1] = W - 1
        for g in (2, 3):
            v = int(rng.choice(np.array([0, SV - 1, SV >> 1]))); n = v + SV * rng.integers(0, W // SV, (16, M))
            t[q, g] = np.where(rng.random((16, M)) < 0.5, n, -1); t[q, g, 9] = n[9]; d[q, g] = -1
            if g == 3: d[q, g, 15, M - 1] = (v + 1) % W
        for g in (6, 7):
            n = rng.integers(0, W, M); z[q, g] = clk[q, g][:, n]; t[q, g, 5] = n
            d[q, g] = -1; d[q, g, 15] = n
            if g == 7: d[q, g, 15, M - 1] = -1
    for g, c, lim in ((4, 20, 219), (5, 35, 212)):
        clk[:, g] = rng.integers(0, 8, (N, 16, W)); clk[:, g, :, W - 1] = c
        d[:, g] = high(N, 16, M); t[:, g] = rng.permuted(d[:, g], axis=1)
        sc[:, g, :, :h] = high(N, 16, h); st[:, g, :, :h] = rng.permuted(sc[:, g, :, :h], axis=1)
        z[:, g] = rng.integers(0, 7, (N, 16, M))
        for q in range(N):
            z[q, g, :, M - 1] = 6 + (np.arange(16) < 4 + q)
            b = (q + int(np.sum(HOPS[:-1]))) % N; sc[b, g, :, 100 + q] = W - 1; st[b, g, :, 100 + q] = W - 1
            th[(b + HOPS[-1]) % N, g] = lim - q
    d[:, 5, 15, 0] = -1
    return pack(clk, sc, st, d, t, z, th)
def check_inputs(d):
    bad = []
    for k, lo, hi in (("clk", 0, 255), ("z0", 0, 255), ("sc", -1, W - 1), ("st", -1, W - 1), ("dl", -1, W - 1), ("tl", -1, W - 1), ("th", 0, 4080)):
        a = np.asarray(d[k]).astype(np.float64)
        if not (np.min(a) >= lo and np.max(a) <= hi): bad.append("range of " + k)
        elif np.any(a != np.floor(a)): bad.append("whole numbers in " + k)
    h = np.asarray(d["th"]).reshape(-1, 16)
    if np.any(h != h[:, :1]): bad.append("th alike in a group")
    return bad
def reference(clk, sc, st, dl, tl, z0, th):
    X = clk.astype(np.float32).astype(np.int64).reshape(N, 8, 16, W); Z = z0.astype(np.float32).astype(np.int64).reshape(N, 8, 16, M)
    C = sc.astype(np.int64).reshape(N, 8, 16, SV); S = st.astype(np.int64).reshape(N, 8, 16, SV)
    D = dl.astype(np.int64).reshape(N, 8, 16, M); T = tl.astype(np.int64).reshape(N, 8, 16, M)
    base = th.astype(np.int64).reshape(N, 8, 16)[:, :, 0]; A = np.zeros((N, 8), np.int64); row = np.arange(16).reshape(1, 16, 1)
    for visit in range(RO):
        nd, nt, nz = [], [], []
        for a in range(N):
            d, t, z = D[a], T[a], Z[a]
            x = np.take_along_axis(X[a], np.maximum(d, 0).reshape(8, 1, 16 * M), 2).reshape(8, 16, 16, M)
            y = np.take_along_axis(X[a], np.maximum(t, 0).reshape(8, 1, 16 * M), 2).reshape(8, 16, 16, M)
            dist = np.sum(np.abs(x - z[:, :, None, :]), axis=1)
            score = np.where(t >= 0, np.sum(np.minimum(y, z[:, :, None, :]), axis=1), -1)
            ks = np.argmax(score, axis=1)
            has = np.any(t >= 0, axis=1); v = np.take_along_axis(t, ks[:, None, :], 1)[:, 0] & (SV - 1)
            eq = (d[:, :, None, :] == t[:, None, :, :]) & (d >= 0)[:, :, None, :]
            cd = np.any(eq, axis=2); ct = np.any(eq, axis=1)
            lim = base[a] + 8 * (A[a] & 31)
            abort = np.any(cd & (dist > lim[:, None, None]), axis=1)
            d1 = np.where(cd, -1, d); t1 = np.where(ct | (row == ks[:, None, :]), -1, t)
            left = np.any(d1 >= 0, axis=1); proof = has & ~abort & ~left; go = has & ~abort & left
            yk = np.take_along_axis(y, ks[:, None, None, :], 2)[:, :, 0]
            top = np.max(np.where((d1 >= 0)[:, None, :, :], x, 0), axis=2)
            cv = np.take_along_axis(C[a], v[:, None, :], 2); sv = np.take_along_axis(S[a], v[:, None, :], 2)
            u = np.sum(z, axis=1) & (SV - 1)
            cu = np.take_along_axis(C[a], u[:, None, :], 2); su = np.take_along_axis(S[a], u[:, None, :], 2)
            hd = np.any(cv[:, :, None, :] == d[:, None, :, :], axis=2); ht = np.any(sv[:, :, None, :] == t[:, None, :, :], axis=2)
            d2 = np.where((d1 < 0) & ~hd, cv, d1); t2 = np.where((t1 < 0) & ~ht, sv, t1)
            ab = abort[:, None, :]; on = go[:, None, :]
            nd.append(np.where(ab, cv, np.where(on, d2, cu))); nt.append(np.where(ab, sv, np.where(on, t2, su)))
            nz.append(np.where(ab, np.abs(z - yk), np.where(on, (yk + top) >> 1, z)))
            A[a] += np.sum(cd & ~ab, axis=(1, 2))
            for g in range(8):
                for m in np.nonzero(proof[g])[0]: C[a, g, :, v[g, m]] = t1[g, :, m]
        D, T, Z = np.stack(nd), np.stack(nt), np.stack(nz)
        if visit < RO - 1: D, T, Z = [np.roll(b, HOPS[visit], axis=0) for b in (D, T, Z)]
    return {"yd": D.reshape(N, 128, M).astype(np.float32), "yt": T.reshape(N, 128, M).astype(np.float32), "yz": Z.reshape(N, 128, M).astype(np.float32), "ys": C.reshape(N, 128, SV).astype(np.float32)}

@@ -1,0 +1,490 @@
+import numpy as np
+from concourse.mybir import dt, AluOpType as A, ActivationFunctionType as F
+
+N = 6
+HOPS = [1, 2, 3]
+M, C, NC = 192, 96, 6
+L = 16 * C
+BIG = 30000.0
+
+H, BF, F4, I4, U2 = "float16", "bfloat16", "float32", "int32", "uint16"
+PER = {
+    "OFF": (U2, 192), "OFX": (U2, 96), "OFN": (U2, 8), "LI": (I4, 192), "KI": (I4, 8),
+    "ZSS": (BF, L), "ZE": (H, L), "MT": (H, L), "SD": (H, L), "AD": (H, L), "XT": (H, L), "TP": (H, L),
+    "EQ0": (H, L), "EQ1": (H, L), "EQ2": (H, L), "CX": (H, 3 * L),
+    "FL": (H, 192), "QL": (H, 8), "OH": (H, 96), "TH": (H, 96), "NH": (H, 96),
+    "CS": (H, 192), "CT": (H, 192), "YK": (H, 96), "F1": (H, 96), "FAR": (H, 96),
+    "DT1": (H, 192), "FD1": (H, 192), "HC": (H, 192), "P1": (H, 192), "P2": (H, 192), "P3": (H, 192),
+    "ZA": (H, 96), "ZA2": (H, 96), "ZG": (H, 96), "ZGI": (H, 96), "ZG2": (H, 96), "ZR": (H, 96),
+    "FIN": (H, 288), "FSG": (H, 192), "FNE": (H, 192), "TSG": (H, 96), "TNE": (H, 96),
+    "MX": (F4, 96), "JK": (F4, 96), "T1": (I4, 192), "OUT": (F4, 288), "TD": (F4, 96),
+}
+ONE = {
+    "SEL": (BF, 2048), "GG": (BF, 2048), "ON1": (BF, 2048),
+    "ID": (BF, 128), "IDN": (BF, 128), "I1K": (BF, 128), "INK": (BF, 128), "I8K": (BF, 128), "I2K": (BF, 128), "IH": (BF, 128), "IHN": (BF, 128),
+    "BK": (BF, 128), "BKN": (BF, 128), "B32": (BF, 128), "BNK": (BF, 128), "B3K": (BF, 128), "BKC": (BF, 128),
+    "RST0": (BF, L), "RSTB": (BF, L), "RSTN": (BF, NC * C), "AK": (BF, 2 * NC * C), "SM": (BF, 2 * NC * C), "PCN": (H, 96), "TBC": (H, 96), "MC": (H, 96), "Z0": (BF, 192),
+    "RSTM": (BF, NC * C), "PRF": (H, 192), "CH": (F4, 8),
+    "IA": (I4, 96), "IB": (I4, 96), "IC": (I4, 96), "R6": (I4, 16), "C6": (I4, 16), "CM": (I4, 96),
+    "CL": (F4, 16), "C2": (F4, 16), "THR": (I4, 8), "NTH": (F4, 8), "NLIM": (F4, 8), "ACN": (F4, 8), "AS": (F4, 8), "AI": (I4, 8), "AI2": (I4, 8),
+    "VI": (I4, 24), "VI2": (I4, 24), "OFV": (U2, 24), "OFW": (U2, 16), "VL": (H, 16), "KB": (F4, 16), "WN": (F4, 16), "WN2": (F4, 16), "DV": (F4, 16), "WO": (F4, 16), "WO2": (F4, 16),
+    "SI": (I4, 1024), "SA": (I4, 1024), "SE": (H, 512), "SG": (H, 512), "SNE": (H, 512),
+}
+WHERE = {}
+_tot = {}
+for _n, (_d, _w) in [(n + str(h), x) for n, x in PER.items() for h in (0, 1)] + list(ONE.items()):
+    WHERE[_n] = (_d, _tot.get(_d, 0), _w)
+    _tot[_d] = _tot.get(_d, 0) + (_w + 15) // 16 * 16
+
+SCRATCH = {"p_" + _d: ("sbuf", [128, _w], _d) for _d, _w in _tot.items()}
+SCRATCH["tab"] = ("sbuf", [128, 4112], BF)
+for _n in ("scw", "stw", "sow"):
+    SCRATCH[_n] = ("sbuf", [128, 608], F4)
+for _h in (0, 1):
+    for _t in range(4):
+        SCRATCH["m%d%d" % (_t, _h)] = ("sbuf", [128, 288], H)
+        if _t < 3:
+            SCRATCH["o%d%d" % (_t, _h)] = ("sbuf", [128, 288], H)
+for _b in ("cm0", "cm1", "cm2", "pk", "pc", "ph", "px", "pm"):
+    SCRATCH[_b] = ("psum", [128, 512], F4)
+NLOAD, NOUT = 10, 7
+SEMAPHORES = ["v", "s", "t", "g", "loc"] + ["l%d" % i for i in range(NLOAD)] + ["a%d%d" % (t, h) for t in (1, 2, 3) for h in (0, 1)] + ["out%d" % i for i in range(NOUT)]
+
+K = {"v": 1.0e-3, "t": 0.5e-3, "fix": 0.06, "wake": 0.08, "gat": 1.56, "hop": 3.5}
+SHIFTS = [5006, 5008, 5010, 5013, 5017, 5019, 5035, 5038, 5042, 5063, 5066, 5075, 5094, 5123, 5134, 5148, 5158, 5187, 5195, 5231, 5237, 5239, 6032, 6046, 6070, 6071, 6085,
+          6120, 6123, 6137, 6150, 6168, 6174, 6184, 6186, 6210, 6227, 16018, 16022, 16053, 16073, 16078, 16083, 16115, 16117, 16202, 16229, 16235, 25045, 25064, 25090, 25179,
+          25225, 25247, 25289, 25321, 25341, 31031, 31038, 31054, 31071, 31148, 31193, 31212, 31214, 31231, 31273, 31323, 36017, 36080, 36087, 36089, 36159, 36209, 36242, 36297,
+          36305, 46081, 46129, 46160, 46232]
+def cv(n, k=1.0): return K["fix"] + K["v"] * max(64, n * k)
+def ct(*ns): return sum(K["t"] * max(64, n) for n in ns) + 0.03
+
+MODES = ["SV", "SV", "SV", "SV", "SV", "SS"]
+NENG = 8
+PLAN = {}
+
+
+def build(T):
+    ops = []
+    now = [0]
+
+    def B(name, lo=0, hi=None, step=1):
+        d, a, w = WHERE[name]
+        hi = w if hi is None else hi
+        t = T["p_" + d]
+        return t[:, a + lo:a + hi] if step == 1 else t[:, a + lo:a + hi:step]
+
+    def op(eng, rd, wr, cost, fn, banks=(), lat=0.0, sem=None, val=1, get=None, put=None):
+        ops.append(dict(h=now[0], e=eng, r=rd.split(), w=wr.split(), c=cost, f=fn, lat=lat, sem=sem, val=val, b=list(banks), i=len(ops), get=get, put=put))
+
+    def mm(calls):
+        def f(q):
+            x = None
+            for o, a, b, s, e in (calls if isinstance(calls, list) else calls()):
+                x = q.matmul(o, a, b, s, e)
+            return x
+        return f
+
+    def group(out, pairs):
+        k = len(pairs)
+        return [(out if o is None else o, a, b, j == 0, j == k - 1) for j, (a, b, o) in enumerate(pairs)]
+
+    pool = lambda k: T["cm%d" % PLAN["bank"][k]]
+    sel = lambda l, nm="SEL": B(nm, 128 * l, 128 * l + 128)
+    V, S, TE, G, Y = "v", "s", "t", "g", "y"
+
+    def ts(rd, wr, out, i, s1, s2, o0, o1=None, n=96, k=1.0, banks=()):
+        op(V, rd, wr, cv(n, k), (lambda q: q.tensor_scalar(out, i, s1, s2, o0, o1)) if o1 is not None else (lambda q: q.tensor_scalar(out, i, s1, None, o0)), banks)
+    def tt(rd, wr, out, a, b, o, n=96, k=2.0, banks=()):
+        op(V, rd, wr, cv(n, k), lambda q: q.tensor_tensor(out, a, b, o), banks)
+    def cp(rd, wr, out, i, n=96, k=1.0, banks=()):
+        op(V, rd, wr, cv(n, k), lambda q: q.tensor_copy(out, i), banks)
+    def scan(rd, wr, out, a, b, o0, o1, n=96, k=1.0, banks=()):
+        op(V, rd, wr, cv(n, k), lambda q: q.tensor_tensor_scan(out, a, b, 0.0, o0, o1), banks)
+    def act(rd, wr, out, i, f, n=96, banks=(), k=1.0, **kw):
+        op(S, rd, wr, K["fix"] + K["v"] * n * k, lambda q: q.activation(out, i, f, **kw), banks)
+    def pe(rd, wr, calls, bank, *ns):
+        op(TE, rd, wr, ct(*ns), mm(calls), [bank])
+
+    def load(i, dst, out, src, eng=Y, rd="", kb=100):
+        op(eng, rd, dst, 0.1, lambda q: q.dma_start(out, src), lat=2.0 + kb / 250.0, sem="l%d" % i, val=16)
+    for h in (0, 1):
+        s = slice(C * h, C * h + C)
+        load(2 * h, "LIt%d" % h, B("LI%d" % h, 96, 192), T.tl[:, s], kb=50)
+        load(2 * h + 1, "LId%d" % h, B("LI%d" % h, 0, 96), T.dl[:, s], kb=50)
+        if h == 0:
+            load(4, "Z0", B("Z0"), T.z0[:], kb=50, eng=S)
+            op(V, "", "tabm", cv(8), lambda q: q.memset(T.tab[:, 2048:2056], -1.0))
+            load(5, "taba", T.tab[:, 0:2048], T.clk[:, 0:2048], kb=520)
+            load(6, "tabb", T.tab[:, 2049:4097], T.clk[:, 2048:4096], rd="tabm", eng=S, kb=520)
+    load(7, "SIc", B("SI", 0, 512), T.sc[:], kb=260)
+    load(8, "SIt", B("SI", 512, 1024), T.st[:], kb=260)
+    load(9, "THR", B("THR", 0, 1), T.th[:], kb=1)
+    TAB = "taba tabb tabm"
+    tab = T.tab[:, 0:4097]
+
+    def ms(name, c):
+        op(V, "", name, cv(WHERE[name][2], 0.5), lambda q: q.memset(B(name), c))
+    def iota(name, n, pat, base, cmul):
+        op(G, "", name, 0.13 + 2 * K["v"] * n, lambda q: q.iota(B(name, 0, n), pat, base, cmul))
+    def aff(out, src, n, pat, cmp, base, cmul):
+        op(G, src, out, 0.17 + 2 * K["v"] * n, lambda q: q.affine_select(B(out, 0, n), B(src, 0, n), pat, cmp, 0.0, base, cmul))
+    ms("ON1", 1.0)
+    aff("BKC", "ON1", 128, [[-16, 8], [0, 16]], A.is_ge, 0, 1)
+    aff("BK", "BKC", 128, [[16, 8], [0, 16]], A.is_ge, 15, -1)
+    aff("ID", "ON1", 128, [[-1, 128]], A.is_equal, 0, 1)
+    iota("IB", 96, [[0, 6], [-1, 16]], 15, 0)
+    aff("RST0", "ON1", L, [[0, C], [1, 16]], A.is_gt, 0, 0)
+    aff("SEL", "ON1", 2048, [[-1, 16], [-16, 8], [0, 16]], A.is_equal, 0, 1)
+    iota("IA", 96, [[0, 96]], 0, 1)
+    iota("CM", 96, [[1, 96]], 0, 0)
+    iota("C6", 12, [[0, 2], [16, 6]], 0, 0)
+    aff("RSTM", "ON1", NC * C, [[0, NC], [1, C]], A.is_equal, 0, 0)
+    ms("ZSS0", 0.0)
+    ms("ZSS1", 0.0)
+    act("RST0", "RSTB", B("RSTB"), B("RST0"), F.Copy, n=L, scale=2 * BIG, bias=-BIG)
+    act("RSTM", "RSTN", B("RSTN"), B("RSTM"), F.Copy, n=NC * C, scale=BIG)
+    act("ON1", "GG", B("GG"), B("ON1"), F.Copy, n=2048, scale=0.0)
+    for p in range(16):
+        act("BK GG", "GGp%d" % p, B("GG", 129 * p, 128 * p + 128, 16), B("BK", 0, 128, 16), F.Copy, n=8)
+    GGK = " ".join("GGp%d" % p for p in range(16))
+    for out, src, k in (("IDN", "ID", -1), ("I8K", "ID", 8192), ("BKN", "BK", -1), ("BNK", "BK", -1000), ("I1K", "ID", 1000), ("INK", "ID", -1000),
+                        ("B32", "BK", -1 / 32), ("B3K", "BK", 32), ("I2K", "ID", 2048), ("IH", "ID", 0.5), ("IHN", "ID", -0.5)):
+        act(src, out, B(out), B(src), F.Copy, n=128, scale=float(k))
+    ts("IB", "TBC", B("TBC"), B("IB"), 1 / 16, None, A.mult)
+    ts("IA", "IC", B("IC"), B("IA"), 15, None, A.bitwise_and)
+    ts("IC", "PCN", B("PCN"), B("IC"), -15.0, 1 / 16, A.add, A.mult)
+    ts("CM", "MC", B("MC"), B("CM"), 1 / 256, None, A.mult)
+    tt("C6 IC", "R6", B("R6", 0, 12), B("C6", 0, 12), B("IC", 0, 12), A.add, n=8)
+    ts("R6", "CL", B("CL", 0, 12), B("R6", 0, 12), 1 / 256, 512 + 48 / 256, A.mult, A.add, n=8)
+    ts("R6", "C2", B("C2", 0, 12), B("R6", 0, 12), 512.0, None, A.add, n=8)
+    ms("AS", 0.0)
+    ms("CH", -2048.0)
+    op(V, "", " ".join("AK%d%d" % (h, c) for h in (0, 1) for c in range(NC)), cv(2 * NC * C, 0.5), lambda q: q.memset(B("AK"), 512.0))
+    ts("THR", "NTH", B("NTH", 0, 1), B("THR", 0, 1), -1.0, -8192.0, A.mult, A.add, n=1)
+    cp("NTH", "NLIM0", B("NLIM", 0, 1), B("NTH", 0, 1), n=1)
+
+    def encode(out, ok, src, sk, tmp, tk, pb, kb, bb, n):
+        ts(sk, tk, tmp, src, 1 + 2.0 ** -12, 2.0 ** -13 - 2048, A.mult, A.add, n=n)
+        ts(sk, kb, pb, src, 0.0, None, A.is_ge, n=n, banks=[bb])
+        tt(tk + " " + kb, ok, out, pb, tmp, A.mult, n=n, k=1, banks=[bb])
+    for h in (0, 1):
+        m = T["m0%d" % h]
+        encode(m[:, 0:192], "m0%d" % h, B("LI%d" % h), "LIt%d LId%d" % (h, h), B("T1%d" % h), "T1%d" % h, T.pm[:, 192 * h:192 * h + 192], "KC MK", "pm", 192)
+        act("Z0", "m0%dz" % h, m[:, 192:288], B("Z0", C * h, C * h + C), F.Copy)
+    encode(T.scw[:, 0:512], "scw", B("SI", 0, 512), "SIc", B("SA", 0, 512), "SAc", T.px[:], "px", "px", 512)
+    encode(T.stw[:, 0:512], "stw", B("SI", 512, 1024), "SIt", B("SA", 512, 1024), "SAt", T.ph[:], "psH0 psH1 psV", "ph", 512)
+    op(V, "", "scwd", cv(96), lambda q: q.memset(T.scw[:, 512:608], 0.0))
+
+    def decode(out, ok, e, ek, sg, gk, ne, nk, n):
+        act(ek, gk, sg, e, F.Sign, n=n)
+        ts(ek, nk, ne, e, 0.0, None, A.not_equal, n=n, k=.5)
+        op(TE, "ID I2K IH IHN %s %s %s" % (ek, gk, nk), "dec" + gk, ct(n, n, n, n), mm(lambda: group(pool(gk)[:, 0:n], [
+            (B("ID"), e, None), (B("I2K"), ne, None), (B("IH"), ne, None), (B("IHN"), sg, None)])), get=gk)
+        op(S, "dec" + gk, ok, cv(n), lambda q: q.activation(out, pool(gk)[:, 0:n], F.Identity, bias=-1.0), put=gk)
+
+    nblk = [0]
+    def chunk(t, h):
+        now[0] = h
+        m = T["m%d%d" % (t, h)]
+        X = lambda n: n + str(h)
+        b = lambda n, *a: B(X(n), *a)
+        D, TT, Z = m[:, 0:96], m[:, 96:192], m[:, 192:288]
+        km = "m%d%d" % (t, h)
+        kz = km + "z" if t == 0 else km
+        x = lambda s: " ".join(X(w[1:]) if w[0] == "." else w for w in s.split())
+        pk, pc, ph, px, pm = T.pk, T.pc, T.ph, T.px, T.pm
+        cv0, cu0 = (96, 0) if h == 0 else (0, 96)
+        vo, uo = (6, 0) if h == 0 else (12, 18)
+        pv, pu, p0 = 192 + vo, 192 + uo, 192 + 12 * h
+        ts(km, x(".OFF"), b("OFF"), m[:, 0:192], 2048.0, None, A.add, n=192, k=.5)
+        cp(x(kz + " .ZSS"), x(".ZSS"), b("ZSS", 0, L, 16), Z, k=.5)
+        scan(x(".ZSS RST0"), x(".ZE"), b("ZE"), B("RST0"), b("ZSS"), A.mult, A.add, n=L, k=.5)
+        tt(x(TAB + " .OFF .ZE"), x(".MT"), b("MT"), tab.indirect(b("OFF", 96, 192)), b("ZE"), A.min, n=L, k=K["gat"])
+        pe(x(GGK + " ID ON1 .ZSS"), "psU%d" % h, group(pk[:, pu:pu + 6], [(B("ID"), B("ON1", 0, 6), None)] + [(sel(r, "GG"), b("ZSS", 16 * r, L, 256), None) for r in range(16)]), "pk", *[64] * 17)
+        pe(x(GGK + " ID TBC .MT"), "psK", group(pk[:, 0:96], [(B("ID"), B("TBC"), None)] + [(sel(r, "GG"), b("MT", 96 * r, 96 * r + 96), None) for r in range(16)]), "pk", *[96] * 17)
+        tt(x(TAB + " .OFF .ZE"), x(".SD"), b("SD"), tab.indirect(b("OFF", 0, 96)), b("ZE"), A.subtract, n=L, k=K["gat"])
+        act(x(".SD"), x(".AD"), b("AD"), b("SD"), F.Abs, n=L)
+        ts(km, x(".FL"), b("FL"), m[:, 0:192], 0.0, None, A.not_equal, n=192, k=.5)
+        pe(x("BK .FL"), "psA", group(pk[:, 256:352], [(B("BK"), b("FL", 96, 192), None)]), "pk", 96)
+        act("psA", x(".NH"), b("NH"), pk[:, 256:352], F.Relu, banks=["pk"], bias=2.0, scale=-2.0)
+        scan("psK RSTB", x(".MX"), b("MX"), B("RSTB", 0, 96), pk[:, 0:96], A.min, A.max, banks=["pk"])
+        ts(x(".MX"), x(".KI"), b("KI", 0, 6), b("MX", 15, 96, 16), -15 / 32, None, A.add, n=6)
+        tt(x(".MX .KI"), x(".QL"), b("QL", 0, 6), b("MX", 15, 96, 16), b("KI", 0, 6), A.subtract, n=6)
+        pe(x("SEL ID PCN .QL"), "psQ", group(None, [(B("ID"), B("PCN"), pk[:, 96:192])] + [(sel(r), b("QL", 0, 6), pk[:, 96 + 6 * r:102 + 6 * r]) for r in range(16)]), "pk", 96, *[64] * 16)
+        ts("psQ", x(".OH"), b("OH"), pk[:, 96:192], 0.0, None, A.is_equal, banks=["pk"])
+        tt(x(".OH " + km), x(".TH"), b("TH"), b("OH"), TT, A.mult)
+        pe(x(GGK + " .TH"), "psN%d" % h, group(pk[:, pv:pv + 6], [(sel(r, "GG"), b("TH", r, 96, 16), None) for r in range(16)]), "pk", *[64] * 16)
+        ts("psN%d psU%d" % (h, h), x(".VI"), B("VI", 12 * h, 12 * h + 12), pk[:, p0:p0 + 12], 1 - 2.0 ** -13, -0.5, A.mult, A.add, n=12, banks=["pk"])
+        ts(x(".VI"), x(".VI2"), B("VI2", 12 * h, 12 * h + 12), B("VI", 12 * h, 12 * h + 12), 511, None, A.bitwise_and, n=12)
+        cp(x(".VI2"), x(".OFV"), B("OFV", 12 * h, 12 * h + 12), B("VI2", 12 * h, 12 * h + 12), n=12)
+        ts("psN%d" % h, x(".OFN"), b("OFN", 0, 6), pk[:, pv:pv + 6], 2048.0, None, A.add, n=6, banks=["pk"])
+        act(x("scw scwd .OFV"), x(".CS"), b("CS"), T.scw[:, 0:512].indirect(B("OFV", 12 * h, 12 * h + 12)), F.Copy, n=192, k=K["gat"])
+        act(x("stw .OFV"), x(".CT"), b("CT"), T.stw[:, 0:512].indirect(B("OFV", 12 * h, 12 * h + 12)), F.Copy, n=192, k=K["gat"])
+        act(x(TAB + " .OFN"), x(".YK"), b("YK"), tab.indirect(b("OFN", 0, 6)), F.Copy, k=K["gat"])
+        def compare(j, src, ks, row, kr):
+            for k in range(4):
+                mode = MODES[2 * j + k // 2]
+                bank = "blk%d" % nblk[0]
+                nblk[0] += 1
+                op(TE, x("SEL IDN %s %s" % (ks, kr)), bank, ct(*[96] * 8), mm((lambda bank, k: lambda: [c for i in range(4) for c in group(
+                    pool(bank)[:, 96 * i:96 * i + 96], [(sel(4 * k + i), src, None), (B("IDN"), row, None)])])(bank, k)), get=bank)
+                a0 = 384 * k
+                eq, cx = b("EQ%d" % j, a0, a0 + 384), b("CX", L * j + a0, L * j + a0 + 384)
+                ke, kx = x(".EQ%d_%d_" % (j, k)), x(".CX%d_%d_" % (j, k))
+                if mode == "V":
+                    op(V, bank, ke, cv(384), (lambda bank, eq: lambda q: q.tensor_scalar(eq, pool(bank)[:, 0:384], 0.0, None, A.is_equal))(bank, eq), put=bank)
+                    continue
+                op(S, bank, kx, cv(384), (lambda bank, cx: lambda q: q.activation(cx, pool(bank)[:, 0:384], F.Abs))(bank, cx), put=bank)
+                if mode == "SS":
+                    act(kx, ke, eq, cx, F.Relu, n=384, bias=1.0, scale=-1.0)
+                elif k % 2:
+                    k0, a0 = k - 1, a0 - 384
+                    ts(kx + " " + x(".CX%d_%d_" % (j, k0)), ke + " " + x(".EQ%d_%d_" % (j, k0)), b("EQ%d" % j, a0, a0 + 768), b("CX", L * j + a0, L * j + a0 + 768), 0.0, None, A.is_equal, n=768, k=.5)
+        eqk = lambda j: " ".join(x(".EQ%d_%d_" % (j, k)) for k in range(4))
+        eqb = lambda j, l: b("EQ%d" % j, 96 * l, 96 * l + 96)
+        compare(0, D, km, TT, km)
+        pe(x(GGK + " ID %s .OH" % eqk(0)), "psC", group(pc[:, 0:96], [(sel(l, "GG"), eqb(0, l), None) for l in range(16)]) +
+           group(pc[:, 96:192], [(B("ID"), eqb(0, l), None) for l in range(16)] + [(B("ID"), b("OH"), None)]), "pc", *[96] * 33)
+        pe(x(GGK + " I8K .AD .FL"), "psD", group(pc[:, 192:288], [(B("I8K"), b("FL", 0, 96), None)] + [(sel(p, "GG"), b("AD", p, L, 16), None) for p in range(16)]), "pc", *[96] * 17)
+        act("psD NLIM%d" % t, x(".F1"), b("F1"), pc[:, 192:288], F.Relu, banks=["pc"], bias=B("NLIM", t, t + 1))
+        act("psC", "KC", pm[:, 0:192], pc[:, 0:192], F.Relu, n=192, banks=["pc", "pm"], bias=1.0, scale=-1.0)
+        tt("KC " + km, x(".DT1"), b("DT1"), pm[:, 0:192], m[:, 0:192], A.mult, n=192, k=1, banks=["pm"])
+        ts(x(".DT1"), x(".OFX"), b("OFX"), b("DT1", 0, 96), 2048.0, None, A.add, k=.5)
+        act(x(TAB + " .OFX"), x(".XT"), b("XT"), tab.indirect(b("OFX")), F.Copy, n=L, k=K["gat"])
+        tt(x("psC .F1"), x(".FAR"), b("FAR"), pc[:, 0:96], b("F1"), A.mult, k=1, banks=["pc"])
+        ts(x(".DT1"), x(".FD1"), b("FD1"), b("DT1"), 0.0, None, A.not_equal, n=192, k=.5)
+        scan(x(".XT RSTB"), x(".TP"), b("TP"), B("RSTB"), b("XT"), A.min, A.max, n=L, k=.5)
+        compare(1, D, km, b("CS", cv0, cv0 + 96), x(".CS"))
+        compare(2, TT, km, b("CT", cv0, cv0 + 96), x(".CT"))
+        for j in (0, 1):
+            pe("ID " + eqk(1 + j), "psH%d" % j, group(ph[:, 96 * j:96 * j + 96], [(B("ID"), eqb(1 + j, l), None) for l in range(16)]), "ph", *[96] * 16)
+        act("psH0 psH1", x(".HC"), b("HC"), ph[:, 0:192], F.Copy, n=192, banks=["ph"], bias=1 / 64)
+        far, left, nh = b("FAR"), b("FD1", 0, 96), b("NH")
+        calls = group(px[:, 192:288], [(B("ID"), B("ON1", 0, 96), None), (B("BKN"), left, None), (B("BNK"), far, None), (B("I1K"), nh, None)])
+        calls += group(px[:, 288:384], [(B("BK"), left, None), (B("BNK"), far, None), (B("INK"), nh, None)])
+        calls += group(px[:, 384:480], [(B("BK"), far, None)])
+        pe(x("ID ON1 BK BKN BNK I1K INK .FAR .FD1 .NH"), "px", calls, "px", *[96] * 8)
+        act("px CH", "MK", pm[:, 192:480], px[:, 192:480], F.Sigmoid, n=288, banks=["px", "pm"], bias=B("CH", 0, 1), scale=4096.0)
+        tt(x("MK .NH"), x(".PRF"), B("PRF", 96 * h, 96 * h + 96), pm[:, 192:288], nh, A.is_gt, k=1, banks=["pm"])
+        calls = [(px[:, 0:192], B("ID"), b("HC"), True, False), (px[:, 0:192], B("ID"), b("FD1"), False, False)]
+        for j in (0, 1):
+            for i, (w, y) in enumerate(((B("B32"), left), (B("BNK"), far), (B("I1K"), nh))):
+                calls.append((px[:, 96 * j:96 * j + 96], w, y, False, j == 1 and i == 2))
+        pe(x("ID B32 BNK I1K .HC .FD1 .FAR .NH"), "pxx px", calls, "px", 192, 192, *[96] * 6)
+        act("pxx", "KC", pm[:, 0:192], px[:, 0:192], F.Sigmoid, n=192, banks=["px", "pm"], scale=-16384.0)
+        for j, ck in ((0, ".CS"), (1, ".CT")):
+            s0, s1 = 96 * j, 96 * j + 96
+            tt(x("MK .DT1"), x(".P2%s_" % j), b("P2", s0, s1), pm[:, 288:384], b("DT1", s0, s1), A.mult, k=1, banks=["pm"])
+            tt(x("MK " + ck), x(".P3%s_" % j), b("P3", s0, s1), pm[:, 192:288], b(ck[1:], cu0, cu0 + 96), A.mult, k=1, banks=["pm"])
+            tt(x("KC " + ck), x(".P1%s_" % j), b("P1", s0, s1), pm[:, s0:s1], b(ck[1:], cv0, cv0 + 96), A.mult, k=1, banks=["pm"])
+        pe(x("ID IDN %s .YK" % kz), "psZ", group(pc[:, 384:480], [(B("ID"), Z, None), (B("IDN"), b("YK"), None)]), "pc", 96, 96)
+        act("psZ", x(".ZA"), b("ZA"), pc[:, 384:480], F.Abs, banks=["pc"])
+        pe(x("ID .YK .TP"), "psG", group(pk[:, 352:448], [(B("ID"), b("YK"), None), (B("ID"), b("TP", 15, L, 16), None)]), "pk", 96, 96)
+        act("psG", x(".ZG"), b("ZG"), pk[:, 352:448], F.Copy, banks=["pk"], bias=1023.75, scale=0.5)
+        act(x(".ZG"), x(".ZGI"), b("ZGI"), b("ZG"), F.Copy, bias=-1024.0)
+        tt(x("MK .ZA"), x(".ZA2"), b("ZA2"), pm[:, 384:480], b("ZA"), A.mult, k=1, banks=["pm"])
+        tt(x("MK .ZGI"), x(".ZG2"), b("ZG2"), pm[:, 288:384], b("ZGI"), A.mult, k=1, banks=["pm"])
+        tt(x("MK " + kz), x(".ZR"), b("ZR"), pm[:, 192:288], Z, A.mult, k=1, banks=["pm"])
+        calls = group(px[:, 0:192], [(B("ID"), b("P2"), None), (B("ID"), b("P3"), None), (B("ID"), b("P1"), None)])
+        calls += group(px[:, 192:288], [(B("ID"), b("ZA2"), None), (B("ID"), b("ZR"), None), (B("ID"), b("ZG2"), None)])
+        pe(x("ID .P10_ .P11_ .P20_ .P21_ .P30_ .P31_ .ZA2 .ZG2 .ZR"), "px pxx", calls, "px", 192, 192, 192, 96, 96, 96)
+        if t < 3:
+            ko = "o%d%d" % (t, h)
+            act("px", ko, T[ko][:], px[:, 0:288], F.Copy, n=288, banks=["px"])
+            op(G, ko, "m%d%d" % (t + 1, h), 1.0, ("send", t, h), lat=K["hop"], sem="a%d%d" % (t + 1, h), val=NENG)
+        else:
+            act("px", x(".FIN"), b("FIN"), px[:, 0:288], F.Copy, n=288, banks=["px"])
+            decode(b("OUT", 0, 192), x(".OUTa"), b("FIN", 0, 192), x(".FIN"), b("FSG"), x(".FSG"), b("FNE"), x(".FNE"), 192)
+            cp(x(".FIN"), x(".OUTz"), b("OUT", 192, 288), b("FIN", 192, 288))
+            s = slice(C * h, C * h + C)
+            for j, (y, k, a) in enumerate(((T.yd, ".OUTa", 0), (T.yt, ".OUTa", 96), (T.yz, ".OUTz", 192))):
+                op(Y, x(k), "y%d%d" % (j, h), 0.1, (lambda y, a: lambda q: q.dma_start(y[:, s], b("OUT", a, a + 96)))(y, a), lat=2.2, sem="out%d" % (3 * h + j), val=16)
+            decode(b("TD"), x(".TD"), b("DT1", 96, 192), x(".DT1"), b("TSG"), x(".TSG"), b("TNE"), x(".TNE"), 96)
+        if t < 3:
+            pe(x("BK BKN BNK .FL .FD1 .FAR"), "psS", group(pc[:, 288:384], [(B("BK"), b("FL", 0, 96), None), (B("BKN"), left, None), (B("BNK"), far, None)]), "pc", 96, 96, 96)
+            act("psS", x(".JK ACN%d%d" % (t, h)), b("JK"), pc[:, 288:384], F.Relu, banks=["pc"], accum_out=B("ACN", 2 * t + h, 2 * t + h + 1))
+
+    def proofs(t):
+        now[0] = 0
+        ph, n = T.ph, 12
+        w = lambda nm: B(nm, 0, 12)
+        v = B("VI2", 6, 18)
+        cp("VI20 VI21", "VL", w("VL"), v, n=n)
+        tt("VI20 VI21 CL", "KB", w("KB"), v, w("CL"), A.add, n=n)
+        tt("VI20 VI21 C2", "DV", w("DV"), v, w("C2"), A.subtract, n=n)
+        for h in (0, 1):
+            pe("ID MC SEL B3K VL PRF%d" % h, "psV", group(None, [(B("ID"), B("MC"), ph[:, 192:288])] + [(sel(r), B("VL", 6 * h, 6 * h + 6), ph[:, 192 + r:288:16]) for r in range(16)] +
+               [(B("B3K"), B("PRF", 96 * h, 96 * h + 96), ph[:, 192:288])]), "ph", 96, 96, *[64] * 16)
+            for c in range(NC):
+                a = 96 * (NC * h + c)
+                act("psV KB", "AK%d%d" % (h, c), B("AK", a + 16 * c, a + 96), ph[:, 192 + 16 * c:288], F.Abs, n=96 - 16 * c, banks=["ph"], bias=B("KB", 6 * h + c, 6 * h + c + 1), scale=-1.0)
+            a0, a1 = NC * C * h, NC * C * h + NC * C
+            scan("RSTN " + " ".join("AK%d%d" % (h, c) for c in range(NC)), "SM%d" % h, B("SM", a0, a1), B("RSTN"), B("AK", a0, a1), A.max, A.min, n=NC * C, k=.5)
+        pe(GGK + " PRF0 PRF1", "psP", group(ph[:, 384:396], [(sel(r, "GG"), B("PRF", r, 192, 16), None) for r in range(16)]), "ph", *[64] * 16)
+        ts("SM0 SM1", "WN", w("WN"), B("SM", 95, 2 * NC * C, 96), 47.5 / 256, 1 / 16, A.is_ge, A.mult, n=n)
+        tt("psP WN", "WN2", w("WN2"), ph[:, 384:396], w("WN"), A.mult, n=n, banks=["ph"])
+        tt("WN2 DV", "WO", w("WO"), w("WN2"), w("DV"), A.mult, n=n)
+        tt("WO C2", "WO2", w("WO2"), w("WO"), w("C2"), A.add, n=n)
+        cp("WO2", "OFW", w("OFW"), w("WO2"), n=n)
+        for h in (0, 1):
+            o = B("OFW", 6 * h, 6 * h + 6)
+            if t < 3:
+                cp("OFW DT1%d" % h, "scw scwd", T.scw[:, 0:608].indirect(o), B("DT1%d" % h, 96, 192), k=3)
+            else:
+                cp("OFW TD%d" % h, "sow", T.sow[:, 0:608].indirect(o), B("TD%d" % h), k=3)
+
+    for t in range(4):
+        if t == 3:
+            cp("scw", "SE", B("SE"), T.scw[:, 0:512], n=512)
+            op(V, "", "sowd", cv(96), lambda q: q.memset(T.sow[:, 512:608], 0.0))
+            decode(T.sow[:, 0:512], "sow", B("SE"), "SE", B("SG"), "SG", B("SNE"), "SNE", 512)
+            ops[-1]["r"].append("sowd")
+        for h in (0, 1):
+            chunk(t, h)
+        now[0] = 0
+        if t < 3:
+            op(V, "AS ACN%d0 ACN%d1" % (t, t), "AS", cv(1), (lambda t: lambda q: q.tensor_scalar(B("AS", t + 1, t + 2), B("ACN", 2 * t, 2 * t + 1), B("ACN", 2 * t + 1, 2 * t + 2), B("AS", t, t + 1), A.add, A.add))(t))
+            cp("AS", "AI", B("AI", 0, 1), B("AS", t + 1, t + 2), n=1)
+            ts("AI", "AI2", B("AI2", 0, 1), B("AI", 0, 1), 31, None, A.bitwise_and, n=1)
+            ts("AI2 NTH", "NLIM%d" % (t + 1), B("NLIM", t + 1, t + 2), B("AI2", 0, 1), -8.0, B("NTH", 0, 1), A.mult, A.add, n=1)
+        proofs(t)
+    op(Y, "sow", "ysd", 0.1, lambda q: q.dma_start(T.ys[:], T.sow[:, 0:512]), lat=2.5, sem="out6", val=16)
+    return ops
+
+
+def depend(ops):
+    last, readers = {}, {}
+    for o in ops:
+        o["d"] = {last[k] for k in o["r"] + o["w"] if k in last} | {i for k in o["w"] for i in readers.get(k, ())}
+        for k in o["r"]:
+            readers.setdefault(k, []).append(o["i"])
+        for k in o["w"]:
+            last[k] = o["i"]
+            readers[k] = []
+        o["d"].discard(o["i"])
+    return ops
+
+
+def shifts(ops):
+    off = [-3.0 * o["h"] for o in ops]
+    kind = [(o["e"] + o["w"][0].rstrip("0123456789_"), o["h"]) for o in ops]
+    names = sorted(set(kind))
+    for i in SHIFTS:
+        rng = np.random.default_rng(i)
+        u, a, w, d = rng.random(), int(rng.integers(1 << 30)), int(rng.integers(4)), float(rng.normal())
+        if u < .5:
+            which, size = [j for j, k in enumerate(kind) if k == names[a % len(names)]], 3
+        else:
+            a %= len(ops)
+            which, size = range(a, min(len(ops), a + (1, 5, 20, 60)[w])), 4
+        for j in which: off[j] += size * d
+    return off
+
+
+def schedule(ops, off):
+    n, wake = len(ops), K["wake"]
+    deps = [set(o["d"]) for o in ops]
+    succ = [[] for _ in ops]
+    left = [0] * n
+    for o in ops:
+        for i in o["d"]:
+            succ[i].append(o["i"]); left[o["i"]] += 1
+    pri = [0.0] * n
+    for o in reversed(ops):
+        pri[o["i"]] = o["c"] + o["lat"] + max([pri[j] + wake for j in succ[o["i"]]] or [0.0])
+    pri = [a + b for a, b in zip(pri, off)]
+    free, bank, end, base, order = {}, {}, [0.0] * n, {}, []
+    banks, given = [[0.0, None] for _ in range(3)], {}
+    ready = [o["i"] for o in ops if not left[o["i"]]]
+    def est(i):
+        o = ops[i]
+        x = max(free.get(o["e"], 0.0), base.get(i, 0.0))
+        for k in o["b"]:
+            e, tm = bank.get(k, ("", 0.0))
+            if e != o["e"]: x = max(x, tm + wake)
+        if o["get"]: x = max(x, min(p[0] for p in banks) + wake)
+        return x
+    while ready:
+        ests = [(est(i), i) for i in ready]
+        t0 = min(ests)[0]
+        best = None
+        for x, i in ests:
+            if x <= t0 + 0.02 and (best is None or pri[i] > pri[best[1]]): best = (x, i)
+        x, i = best
+        o = ops[i]
+        ready.remove(i)
+        free[o["e"]] = x + o["c"]
+        end[i] = x + o["c"] + o["lat"]
+        for k in o["b"]: bank[k] = (o["e"], x + o["c"])
+        if o["get"]:
+            j = min(range(3), key=lambda j: banks[j][0])
+            if banks[j][1] is not None: deps[i].add(banks[j][1])
+            given[o["get"]] = j
+            banks[j][0] = 1e9
+        if o["put"]: banks[given[o["put"]]] = [x + o["c"], i]
+        order.append(i)
+        for j in succ[i]:
+            base[j] = max(base.get(j, 0.0), end[i] + wake)
+            left[j] -= 1
+            if not left[j]: ready.append(j)
+    prev = {}
+    for i in order:
+        o = ops[i]
+        for k in o["b"]:
+            p = prev.setdefault(k, {})
+            for e, j in p.items():
+                if e != o["e"]: deps[i].add(j)
+            p[o["e"]] = i
+    return order, max(end), given, deps
+
+
+def rank_program(g, core, T, topo):
+    rank = T.rank_of(core)
+    if rank is None:
+        return
+    ops = build(T)
+    if "order" not in PLAN:
+        depend(ops)
+        PLAN["order"], PLAN["time"], PLAN["bank"], PLAN["d"] = schedule(ops, shifts(ops))
+    queue = {"v": g.vector, "s": g.scalar, "t": g.tensor, "g": g, "y": g.sync}
+    know = {e: {} for e in queue}
+    count, clock = {}, {}
+    sends = 0
+    for i in PLAN["order"]:
+        o = ops[i]
+        e, q = o["e"], queue[o["e"]]
+        kn = know[e]
+        for j in sorted(PLAN["d"][i], key=lambda j: -clock[j][2]):
+            s, v, _, c = clock[j]
+            if kn.get(s, 0) < v:
+                q.wait_ge(T.sem[s], v)
+                for k, w in c.items():
+                    if kn.get(k, 0) < w: kn[k] = w
+                kn[s] = max(kn.get(s, 0), v)
+        if isinstance(o["f"], tuple):
+            _, t, h = o["f"]
+            dst = T.cores[(rank + HOPS[t]) % N]
+            rid, pid, _ = topo.addr(dst)
+            mask = sum(1 << x for x in topo.engines(core, dst)[:NENG])
+            g.remote_dma(T["m%d%d" % (t + 1, h)][:], T["o%d%d" % (t, h)][:], T.sem[o["sem"]], T.sem.loc, pid, rid, mask)
+            sends += NENG
+            clock[i] = (o["sem"], o["val"], len(clock), dict(kn))
+            continue
+        x = o["f"](q)
+        if o["sem"]:
+            x.then_inc(T.sem[o["sem"]], o["val"])
+            clock[i] = (o["sem"], o["val"], len(clock), dict(kn))
+        else:
+            count[e] = count.get(e, 0) + 1
+            x.then_inc(T.sem[e], 1)
+            clock[i] = (e, count[e], len(clock), dict(kn))
+    for e, c in count.items():
+        g.wait_ge(T.sem[e], c)
+    for i in range(NLOAD):
+        g.wait_ge(T.sem["l%d" % i], 16)
+    for i in range(NOUT):
+        g.wait_ge(T.sem["out%d" % i], 16)
+    g.wait_ge(T.sem.loc, sends)
+    for t in (1, 2, 3):
+        for h in (0, 1):
+            g.wait_ge(T.sem["a%d%d" % (t, h)], NENG)

@@ -3,62 +3,65 @@ from concourse.mybir import dt, AluOpType as A, ActivationFunctionType as F
 
 N = 6
 HOPS = [1, 2, 3]
-M, C, NC = 192, 96, 6
-L = 16 * C
+M, C = 192, 96
+NH_, NC, L = M // C, C // 16, 16 * C
+LB = 4
+NB = 16 // LB
 BIG = 30000.0
+ZO = 1536.0
+EQ = 3 / 128
 
 H, BF, F4, I4, U2 = "float16", "bfloat16", "float32", "int32", "uint16"
 PER = {
-    "OFF": (U2, 192), "OFX": (U2, 96), "OFN": (U2, 8), "LI": (I4, 192), "KI": (I4, 8),
-    "ZSS": (BF, L), "ZE": (H, L), "MT": (H, L), "SD": (H, L), "AD": (H, L), "XT": (H, L), "TP": (H, L),
-    "EQ0": (H, L), "EQ1": (H, L), "EQ2": (H, L), "CX": (H, 3 * L),
-    "FL": (H, 192), "QL": (H, 8), "OH": (H, 96), "TH": (H, 96), "NH": (H, 96),
-    "CS": (H, 192), "CT": (H, 192), "YK": (H, 96), "F1": (H, 96), "FAR": (H, 96),
-    "DT1": (H, 192), "FD1": (H, 192), "HC": (H, 192), "P1": (H, 192), "P2": (H, 192), "P3": (H, 192),
-    "ZA": (H, 96), "ZA2": (H, 96), "ZG": (H, 96), "ZGI": (H, 96), "ZG2": (H, 96), "ZR": (H, 96),
-    "FIN": (H, 288), "FSG": (H, 192), "FNE": (H, 192), "TSG": (H, 96), "TNE": (H, 96),
-    "MX": (F4, 96), "JK": (F4, 96), "T1": (I4, 192), "OUT": (F4, 288), "TD": (F4, 96),
+    "OFT": (U2, C), "OFX": (U2, C), "OFN": (U2, 8), "OFV": (U2, 2 * NC), "OFW": (U2, 2 * NC), "LI": (I4, 2 * C), "VI": (I4, 2 * NC), "VI2": (I4, 2 * NC),
+    "ZSS": (H, L), "ZE": (H, L), "GD": (H, L), "GN": (H, L), "XT": (H, L), "TP": (H, L),
+    "EQ0": (BF, L), "EQ1": (BF, L), "EQ2": (BF, L),
+    "FL": (H, 2 * C), "FK": (H, 2 * C), "NH": (H, C), "OH": (H, 128), "NF": (H, 128), "FAR": (BF, C), "R0": (H, 2 * C), "R1": (BF, 2 * C),
+    "DT1": (H, 2 * C), "M1": (H, 2 * C), "SA": (H, 2 * C), "SB": (H, 2 * C),
+    "CV": (H, 4 * C), "YK": (H, C), "YM": (H, C), "NG": (H, 2 * C), "A2": (H, 3 * C), "A3": (H, 3 * C), "FIN": (H, 3 * C),
+    "VL": (H, NC), "EP": (H, C), "LS": (H, C), "WO": (H, NC),
+    "MX": (F4, 128), "SM": (F4, 128), "JK": (F4, C), "TN": (F4, C), "OUT": (F4, 3 * C),
 }
+SCALED = {"IDN": -1, "I3N": -3, "I4": 4, "I128N": -128, "I512": 512, "I512N": -512, "I2K": 2048, "I2KN": -2048, "I8K": 8192, "IH": 0.5}
 ONE = {
-    "SEL": (BF, 2048), "GG": (BF, 2048), "ON1": (BF, 2048),
-    "ID": (BF, 128), "IDN": (BF, 128), "I1K": (BF, 128), "INK": (BF, 128), "I8K": (BF, 128), "I2K": (BF, 128), "IH": (BF, 128), "IHN": (BF, 128),
-    "BK": (BF, 128), "BKN": (BF, 128), "B32": (BF, 128), "BNK": (BF, 128), "B3K": (BF, 128), "BKC": (BF, 128),
-    "RST0": (BF, L), "RSTB": (BF, L), "RSTN": (BF, NC * C), "AK": (BF, 2 * NC * C), "SM": (BF, 2 * NC * C), "PCN": (H, 96), "TBC": (H, 96), "MC": (H, 96), "Z0": (BF, 192),
-    "RSTM": (BF, NC * C), "PRF": (H, 192), "CH": (F4, 8),
-    "IA": (I4, 96), "IB": (I4, 96), "IC": (I4, 96), "R6": (I4, 16), "C6": (I4, 16), "CM": (I4, 96),
-    "CL": (F4, 16), "C2": (F4, 16), "THR": (I4, 8), "NTH": (F4, 8), "NLIM": (F4, 8), "ACN": (F4, 8), "AS": (F4, 8), "AI": (I4, 8), "AI2": (I4, 8),
-    "VI": (I4, 24), "VI2": (I4, 24), "OFV": (U2, 24), "OFW": (U2, 16), "VL": (H, 16), "KB": (F4, 16), "WN": (F4, 16), "WN2": (F4, 16), "DV": (F4, 16), "WO": (F4, 16), "WO2": (F4, 16),
-    "SI": (I4, 1024), "SA": (I4, 1024), "SE": (H, 512), "SG": (H, 512), "SNE": (H, 512),
+    "SEI": (BF, 2048), "GG": (BF, 2048), "SX": (BF, 2000), "DF": (BF, 1024), "PP": (BF, 192), "ON1": (BF, 1024),
+    "ID": (BF, 128), "BK": (BF, 128), "BKN": (BF, 128), "BKC": (BF, 128), "W16": (BF, 16),
+    "RSTB": (BF, L), "RST0": (BF, C), "CZ": (BF, C), "CY": (BF, 2 * C), "C3": (BF, 3 * C), "LC": (BF, 2 * NC), "TRI": (BF, C), "TR1": (BF, C), "Z0": (BF, M),
+    "CM0": (H, 256), "CM1": (H, 256), "CB": (F4, 8),
+    "IA": (I4, C), "IB": (I4, 128), "IC": (I4, C), "ID4": (I4, C),
+    "THR": (I4, 8), "TH1": (I4, 8), "TH2": (I4, 8), "NTH": (F4, 8), "NLIM": (F4, 8), "ACN": (F4, 16), "AS": (F4, 8), "AI": (I4, 8), "AI2": (I4, 8), "SP": (F4, 8),
+    "SI": (I4, 1024),
 }
+ONE.update({_n: (BF, 128) for _n in SCALED})
 WHERE = {}
 _tot = {}
-for _n, (_d, _w) in [(n + str(h), x) for n, x in PER.items() for h in (0, 1)] + list(ONE.items()):
+for _n, (_d, _w) in [(n + str(h), x) for n, x in PER.items() for h in range(NH_)] + list(ONE.items()):
     WHERE[_n] = (_d, _tot.get(_d, 0), _w)
     _tot[_d] = _tot.get(_d, 0) + (_w + 15) // 16 * 16
 
 SCRATCH = {"p_" + _d: ("sbuf", [128, _w], _d) for _d, _w in _tot.items()}
 SCRATCH["tab"] = ("sbuf", [128, 4112], BF)
-for _n in ("scw", "stw", "sow"):
-    SCRATCH[_n] = ("sbuf", [128, 608], F4)
-for _h in (0, 1):
+SCRATCH["scw"] = ("sbuf", [128, 528], F4)
+SCRATCH["stw"] = ("sbuf", [128, 512], F4)
+for _h in range(NH_):
     for _t in range(4):
-        SCRATCH["m%d%d" % (_t, _h)] = ("sbuf", [128, 288], H)
+        SCRATCH["m%d%d" % (_t, _h)] = ("sbuf", [128, 4 * C], H)
         if _t < 3:
-            SCRATCH["o%d%d" % (_t, _h)] = ("sbuf", [128, 288], H)
-for _b in ("cm0", "cm1", "cm2", "pk", "pc", "ph", "px", "pm"):
+            SCRATCH["o%d%d" % (_t, _h)] = ("sbuf", [128, 3 * C], H)
+NPOOL = 3
+for _b in ("cm0", "cm1", "cm2", "bm", "bx0", "bx1", "by0", "by1"):
     SCRATCH[_b] = ("psum", [128, 512], F4)
-NLOAD, NOUT = 10, 7
-SEMAPHORES = ["v", "s", "t", "g", "loc"] + ["l%d" % i for i in range(NLOAD)] + ["a%d%d" % (t, h) for t in (1, 2, 3) for h in (0, 1)] + ["out%d" % i for i in range(NOUT)]
+NLOAD, NOUT = 2 * NH_ + 6, 3 * NH_ + 1
+SEMAPHORES = ["v", "s", "t", "g", "loc"] + ["l%d" % i for i in range(NLOAD)] + ["a%d%d" % (t, h) for t in (1, 2, 3) for h in range(NH_)] + ["out%d" % i for i in range(NOUT)]
+SEMAPHORES += ["k%d%d%d" % (t, h, j) for t in range(4) for h in range(NH_) for j in range(4)]
+MAGIC = 1.5 * 2.0 ** 30
 
-K = {"v": 1.0e-3, "t": 0.5e-3, "fix": 0.06, "wake": 0.08, "gat": 1.56, "hop": 3.5}
-SHIFTS = [5006, 5008, 5010, 5013, 5017, 5019, 5035, 5038, 5042, 5063, 5066, 5075, 5094, 5123, 5134, 5148, 5158, 5187, 5195, 5231, 5237, 5239, 6032, 6046, 6070, 6071, 6085,
-          6120, 6123, 6137, 6150, 6168, 6174, 6184, 6186, 6210, 6227, 16018, 16022, 16053, 16073, 16078, 16083, 16115, 16117, 16202, 16229, 16235, 25045, 25064, 25090, 25179,
-          25225, 25247, 25289, 25321, 25341, 31031, 31038, 31054, 31071, 31148, 31193, 31212, 31214, 31231, 31273, 31323, 36017, 36080, 36087, 36089, 36159, 36209, 36242, 36297,
-          36305, 46081, 46129, 46160, 46232]
+K = {"v": 1.0e-3, "t": 0.5e-3, "fix": 0.06, "wake": 0.08, "gat": 1.56, "sca": 3.8, "hop": 3.5, "lag": 9.0}
 def cv(n, k=1.0): return K["fix"] + K["v"] * max(64, n * k)
 def ct(*ns): return sum(K["t"] * max(64, n) for n in ns) + 0.03
 
-MODES = ["SV", "SV", "SV", "SV", "SV", "SS"]
+MODES = "SSSS" "SSSS" "SSSS"
+ON = {"ZSS": "s", "FAR": "s", "FKD": "s", "FKT": "s"}
 NENG = 8
 PLAN = {}
 
@@ -67,11 +70,16 @@ def build(T):
     ops = []
     now = [0]
 
-    def B(name, lo=0, hi=None, step=1):
+    def B(name, lo=0, hi=None, step=1, p=None):
         d, a, w = WHERE[name]
         hi = w if hi is None else hi
         t = T["p_" + d]
-        return t[:, a + lo:a + hi] if step == 1 else t[:, a + lo:a + hi:step]
+        rows = slice(0, 128) if p is None else slice(*p)
+        return t[rows, a + lo:a + hi] if step == 1 else t[rows, a + lo:a + hi:step]
+
+    def back(name, n, p):
+        d, a, w = WHERE[name]
+        return T["p_" + d][slice(*p), a + n - 1:(a - 1 if a else None):-1]
 
     def op(eng, rd, wr, cost, fn, banks=(), lat=0.0, sem=None, val=1, get=None, put=None):
         ops.append(dict(h=now[0], e=eng, r=rd.split(), w=wr.split(), c=cost, f=fn, lat=lat, sem=sem, val=val, b=list(banks), i=len(ops), get=get, put=put))
@@ -84,271 +92,308 @@ def build(T):
             return x
         return f
 
-    def group(out, pairs):
+    def group(out, pairs, start=True, stop=True):
         k = len(pairs)
-        return [(out if o is None else o, a, b, j == 0, j == k - 1) for j, (a, b, o) in enumerate(pairs)]
+        return [(out if len(x) == 2 else x[2], x[0], x[1], start and j == 0, stop and j == k - 1) for j, x in enumerate(pairs)]
 
     pool = lambda k: T["cm%d" % PLAN["bank"][k]]
     sel = lambda l, nm="SEL": B(nm, 128 * l, 128 * l + 128)
     V, S, TE, G, Y = "v", "s", "t", "g", "y"
 
-    def ts(rd, wr, out, i, s1, s2, o0, o1=None, n=96, k=1.0, banks=()):
+    def ts(rd, wr, out, i, s1, s2, o0, o1=None, n=C, k=1.0, banks=()):
         op(V, rd, wr, cv(n, k), (lambda q: q.tensor_scalar(out, i, s1, s2, o0, o1)) if o1 is not None else (lambda q: q.tensor_scalar(out, i, s1, None, o0)), banks)
-    def tt(rd, wr, out, a, b, o, n=96, k=2.0, banks=()):
+    def tt(rd, wr, out, a, b, o, n=C, k=2.0, banks=()):
         op(V, rd, wr, cv(n, k), lambda q: q.tensor_tensor(out, a, b, o), banks)
-    def cp(rd, wr, out, i, n=96, k=1.0, banks=()):
+    def cp(rd, wr, out, i, n=C, k=1.0, banks=()):
         op(V, rd, wr, cv(n, k), lambda q: q.tensor_copy(out, i), banks)
-    def scan(rd, wr, out, a, b, o0, o1, n=96, k=1.0, banks=()):
+    def scan(rd, wr, out, a, b, o0, o1, n=C, k=1.0, banks=()):
         op(V, rd, wr, cv(n, k), lambda q: q.tensor_tensor_scan(out, a, b, 0.0, o0, o1), banks)
-    def act(rd, wr, out, i, f, n=96, banks=(), k=1.0, **kw):
+    def act(rd, wr, out, i, f, n=C, banks=(), k=1.0, **kw):
         op(S, rd, wr, K["fix"] + K["v"] * n * k, lambda q: q.activation(out, i, f, **kw), banks)
     def pe(rd, wr, calls, bank, *ns):
         op(TE, rd, wr, ct(*ns), mm(calls), [bank])
 
-    def load(i, dst, out, src, eng=Y, rd="", kb=100):
-        op(eng, rd, dst, 0.1, lambda q: q.dma_start(out, src), lat=2.0 + kb / 250.0, sem="l%d" % i, val=16)
-    for h in (0, 1):
+    nl = [0]
+    def load(dst, out, src, eng=Y, rd="", kb=100):
+        op(eng, rd, dst, 0.1, lambda q: q.dma_start(out, src), lat=2.0 + kb / 250.0, sem="l%d" % nl[0], val=16)
+        nl[0] += 1
+    for h in range(NH_):
         s = slice(C * h, C * h + C)
-        load(2 * h, "LIt%d" % h, B("LI%d" % h, 96, 192), T.tl[:, s], kb=50)
-        load(2 * h + 1, "LId%d" % h, B("LI%d" % h, 0, 96), T.dl[:, s], kb=50)
+        load("LIt%d" % h, B("LI%d" % h, C, 2 * C), T.tl[:, s], kb=50)
+        load("LId%d" % h, B("LI%d" % h, 0, C), T.dl[:, s], kb=50)
         if h == 0:
-            load(4, "Z0", B("Z0"), T.z0[:], kb=50, eng=S)
-            op(V, "", "tabm", cv(8), lambda q: q.memset(T.tab[:, 2048:2056], -1.0))
-            load(5, "taba", T.tab[:, 0:2048], T.clk[:, 0:2048], kb=520)
-            load(6, "tabb", T.tab[:, 2049:4097], T.clk[:, 2048:4096], rd="tabm", eng=S, kb=520)
-    load(7, "SIc", B("SI", 0, 512), T.sc[:], kb=260)
-    load(8, "SIt", B("SI", 512, 1024), T.st[:], kb=260)
-    load(9, "THR", B("THR", 0, 1), T.th[:], kb=1)
+            load("Z0", B("Z0"), T.z0[:], kb=50, eng=S)
+            load("taba", T.tab[:, 16:2064], T.clk[:, 0:2048], kb=520)
+            load("tabb", T.tab[:, 2064:4112], T.clk[:, 2048:4096], eng=S, kb=520)
+            load("THR", B("THR", 0, 1), T.th[:], kb=1)
+    load("SIc", B("SI", 0, 512), T.sc[:], kb=260)
+    load("SIt", B("SI", 512, 1024), T.st[:], kb=260)
+    op(V, "", "tabm", cv(16), lambda q: q.memset(T.tab[:, 0:16], -1.0))
     TAB = "taba tabb tabm"
-    tab = T.tab[:, 0:4097]
+    tab = T.tab[:, 0:4112]
 
-    def ms(name, c):
-        op(V, "", name, cv(WHERE[name][2], 0.5), lambda q: q.memset(B(name), c))
+    def ms(name, c, lo=0, hi=None, step=1, p=None, key=None, rd=""):
+        n = len(range(lo, WHERE[name][2] if hi is None else hi, step))
+        op(V, rd, key or name, cv(n, 0.5), lambda q: q.memset(B(name, lo, hi, step, p), c))
     def iota(name, n, pat, base, cmul):
         op(G, "", name, 0.13 + 2 * K["v"] * n, lambda q: q.iota(B(name, 0, n), pat, base, cmul))
-    def aff(out, src, n, pat, cmp, base, cmul):
-        op(G, src, out, 0.17 + 2 * K["v"] * n, lambda q: q.affine_select(B(out, 0, n), B(src, 0, n), pat, cmp, 0.0, base, cmul))
+    def aff(out, src, n, pat, cmp, base, cmul, fill=0.0, at=0, p=None, key=""):
+        a = at if src == out else 0
+        op(G, src + (key if src == out else ""), out + key, 0.17 + 2 * K["v"] * n, lambda q: q.affine_select(B(out, at, at + n, p=p), B(src, a, a + n, p=p), pat, cmp, fill, base, cmul))
+    LO, HI = (0, 64), (64, 128)
     ms("ON1", 1.0)
+    aff("ID", "ON1", 128, [[-1, 128]], A.is_equal, 0, 1)
     aff("BKC", "ON1", 128, [[-16, 8], [0, 16]], A.is_ge, 0, 1)
     aff("BK", "BKC", 128, [[16, 8], [0, 16]], A.is_ge, 15, -1)
-    aff("ID", "ON1", 128, [[-1, 128]], A.is_equal, 0, 1)
-    iota("IB", 96, [[0, 6], [-1, 16]], 15, 0)
-    aff("RST0", "ON1", L, [[0, C], [1, 16]], A.is_gt, 0, 0)
-    aff("SEL", "ON1", 2048, [[-1, 16], [-16, 8], [0, 16]], A.is_equal, 0, 1)
-    iota("IA", 96, [[0, 96]], 0, 1)
-    iota("CM", 96, [[1, 96]], 0, 0)
-    iota("C6", 12, [[0, 2], [16, 6]], 0, 0)
-    aff("RSTM", "ON1", NC * C, [[0, NC], [1, C]], A.is_equal, 0, 0)
-    ms("ZSS0", 0.0)
-    ms("ZSS1", 0.0)
-    act("RST0", "RSTB", B("RSTB"), B("RST0"), F.Copy, n=L, scale=2 * BIG, bias=-BIG)
-    act("RSTM", "RSTN", B("RSTN"), B("RSTM"), F.Copy, n=NC * C, scale=BIG)
-    act("ON1", "GG", B("GG"), B("ON1"), F.Copy, n=2048, scale=0.0)
-    for p in range(16):
-        act("BK GG", "GGp%d" % p, B("GG", 129 * p, 128 * p + 128, 16), B("BK", 0, 128, 16), F.Copy, n=8)
-    GGK = " ".join("GGp%d" % p for p in range(16))
-    for out, src, k in (("IDN", "ID", -1), ("I8K", "ID", 8192), ("BKN", "BK", -1), ("BNK", "BK", -1000), ("I1K", "ID", 1000), ("INK", "ID", -1000),
-                        ("B32", "BK", -1 / 32), ("B3K", "BK", 32), ("I2K", "ID", 2048), ("IH", "ID", 0.5), ("IHN", "ID", -0.5)):
-        act(src, out, B(out), B(src), F.Copy, n=128, scale=float(k))
-    ts("IB", "TBC", B("TBC"), B("IB"), 1 / 16, None, A.mult)
+    aff("DF", "ON1", 1024, [[-1, 16], [-16, 4], [0, 16]], A.is_equal, -64, 1, key="u")
+    iota("IB", 128, [[0, 8], [-1, 16]], 15, 0)
+    iota("IA", C, [[0, C]], 0, 1)
+    iota("ID4", C, [[0, NC], [1, 16]], 0, 0)
+    act("ID DFu", "DFl", B("DF", 0, 64, p=LO), B("ID", 0, 64, p=LO), F.Copy, n=64, scale=-1.0)
+    for w in (64, 128, 256, 512):
+        act("DFl", "DFl", B("DF", w, 2 * w, p=LO), B("DF", 0, w, p=LO), F.Copy, n=w)
+    for j in range(4):
+        k = "q%d" % j
+        aff("SEI", "ON1", 512, [[-1, 4], [-16, 8], [0, 16]], A.is_equal, -4 * j, 1, at=512 * j, key=k)
+        aff("SEI", "SEI", 512, [[0, 4], [-1, 128]], A.not_equal, 0, 1, -1.0, at=512 * j, key=k)
+        aff("SEI", "SEI", 512, [[-1, 4], [-512, 8], [-31, 16]], A.not_equal, -4 * j, 32, at=512 * j, key=k)
+    ms("RSTB", BIG)
+    ms("RSTB", -BIG, 0, L, 16)
+    for h in range(NH_):
+        ms("ZSS%d" % h, 0.0)
+    ms("SX", 0.0)
+    ms("GG", 0.0)
+    ms("PP", 0.0)
+    for g in range(8):
+        a = 64 * (g % 2) + 16 * (g // 2)
+        act("BK SX", "SXg%d" % g, B("SX", 16 * (g // 2) + g % 2, 2000, 130), B("BK", a, a + 16), F.Copy, n=16, scale=-128.0)
+        act("BK GG", "GGg%d" % g, B("GG", 16 * g, 2048, 129), B("BK", 16 * g, 16 * g + 16), F.Copy, n=16, scale=-128.0)
+    act("ID PP", "PPa", B("PP", 64, 128, p=LO), B("ID", 0, 64, p=LO), F.Copy, n=64, scale=-128.0)
+    act("ID PP", "PPb", B("PP", 64, 128, p=HI), B("ID", 64, 128, p=HI), F.Copy, n=64, scale=-128.0)
+    GGK = " ".join("GGg%d" % g for g in range(8))
+    SXK = " ".join("SXg%d" % g for g in range(8)) + " PPa PPb"
+    for out, k in SCALED.items():
+        act("ID", out, B(out), B("ID"), F.Copy, n=128, scale=float(k))
+    act("BK", "BKN", B("BKN"), B("BK"), F.Copy, n=128, scale=-1.0)
+    act("BK", "W16a", B("W16", 0, 8), B("BK", 0, 128, 16), F.Copy, n=8)
+    act("BK", "W16b", B("W16", 8, 16), B("BK", 0, 128, 16), F.Copy, n=8, scale=-2.0)
+    def sums(name, parts):
+        a = 0
+        for w, hi, lo in parts:
+            if lo is None:
+                ms(name, hi / 128, a, a + w)
+            else:
+                ms(name, hi / 64, a, a + w, p=LO)
+                ms(name, lo / 64, a, a + w, p=HI)
+            a += w
+    sums("CZ", [(C, 2 * ZO, None)])
+    sums("CY", [(2 * C, 24576, 1)])
+    sums("C3", [(2 * C, -4, None), (C, ZO, -0.25)])
+    ms("LC", 0.0)
+    ms("LC", 128.0, NC, 2 * NC)
+    ms("RST0", 1.0)
+    ms("RST0", 0.0, 0, C, 16)
+    ms("CB", 2048.0, 0, 1, key="CB0")
+    ms("CB", float(np.log(EQ / (1 - EQ))), 1, 2, key="CB1")
+    ms("CB", 4096 * 2047.5, 2, 3, key="CB2")
+    ms("CB", -3072.0, 3, 4, key="CB3")
+    ms("CB", 32.0, 4, 5, key="CB4")
+    for j in (0, 1):
+        ts("IB", "CMa%d" % j, B("CM%d" % j, 0, 128), B("IB"), 1 / 2048, None, A.mult, n=128)
     ts("IA", "IC", B("IC"), B("IA"), 15, None, A.bitwise_and)
-    ts("IC", "PCN", B("PCN"), B("IC"), -15.0, 1 / 16, A.add, A.mult)
-    ts("CM", "MC", B("MC"), B("CM"), 1 / 256, None, A.mult)
-    tt("C6 IC", "R6", B("R6", 0, 12), B("C6", 0, 12), B("IC", 0, 12), A.add, n=8)
-    ts("R6", "CL", B("CL", 0, 12), B("R6", 0, 12), 1 / 256, 512 + 48 / 256, A.mult, A.add, n=8)
-    ts("R6", "C2", B("C2", 0, 12), B("R6", 0, 12), 512.0, None, A.add, n=8)
+    tt("ID4 IC", "TR1", B("TR1"), B("ID4"), B("IC"), A.subtract)
+    ts("TR1", "TRI", B("TRI"), B("TR1"), 0.0, 4096.0, A.is_lt, A.mult)
+    ts("TR1", "TR1", B("TR1"), B("TR1"), 0.0, 2048.0, A.not_equal, A.mult)
+    tt("TR1 TRI", "TRI", B("TRI"), B("TRI"), B("TR1"), A.add)
+    ts("IC", "SP", B("SP", 0, 1), B("IC", 0, 1), 512.0, None, A.add, n=1)
     ms("AS", 0.0)
-    ms("CH", -2048.0)
-    op(V, "", " ".join("AK%d%d" % (h, c) for h in (0, 1) for c in range(NC)), cv(2 * NC * C, 0.5), lambda q: q.memset(B("AK"), 512.0))
-    ts("THR", "NTH", B("NTH", 0, 1), B("THR", 0, 1), -1.0, -8192.0, A.mult, A.add, n=1)
-    cp("NTH", "NLIM0", B("NLIM", 0, 1), B("NTH", 0, 1), n=1)
+    tt("THR IC", "TH1", B("TH1", 0, 1), B("THR", 0, 1), B("IC", 0, 1), A.add, n=1)
+    ts("TH1", "TH2", B("TH2", 0, 1), B("TH1", 0, 1), 4, None, A.arith_shift_right, n=1)
+    ts("TH2", "NTH", B("NTH", 0, 1), B("TH2", 0, 1), -1.0, ZO - 512, A.mult, A.add, n=1)
+    ts("BK NTH", "CMb0", B("CM0", 128, 256), B("BK"), B("NTH", 0, 1), None, A.mult, n=128)
 
-    def encode(out, ok, src, sk, tmp, tk, pb, kb, bb, n):
-        ts(sk, tk, tmp, src, 1 + 2.0 ** -12, 2.0 ** -13 - 2048, A.mult, A.add, n=n)
-        ts(sk, kb, pb, src, 0.0, None, A.is_ge, n=n, banks=[bb])
-        tt(tk + " " + kb, ok, out, pb, tmp, A.mult, n=n, k=1, banks=[bb])
-    for h in (0, 1):
+    for h in range(NH_):
         m = T["m0%d" % h]
-        encode(m[:, 0:192], "m0%d" % h, B("LI%d" % h), "LIt%d LId%d" % (h, h), B("T1%d" % h), "T1%d" % h, T.pm[:, 192 * h:192 * h + 192], "KC MK", "pm", 192)
-        act("Z0", "m0%dz" % h, m[:, 192:288], B("Z0", C * h, C * h + C), F.Copy)
-    encode(T.scw[:, 0:512], "scw", B("SI", 0, 512), "SIc", B("SA", 0, 512), "SAc", T.px[:], "px", "px", 512)
-    encode(T.stw[:, 0:512], "stw", B("SI", 512, 1024), "SIt", B("SA", 512, 1024), "SAt", T.ph[:], "psH0 psH1 psV", "ph", 512)
-    op(V, "", "scwd", cv(96), lambda q: q.memset(T.scw[:, 512:608], 0.0))
-
-    def decode(out, ok, e, ek, sg, gk, ne, nk, n):
-        act(ek, gk, sg, e, F.Sign, n=n)
-        ts(ek, nk, ne, e, 0.0, None, A.not_equal, n=n, k=.5)
-        op(TE, "ID I2K IH IHN %s %s %s" % (ek, gk, nk), "dec" + gk, ct(n, n, n, n), mm(lambda: group(pool(gk)[:, 0:n], [
-            (B("ID"), e, None), (B("I2K"), ne, None), (B("IH"), ne, None), (B("IHN"), sg, None)])), get=gk)
-        op(S, "dec" + gk, ok, cv(n), lambda q: q.activation(out, pool(gk)[:, 0:n], F.Identity, bias=-1.0), put=gk)
+        ts("LIt%d LId%d" % (h, h), "m0%d" % h, m[:, 0:2 * C], B("LI%d" % h), 1 / 2048, -2047 / 2048, A.mult, A.add, n=2 * C)
+        act("Z0", "m0%dz" % h, m[:, 2 * C:3 * C], B("Z0", C * h, C * h + C), F.Copy, bias=ZO)
+    cp("SIc", "scw", T.scw[:, 0:512], B("SI", 0, 512), n=512)
+    cp("SIt", "stw", T.stw[:, 0:512], B("SI", 512, 1024), n=512)
+    op(V, "", "scwd", cv(16), lambda q: q.memset(T.scw[:, 512:528], 0.0))
 
     nblk = [0]
+    def newbank():
+        nblk[0] += 1
+        return "blk%d" % nblk[0]
+
     def chunk(t, h):
         now[0] = h
         m = T["m%d%d" % (t, h)]
         X = lambda n: n + str(h)
-        b = lambda n, *a: B(X(n), *a)
-        D, TT, Z = m[:, 0:96], m[:, 96:192], m[:, 192:288]
+        b = lambda n, *a, **k: B(X(n), *a, **k)
+        D, TT, Z, DT = m[:, 0:C], m[:, C:2 * C], m[:, 2 * C:3 * C], m[:, 0:2 * C]
         km = "m%d%d" % (t, h)
         kz = km + "z" if t == 0 else km
         x = lambda s: " ".join(X(w[1:]) if w[0] == "." else w for w in s.split())
-        pk, pc, ph, px, pm = T.pk, T.pc, T.ph, T.px, T.pm
-        cv0, cu0 = (96, 0) if h == 0 else (0, 96)
-        vo, uo = (6, 0) if h == 0 else (12, 18)
-        pv, pu, p0 = 192 + vo, 192 + uo, 192 + 12 * h
-        ts(km, x(".OFF"), b("OFF"), m[:, 0:192], 2048.0, None, A.add, n=192, k=.5)
-        cp(x(kz + " .ZSS"), x(".ZSS"), b("ZSS", 0, L, 16), Z, k=.5)
-        scan(x(".ZSS RST0"), x(".ZE"), b("ZE"), B("RST0"), b("ZSS"), A.mult, A.add, n=L, k=.5)
-        tt(x(TAB + " .OFF .ZE"), x(".MT"), b("MT"), tab.indirect(b("OFF", 96, 192)), b("ZE"), A.min, n=L, k=K["gat"])
-        pe(x(GGK + " ID ON1 .ZSS"), "psU%d" % h, group(pk[:, pu:pu + 6], [(B("ID"), B("ON1", 0, 6), None)] + [(sel(r, "GG"), b("ZSS", 16 * r, L, 256), None) for r in range(16)]), "pk", *[64] * 17)
-        pe(x(GGK + " ID TBC .MT"), "psK", group(pk[:, 0:96], [(B("ID"), B("TBC"), None)] + [(sel(r, "GG"), b("MT", 96 * r, 96 * r + 96), None) for r in range(16)]), "pk", *[96] * 17)
-        tt(x(TAB + " .OFF .ZE"), x(".SD"), b("SD"), tab.indirect(b("OFF", 0, 96)), b("ZE"), A.subtract, n=L, k=K["gat"])
-        act(x(".SD"), x(".AD"), b("AD"), b("SD"), F.Abs, n=L)
-        ts(km, x(".FL"), b("FL"), m[:, 0:192], 0.0, None, A.not_equal, n=192, k=.5)
-        pe(x("BK .FL"), "psA", group(pk[:, 256:352], [(B("BK"), b("FL", 96, 192), None)]), "pk", 96)
-        act("psA", x(".NH"), b("NH"), pk[:, 256:352], F.Relu, banks=["pk"], bias=2.0, scale=-2.0)
-        scan("psK RSTB", x(".MX"), b("MX"), B("RSTB", 0, 96), pk[:, 0:96], A.min, A.max, banks=["pk"])
-        ts(x(".MX"), x(".KI"), b("KI", 0, 6), b("MX", 15, 96, 16), -15 / 32, None, A.add, n=6)
-        tt(x(".MX .KI"), x(".QL"), b("QL", 0, 6), b("MX", 15, 96, 16), b("KI", 0, 6), A.subtract, n=6)
-        pe(x("SEL ID PCN .QL"), "psQ", group(None, [(B("ID"), B("PCN"), pk[:, 96:192])] + [(sel(r), b("QL", 0, 6), pk[:, 96 + 6 * r:102 + 6 * r]) for r in range(16)]), "pk", 96, *[64] * 16)
-        ts("psQ", x(".OH"), b("OH"), pk[:, 96:192], 0.0, None, A.is_equal, banks=["pk"])
-        tt(x(".OH " + km), x(".TH"), b("TH"), b("OH"), TT, A.mult)
-        pe(x(GGK + " .TH"), "psN%d" % h, group(pk[:, pv:pv + 6], [(sel(r, "GG"), b("TH", r, 96, 16), None) for r in range(16)]), "pk", *[64] * 16)
-        ts("psN%d psU%d" % (h, h), x(".VI"), B("VI", 12 * h, 12 * h + 12), pk[:, p0:p0 + 12], 1 - 2.0 ** -13, -0.5, A.mult, A.add, n=12, banks=["pk"])
-        ts(x(".VI"), x(".VI2"), B("VI2", 12 * h, 12 * h + 12), B("VI", 12 * h, 12 * h + 12), 511, None, A.bitwise_and, n=12)
-        cp(x(".VI2"), x(".OFV"), B("OFV", 12 * h, 12 * h + 12), B("VI2", 12 * h, 12 * h + 12), n=12)
-        ts("psN%d" % h, x(".OFN"), b("OFN", 0, 6), pk[:, pv:pv + 6], 2048.0, None, A.add, n=6, banks=["pk"])
-        act(x("scw scwd .OFV"), x(".CS"), b("CS"), T.scw[:, 0:512].indirect(B("OFV", 12 * h, 12 * h + 12)), F.Copy, n=192, k=K["gat"])
-        act(x("stw .OFV"), x(".CT"), b("CT"), T.stw[:, 0:512].indirect(B("OFV", 12 * h, 12 * h + 12)), F.Copy, n=192, k=K["gat"])
-        act(x(TAB + " .OFN"), x(".YK"), b("YK"), tab.indirect(b("OFN", 0, 6)), F.Copy, k=K["gat"])
-        def compare(j, src, ks, row, kr):
-            for k in range(4):
-                mode = MODES[2 * j + k // 2]
-                bank = "blk%d" % nblk[0]
-                nblk[0] += 1
-                op(TE, x("SEL IDN %s %s" % (ks, kr)), bank, ct(*[96] * 8), mm((lambda bank, k: lambda: [c for i in range(4) for c in group(
-                    pool(bank)[:, 96 * i:96 * i + 96], [(sel(4 * k + i), src, None), (B("IDN"), row, None)])])(bank, k)), get=bank)
-                a0 = 384 * k
-                eq, cx = b("EQ%d" % j, a0, a0 + 384), b("CX", L * j + a0, L * j + a0 + 384)
-                ke, kx = x(".EQ%d_%d_" % (j, k)), x(".CX%d_%d_" % (j, k))
-                if mode == "V":
-                    op(V, bank, ke, cv(384), (lambda bank, eq: lambda q: q.tensor_scalar(eq, pool(bank)[:, 0:384], 0.0, None, A.is_equal))(bank, eq), put=bank)
-                    continue
-                op(S, bank, kx, cv(384), (lambda bank, cx: lambda q: q.activation(cx, pool(bank)[:, 0:384], F.Abs))(bank, cx), put=bank)
-                if mode == "SS":
-                    act(kx, ke, eq, cx, F.Relu, n=384, bias=1.0, scale=-1.0)
-                elif k % 2:
-                    k0, a0 = k - 1, a0 - 384
-                    ts(kx + " " + x(".CX%d_%d_" % (j, k0)), ke + " " + x(".EQ%d_%d_" % (j, k0)), b("EQ%d" % j, a0, a0 + 768), b("CX", L * j + a0, L * j + a0 + 768), 0.0, None, A.is_equal, n=768, k=.5)
-        eqk = lambda j: " ".join(x(".EQ%d_%d_" % (j, k)) for k in range(4))
-        eqb = lambda j, l: b("EQ%d" % j, 96 * l, 96 * l + 96)
-        compare(0, D, km, TT, km)
-        pe(x(GGK + " ID %s .OH" % eqk(0)), "psC", group(pc[:, 0:96], [(sel(l, "GG"), eqb(0, l), None) for l in range(16)]) +
-           group(pc[:, 96:192], [(B("ID"), eqb(0, l), None) for l in range(16)] + [(B("ID"), b("OH"), None)]), "pc", *[96] * 33)
-        pe(x(GGK + " I8K .AD .FL"), "psD", group(pc[:, 192:288], [(B("I8K"), b("FL", 0, 96), None)] + [(sel(p, "GG"), b("AD", p, L, 16), None) for p in range(16)]), "pc", *[96] * 17)
-        act("psD NLIM%d" % t, x(".F1"), b("F1"), pc[:, 192:288], F.Relu, banks=["pc"], bias=B("NLIM", t, t + 1))
-        act("psC", "KC", pm[:, 0:192], pc[:, 0:192], F.Relu, n=192, banks=["pc", "pm"], bias=1.0, scale=-1.0)
-        tt("KC " + km, x(".DT1"), b("DT1"), pm[:, 0:192], m[:, 0:192], A.mult, n=192, k=1, banks=["pm"])
-        ts(x(".DT1"), x(".OFX"), b("OFX"), b("DT1", 0, 96), 2048.0, None, A.add, k=.5)
-        act(x(TAB + " .OFX"), x(".XT"), b("XT"), tab.indirect(b("OFX")), F.Copy, n=L, k=K["gat"])
-        tt(x("psC .F1"), x(".FAR"), b("FAR"), pc[:, 0:96], b("F1"), A.mult, k=1, banks=["pc"])
-        ts(x(".DT1"), x(".FD1"), b("FD1"), b("DT1"), 0.0, None, A.not_equal, n=192, k=.5)
-        scan(x(".XT RSTB"), x(".TP"), b("TP"), B("RSTB"), b("XT"), A.min, A.max, n=L, k=.5)
-        compare(1, D, km, b("CS", cv0, cv0 + 96), x(".CS"))
-        compare(2, TT, km, b("CT", cv0, cv0 + 96), x(".CT"))
-        for j in (0, 1):
-            pe("ID " + eqk(1 + j), "psH%d" % j, group(ph[:, 96 * j:96 * j + 96], [(B("ID"), eqb(1 + j, l), None) for l in range(16)]), "ph", *[96] * 16)
-        act("psH0 psH1", x(".HC"), b("HC"), ph[:, 0:192], F.Copy, n=192, banks=["ph"], bias=1 / 64)
-        far, left, nh = b("FAR"), b("FD1", 0, 96), b("NH")
-        calls = group(px[:, 192:288], [(B("ID"), B("ON1", 0, 96), None), (B("BKN"), left, None), (B("BNK"), far, None), (B("I1K"), nh, None)])
-        calls += group(px[:, 288:384], [(B("BK"), left, None), (B("BNK"), far, None), (B("INK"), nh, None)])
-        calls += group(px[:, 384:480], [(B("BK"), far, None)])
-        pe(x("ID ON1 BK BKN BNK I1K INK .FAR .FD1 .NH"), "px", calls, "px", *[96] * 8)
-        act("px CH", "MK", pm[:, 192:480], px[:, 192:480], F.Sigmoid, n=288, banks=["px", "pm"], bias=B("CH", 0, 1), scale=4096.0)
-        tt(x("MK .NH"), x(".PRF"), B("PRF", 96 * h, 96 * h + 96), pm[:, 192:288], nh, A.is_gt, k=1, banks=["pm"])
-        calls = [(px[:, 0:192], B("ID"), b("HC"), True, False), (px[:, 0:192], B("ID"), b("FD1"), False, False)]
-        for j in (0, 1):
-            for i, (w, y) in enumerate(((B("B32"), left), (B("BNK"), far), (B("I1K"), nh))):
-                calls.append((px[:, 96 * j:96 * j + 96], w, y, False, j == 1 and i == 2))
-        pe(x("ID B32 BNK I1K .HC .FD1 .FAR .NH"), "pxx px", calls, "px", 192, 192, *[96] * 6)
-        act("pxx", "KC", pm[:, 0:192], px[:, 0:192], F.Sigmoid, n=192, banks=["px", "pm"], scale=-16384.0)
-        for j, ck in ((0, ".CS"), (1, ".CT")):
-            s0, s1 = 96 * j, 96 * j + 96
-            tt(x("MK .DT1"), x(".P2%s_" % j), b("P2", s0, s1), pm[:, 288:384], b("DT1", s0, s1), A.mult, k=1, banks=["pm"])
-            tt(x("MK " + ck), x(".P3%s_" % j), b("P3", s0, s1), pm[:, 192:288], b(ck[1:], cu0, cu0 + 96), A.mult, k=1, banks=["pm"])
-            tt(x("KC " + ck), x(".P1%s_" % j), b("P1", s0, s1), pm[:, s0:s1], b(ck[1:], cv0, cv0 + 96), A.mult, k=1, banks=["pm"])
-        pe(x("ID IDN %s .YK" % kz), "psZ", group(pc[:, 384:480], [(B("ID"), Z, None), (B("IDN"), b("YK"), None)]), "pc", 96, 96)
-        act("psZ", x(".ZA"), b("ZA"), pc[:, 384:480], F.Abs, banks=["pc"])
-        pe(x("ID .YK .TP"), "psG", group(pk[:, 352:448], [(B("ID"), b("YK"), None), (B("ID"), b("TP", 15, L, 16), None)]), "pk", 96, 96)
-        act("psG", x(".ZG"), b("ZG"), pk[:, 352:448], F.Copy, banks=["pk"], bias=1023.75, scale=0.5)
-        act(x(".ZG"), x(".ZGI"), b("ZGI"), b("ZG"), F.Copy, bias=-1024.0)
-        tt(x("MK .ZA"), x(".ZA2"), b("ZA2"), pm[:, 384:480], b("ZA"), A.mult, k=1, banks=["pm"])
-        tt(x("MK .ZGI"), x(".ZG2"), b("ZG2"), pm[:, 288:384], b("ZGI"), A.mult, k=1, banks=["pm"])
-        tt(x("MK " + kz), x(".ZR"), b("ZR"), pm[:, 192:288], Z, A.mult, k=1, banks=["pm"])
-        calls = group(px[:, 0:192], [(B("ID"), b("P2"), None), (B("ID"), b("P3"), None), (B("ID"), b("P1"), None)])
-        calls += group(px[:, 192:288], [(B("ID"), b("ZA2"), None), (B("ID"), b("ZR"), None), (B("ID"), b("ZG2"), None)])
-        pe(x("ID .P10_ .P11_ .P20_ .P21_ .P30_ .P31_ .ZA2 .ZG2 .ZR"), "px pxx", calls, "px", 192, 192, 192, 96, 96, 96)
-        if t < 3:
-            ko = "o%d%d" % (t, h)
-            act("px", ko, T[ko][:], px[:, 0:288], F.Copy, n=288, banks=["px"])
-            op(G, ko, "m%d%d" % (t + 1, h), 1.0, ("send", t, h), lat=K["hop"], sem="a%d%d" % (t + 1, h), val=NENG)
+        nx, ny = "bx%d" % (h % 2), "by%d" % (h % 2)
+        bm, bx, by = T.bm, T[nx], T[ny]
+        kx = lambda *js: " ".join(nx + str(j) for j in js)
+        ky = lambda *js: " ".join(ny + str(j) for j in js)
+        c = lambda bank, i, j=None: bank[:, C * i:C * (i + 1 if j is None else j)]
+        P = (0, C)
+        ones = B("ON1", 0, 128)
+        def stack(j, wr, out, src):
+            op(Y, km, x(wr), 0.1, lambda q: q.dma_start(out, src), lat=2.1, sem="k%d%d%d" % (t, h, j), val=16)
+        stack(0, ".SAu", b("SA", p=HI), m[0:64, 0:2 * C])
+        stack(1, ".SAl", b("SA", 0, C, p=LO), m[0:64, C:2 * C])
+        stack(2, ".SBl", b("SB", p=LO), m[64:128, 0:2 * C])
+        stack(3, ".SBu", b("SB", 0, C, p=HI), m[64:128, C:2 * C])
+        ts(km, x(".OFT"), b("OFT"), TT, 2048.0, 2063.0, A.mult, A.add, k=.5)
+        if ON["ZSS"] == V:
+            cp(x(kz + " .ZSS"), x(".ZSS"), b("ZSS", 0, L, 16), Z, k=.5)
         else:
-            act("px", x(".FIN"), b("FIN"), px[:, 0:288], F.Copy, n=288, banks=["px"])
-            decode(b("OUT", 0, 192), x(".OUTa"), b("FIN", 0, 192), x(".FIN"), b("FSG"), x(".FSG"), b("FNE"), x(".FNE"), 192)
-            cp(x(".FIN"), x(".OUTz"), b("OUT", 192, 288), b("FIN", 192, 288))
-            s = slice(C * h, C * h + C)
-            for j, (y, k, a) in enumerate(((T.yd, ".OUTa", 0), (T.yt, ".OUTa", 96), (T.yz, ".OUTz", 192))):
-                op(Y, x(k), "y%d%d" % (j, h), 0.1, (lambda y, a: lambda q: q.dma_start(y[:, s], b("OUT", a, a + 96)))(y, a), lat=2.2, sem="out%d" % (3 * h + j), val=16)
-            decode(b("TD"), x(".TD"), b("DT1", 96, 192), x(".DT1"), b("TSG"), x(".TSG"), b("TNE"), x(".TNE"), 96)
-        if t < 3:
-            pe(x("BK BKN BNK .FL .FD1 .FAR"), "psS", group(pc[:, 288:384], [(B("BK"), b("FL", 0, 96), None), (B("BKN"), left, None), (B("BNK"), far, None)]), "pc", 96, 96, 96)
-            act("psS", x(".JK ACN%d%d" % (t, h)), b("JK"), pc[:, 288:384], F.Relu, banks=["pc"], accum_out=B("ACN", 2 * t + h, 2 * t + h + 1))
-
-    def proofs(t):
-        now[0] = 0
-        ph, n = T.ph, 12
-        w = lambda nm: B(nm, 0, 12)
-        v = B("VI2", 6, 18)
-        cp("VI20 VI21", "VL", w("VL"), v, n=n)
-        tt("VI20 VI21 CL", "KB", w("KB"), v, w("CL"), A.add, n=n)
-        tt("VI20 VI21 C2", "DV", w("DV"), v, w("C2"), A.subtract, n=n)
-        for h in (0, 1):
-            pe("ID MC SEL B3K VL PRF%d" % h, "psV", group(None, [(B("ID"), B("MC"), ph[:, 192:288])] + [(sel(r), B("VL", 6 * h, 6 * h + 6), ph[:, 192 + r:288:16]) for r in range(16)] +
-               [(B("B3K"), B("PRF", 96 * h, 96 * h + 96), ph[:, 192:288])]), "ph", 96, 96, *[64] * 16)
-            for c in range(NC):
-                a = 96 * (NC * h + c)
-                act("psV KB", "AK%d%d" % (h, c), B("AK", a + 16 * c, a + 96), ph[:, 192 + 16 * c:288], F.Abs, n=96 - 16 * c, banks=["ph"], bias=B("KB", 6 * h + c, 6 * h + c + 1), scale=-1.0)
-            a0, a1 = NC * C * h, NC * C * h + NC * C
-            scan("RSTN " + " ".join("AK%d%d" % (h, c) for c in range(NC)), "SM%d" % h, B("SM", a0, a1), B("RSTN"), B("AK", a0, a1), A.max, A.min, n=NC * C, k=.5)
-        pe(GGK + " PRF0 PRF1", "psP", group(ph[:, 384:396], [(sel(r, "GG"), B("PRF", r, 192, 16), None) for r in range(16)]), "ph", *[64] * 16)
-        ts("SM0 SM1", "WN", w("WN"), B("SM", 95, 2 * NC * C, 96), 47.5 / 256, 1 / 16, A.is_ge, A.mult, n=n)
-        tt("psP WN", "WN2", w("WN2"), ph[:, 384:396], w("WN"), A.mult, n=n, banks=["ph"])
-        tt("WN2 DV", "WO", w("WO"), w("WN2"), w("DV"), A.mult, n=n)
-        tt("WO C2", "WO2", w("WO2"), w("WO"), w("C2"), A.add, n=n)
-        cp("WO2", "OFW", w("OFW"), w("WO2"), n=n)
-        for h in (0, 1):
-            o = B("OFW", 6 * h, 6 * h + 6)
-            if t < 3:
-                cp("OFW DT1%d" % h, "scw scwd", T.scw[:, 0:608].indirect(o), B("DT1%d" % h, 96, 192), k=3)
+            act(x(kz + " .ZSS"), x(".ZSS"), b("ZSS", 0, L, 16), Z, F.Copy)
+        scan(x(".ZSS RSTB"), x(".ZE"), b("ZE"), B("RSTB"), b("ZSS"), A.min, A.max, n=L, k=.5)
+        tt(x(TAB + " .OFT .ZE"), x(".GD"), b("GD"), tab.indirect(b("OFT")), b("ZE"), A.subtract, n=L, k=K["gat"])
+        ts(x(".GD"), x(".GN"), b("GN"), b("GD"), ZO, 0.0, A.add, A.min, n=L, k=.5)
+        ts(km, x(".FL"), b("FL"), DT, -1.0, None, A.is_gt, n=2 * C, k=.5)
+        pe(x("BK .FL"), kx(4, "o"), group(c(bx, 4), [(B("BK"), b("FL", C, 2 * C))]), nx, C)
+        act(kx(4) + " CB4", x(".NH"), b("NH"), c(bx, 4), F.Relu, banks=[nx], bias=B("CB", 4, 5), scale=-32.0)
+        cm = "CM%d" % (t % 2)
+        calls = [(B("ON1", 0, C), B(cm), bm[0:C, 0:256]), (b("FL", C, 2 * C), B("I8K"), bm[0:C, 128:256])]
+        calls += [(b("GD", p, L, 16), B("W16", 0, 8), bm[0:C, 128 + p:256:16]) for p in range(16)]
+        calls += [(b("GN", p, L, 16), B("W16"), bm[0:C, p:256:16]) for p in range(16)]
+        pe(x("ON1 CMa%d CMb%d I8K W16a W16b .FL .GD .GN" % (t % 2, t % 2)), "psK psD", group(None, calls), "bm", 256, 128, *[64] * 32)
+        scan("psK RSTB", x(".MX"), b("MX", p=P), B("RSTB", 0, 128, p=P), bm[0:C, 0:128], A.min, A.max, n=128, banks=["bm"])
+        act("psD CB0", x(".NF"), b("NF", p=P), bm[0:C, 128:256], F.Sigmoid, n=128, banks=["bm"], bias=B("CB", 0, 1, p=P), scale=-4096.0)
+        scan(x(".MX RSTB"), x(".SM"), back(X("SM"), 128, P), B("RSTB", 0, 128, p=P), back(X("MX"), 128, P), A.min, A.max, n=128)
+        tt(x("psK .SM"), x(".OH"), b("OH", p=P), bm[0:C, 0:128], b("SM", p=P), A.is_equal, n=128, k=1, banks=["bm"])
+        pe(x(".OH I2K"), "psO", group(bm[:, 256:256 + C], [(b("OH", p=P), B("I2K", 0, C, p=P))]), "bm", C)
+        tt("psO " + km, x(".TH"), m[:, 3 * C:4 * C], bm[:, 256:256 + C], TT, A.mult, k=1, banks=["bm"])
+        pl = bm[:, 352:352 + 2 * NC]
+        pe(x(GGK + " ID LC .TH " + kz), "psN", group(pl, [(B("ID"), B("LC"))] + [(sel(r, "GG"), m[:, 2 * C + r:4 * C:16]) for r in range(16)]), "bm", *[64] * 17)
+        ts("psN", x(".VI"), b("VI"), pl, -1 / 128, None, A.mult, n=2 * NC, banks=["bm"])
+        ts("psN", x(".OFN"), b("OFN", 0, NC), bm[:, 352 + NC:352 + 2 * NC], -1 / 128, 2064.0, A.mult, A.add, n=NC, banks=["bm"])
+        ts(x(".VI"), x(".VI2"), b("VI2"), b("VI"), 511, None, A.bitwise_and, n=2 * NC)
+        cp(x(".VI2"), x(".OFV"), b("OFV"), b("VI2"), n=2 * NC)
+        for j, (win, kw, a) in enumerate(((T.scw, "scw", NC), (T.stw, "stw", NC), (T.scw, "scw", 0), (T.stw, "stw", 0))):
+            act(x(kw + " .OFV"), x(".CV%d_" % j), b("CV", C * j, C * j + C), win[:, 0:512].indirect(b("OFV", a, a + NC)), F.Copy, k=K["gat"], scale=1 / 2048, bias=-2047 / 2048)
+        act(x(TAB + " .OFN"), x(".YK"), b("YK"), tab.indirect(b("OFN", 0, NC)), F.Relu, k=K["gat"])
+        def compare(j, col, to, kt, bank_to, last, also=None):
+            for k in range(NB):
+                bank, w, up = newbank(), LB * C, k >= NB // 2
+                ss = range(LB * k % 8, LB * k % 8 + LB)
+                src, ks = b("SB" if up else "SA", C * col, C * col + C), (".SBl .SBu" if up else ".SAu .SAl") + (" .SB2" if up else " .SA2") * col
+                op(TE, x("DFu DFl " + ks), bank, ct(*[C] * LB), mm((lambda bank, ss, src: lambda: [
+                    (pool(bank)[:, C * i:C * i + C], sel(s, "DF"), src, True, True) for i, s in enumerate(ss)])(bank, ss, src)), get=bank)
+                eq, ke = b("EQ%d" % j, w * k, w * k + w), x(".EQ%d_%d_" % (j, k))
+                if MODES[(4 * j + k * 4 // NB)] == "V":
+                    op(V, bank, ke, cv(w), (lambda bank, eq: lambda q: q.tensor_scalar(eq, pool(bank)[:, 0:w], 0.0, EQ, A.is_equal, A.mult))(bank, eq), put=bank)
+                else:
+                    op(S, bank + " CB1", ke, cv(w), (lambda bank, eq: lambda q: q.activation(eq, pool(bank)[:, 0:w], F.Sigmoid, bias=B("CB", 1, 2), scale=524288.0))(bank, eq), put=bank)
+                one = lambda s: B("PP", 0, 128) if up else B("PP", 64, 192)
+                two = lambda s: B("SX", 976 * up + 128 * s, 976 * up + 128 * s + 128)
+                calls = []
+                for i, s in enumerate(ss):
+                    e = b("EQ%d" % j, w * k + C * i, w * k + C * i + C)
+                    calls.append(((two if up else one)(s), e, to))
+                    if also is not None: calls.append(((one if up else two)(s), e, also))
+                pe(SXK + " " + ke, kt, group(None, calls, False, last and k == NB - 1), bank_to, *[C] * len(calls))
+        pe("ID " + km, kx(0, 1, "o"), group(c(bx, 0, 2), [(B("ID"), DT)], True, False), nx, 2 * C)
+        compare(0, 0, c(bx, 1), kx(0, 1, "o"), nx, True, c(bx, 0))
+        ts(kx(0, 1), x(".R0"), b("R0"), c(bx, 0, 2), MAGIC, -MAGIC, A.add, A.add, n=2 * C, banks=[nx])
+        tt(x(kx(0, 1) + " .R0"), x(".DT1"), b("DT1"), c(bx, 0, 2), b("R0"), A.subtract, n=2 * C, k=1, banks=[nx])
+        D1, T1 = b("DT1", 0, C), b("DT1", C, 2 * C)
+        ts(x(".DT1"), x(".OFX"), b("OFX"), D1, 2048.0, 2063.0, A.mult, A.add, k=.5)
+        def filled(j, key, src, k, banks):
+            if ON["FK" + "DT"[j]] == V:
+                ts(key, x(".FK%d_" % j), b("FK", C * j, C * j + C), src, -1.0, None, A.is_gt, k=k, banks=banks)
             else:
-                cp("OFW TD%d" % h, "sow", T.sow[:, 0:608].indirect(o), B("TD%d" % h), k=3)
+                act(key + " CB2", x(".FK%d_" % j), b("FK", C * j, C * j + C), src, F.Sigmoid, banks=banks, bias=B("CB", 2, 3), scale=2.0 ** 23)
+        filled(0, x(".DT1"), D1, .5, [])
+        act(x(TAB + " .OFX"), x(".XT"), b("XT"), tab.indirect(b("OFX")), F.Copy, n=L, k=K["gat"])
+        scan(x(".XT RSTB"), x(".TP"), b("TP"), B("RSTB"), b("XT"), A.min, A.max, n=L, k=.5)
+        oh = (b("OH", p=P), B("I3N", 0, C, p=P))
+        pe(x(".NF .DT1 I128N IDN"), kx(3, "o"), group(c(bx, 3), [(B("IDN"), T1), (b("NF", p=P), B("I128N", 0, C, p=P))]), nx, C, C)
+        act(kx(3) + " CB3", x(".FAR"), b("FAR"), c(bx, 3), F.Relu, banks=[nx], scale=2048.0, bias=B("CB", 3, 4))
+        pe(x(".OH .DT1 I3N ID"), kx(4, "o"), group(c(bx, 4), [(B("ID"), T1), oh]), nx, C, C)
+        filled(1, kx(4), c(bx, 4), 1, [nx])
+        act(kx(4) + " CB0", x(".TN"), b("TN"), c(bx, 4), F.Relu, banks=[nx], bias=B("CB", 0, 1), scale=2048.0)
+        far, left, nh = b("FAR"), b("FK", 0, C), b("NH")
+        ng = b("NG", 0, C)
+        pe(x("ID IDN BK BKN .FAR .FK0_ .NH"), ky(2, 3, 4, "o"), group(c(by, 2), [(B("BKN"), left), (B("ID"), nh), (B("BK"), far)]) +
+           group(c(by, 3), [(B("BKN"), left), (B("IDN"), nh), (B("BKN"), far)]) + group(c(by, 4), [(B("BK"), far)]), ny, *[C] * 7)
+        act(ky(2, 3) + " CB0", x(".NG"), b("NG"), c(by, 2, 4), F.Sigmoid, n=2 * C, banks=[ny], bias=B("CB", 0, 1), scale=4096.0)
+        tt(x(ky(4) + " .YK"), x(".YM"), b("YM"), c(by, 4), b("YK"), A.min, k=1, banks=[ny])
+        pe(x("ID IDN I512 .YM .NG " + kz), kx(3, "o"), group(c(bx, 3), [(B("ID"), Z), (B("I512"), ng), (B("IDN"), b("YM"))]), nx, C, C, C)
+        act(kx(3), x(".A2z"), b("A2", 2 * C, 3 * C), c(bx, 3), F.Copy, banks=[nx], bias=-512.0)
+        pe(x("ID IDN I3N I512N ON1 CZ .DT1 .OH .YM .NG " + kz), kx(0, 1, 2, "o"), group(None, [(B("ID"), b("DT1"), c(bx, 0, 2)), oh + (c(bx, 1),), (B("I512N"), ng, c(bx, 0)), (B("I512N"), ng, c(bx, 1))]) +
+           group(c(bx, 2), [(ones, B("CZ")), (B("IDN"), Z), (B("ID"), b("YM"))]), nx, 2 * C, *[C] * 6)
+        cp(x(".CV0_ .CV1_"), x(".SAl .SA2"), b("SA", p=LO), b("CV", 0, 2 * C, p=LO), n=2 * C, k=.5)
+        cp(x(".CV0_ .CV1_"), x(".SBu .SB2"), b("SB", p=HI), b("CV", 0, 2 * C, p=HI), n=2 * C, k=.5)
+        pe(x("ON1 CY I3N .FK0_ .FK1_"), ky(0, 1, "o"), group(c(by, 0, 2), [(ones, B("CY")), (B("I3N"), b("FK"))], True, False), ny, 2 * C, 2 * C)
+        compare(1, 0, c(by, 0), ky(0, 1, "o"), ny, False)
+        compare(2, 1, c(by, 1), ky(0, 1, "o"), ny, True)
+        act(ky(0, 1), x(".R1"), b("R1"), c(by, 0, 2), F.Copy, n=2 * C, banks=[ny], bias=24.0)
+        tt(x(ky(0, 1) + " .R1"), x(".M1"), b("M1"), c(by, 0, 2), b("R1"), A.subtract, n=2 * C, k=1, banks=[ny])
+        pe(x("ID I512N BK .M1 .NG .FAR"), ky(0, 1, "o"), group(None, [(B("ID"), b("M1"), c(by, 0, 2))] + [(w, y, c(by, j)) for j in (0, 1) for w, y in ((B("I512N"), ng), (B("BK"), far))]), ny, 2 * C, *[C] * 4)
+        tt(x(ky(0, 1) + " .CV0_ .CV1_"), x(".A2"), b("A2", 0, 2 * C), c(by, 0, 2), b("CV", 0, 2 * C), A.min, n=2 * C, k=1, banks=[ny])
+        tt(x(kx(0, 1, 2) + " .A2 .A2z"), x(".A3"), b("A3"), c(bx, 0, 3), b("A2"), A.max, n=3 * C, k=1, banks=[nx])
+        bank = newbank()
+        op(TE, x("ON1 C3 ID I4 BKN IH I512N .CV2_ .CV3_ .NG .FAR .YK .TP"), bank, ct(3 * C, 2 * C, *[C] * 7), mm(lambda: group(None, [
+            (ones, B("C3"), c(pool(bank), 0, 3)), (B("ID"), b("CV", 2 * C, 4 * C), c(pool(bank), 0, 2))] +
+            [(w, y, c(pool(bank), j)) for j in (0, 1) for w, y in ((B("I4"), ng), (B("BKN"), far))] +
+            [(w, y, c(pool(bank), 2)) for w, y in ((B("I512N"), ng), (B("IH"), b("YK")), (B("IH"), b("TP", 15, L, 16)))])), get=bank)
+        ko, out = ("o%d%d" % (t, h), T["o%d%d" % (t, h)][:]) if t < 3 else (x(".FIN"), b("FIN"))
+        op(V, x(bank + " .A3"), ko, cv(3 * C), lambda q: q.tensor_tensor(out, c(pool(bank), 0, 3), b("A3"), A.max), put=bank)
+        if t < 3:
+            op(G, ko, "m%d%d" % (t + 1, h), 1.0, ("send", HOPS[t], T["m%d%d" % (t + 1, h)][:, 0:3 * C], out), lat=K["hop"], sem="a%d%d" % (t + 1, h), val=NENG)
+            pe(x("BK BKN .FL .FK0_ .FAR"), "psS", group(bm[:, 384:384 + C], [(B("BK"), b("FL", 0, C)), (B("BKN"), left), (B("BKN"), far)]), "bm", C, C, C)
+            act("psS", x(".JK ACN%d%d" % (t, h)), b("JK"), bm[:, 384:384 + C], F.Relu, banks=["bm"], accum_out=B("ACN", NH_ * t + h, NH_ * t + h + 1))
+        else:
+            ts(ko, x(".R0"), b("R0"), b("FIN", 0, 2 * C), -1.0, None, A.max, n=2 * C, k=.5)
+            act(x(".R0"), x(".OUTa"), b("OUT", 0, 2 * C), b("R0"), F.Copy, n=2 * C, scale=2048.0, bias=2047.0)
+            ts(ko, x(".OUTz"), b("OUT", 2 * C, 3 * C), b("FIN", 2 * C, 3 * C), -ZO, None, A.add)
+            s = slice(C * h, C * h + C)
+            for j, (y, k) in enumerate(((T.yd, ".OUTa"), (T.yt, ".OUTa"), (T.yz, ".OUTz"))):
+                op(Y, x(k), "y%d%d" % (j, h), 0.1, (lambda y, j: lambda q: q.dma_start(y[:, s], b("OUT", C * j, C * j + C)))(y, j), lat=2.2, sem="out%d" % (3 * h + j), val=16)
+
+    def proofs(t, h):
+        now[0] = h
+        X = lambda n: n + str(h)
+        b = lambda n, *a, **k: B(X(n), *a, **k)
+        x = lambda s: " ".join(X(w[1:]) if w[0] == "." else w for w in s.split())
+        bank = newbank()
+        cp(x(".VI2"), x(".VL"), b("VL"), b("VI2", NC, 2 * NC), n=NC)
+        op(TE, x("ID TRI SEIq0 SEIq1 SEIq2 SEIq3 I2KN .VL .NG"), bank, ct(C, C, *[64] * 16), mm(lambda: group(None, [(B("ID"), B("TRI"), pool(bank)[:, 0:C])] + [
+            (sel(r, "SEI"), b("VL"), pool(bank)[:, r:C:16]) for r in range(16)] + [(B("I2KN"), b("NG", C, 2 * C), pool(bank)[:, 0:C])])), get=bank)
+        op(V, bank + " SP", x(".EP"), cv(C), lambda q: q.tensor_scalar(b("EP"), pool(bank)[:, 0:C], 0.0, B("SP", 0, 1), A.is_equal, A.mult), put=bank)
+        scan(x(".EP RST0"), x(".LS"), b("LS"), B("RST0"), b("EP"), A.mult, A.max, k=.5)
+        tt(x(".LS .VL"), x(".WO"), b("WO"), b("LS", 15, C, 16), b("VL"), A.max, n=NC)
+        cp(x(".WO"), x(".OFW"), b("OFW", 0, 2 * NC, 2), b("WO"), n=NC)
+
+    def writes(t, h):
+        now[0] = h
+        for j in range(NC):
+            ts("OFW%d TN%d scwd" % (h, h), "scw", T.scw[:, 0:528].indirect(B("OFW%d" % h, 2 * j, 2 * j + 1)), B("TN%d" % h, 16 * j, 16 * j + 16), 1.0, -1.0, A.mult, A.add, n=16, k=K["sca"])
 
     for t in range(4):
-        if t == 3:
-            cp("scw", "SE", B("SE"), T.scw[:, 0:512], n=512)
-            op(V, "", "sowd", cv(96), lambda q: q.memset(T.sow[:, 512:608], 0.0))
-            decode(T.sow[:, 0:512], "sow", B("SE"), "SE", B("SG"), "SG", B("SNE"), "SNE", 512)
-            ops[-1]["r"].append("sowd")
-        for h in (0, 1):
+        for h in range(NH_):
             chunk(t, h)
         now[0] = 0
         if t < 3:
-            op(V, "AS ACN%d0 ACN%d1" % (t, t), "AS", cv(1), (lambda t: lambda q: q.tensor_scalar(B("AS", t + 1, t + 2), B("ACN", 2 * t, 2 * t + 1), B("ACN", 2 * t + 1, 2 * t + 2), B("AS", t, t + 1), A.add, A.add))(t))
-            cp("AS", "AI", B("AI", 0, 1), B("AS", t + 1, t + 2), n=1)
-            ts("AI", "AI2", B("AI2", 0, 1), B("AI", 0, 1), 31, None, A.bitwise_and, n=1)
-            ts("AI2 NTH", "NLIM%d" % (t + 1), B("NLIM", t + 1, t + 2), B("AI2", 0, 1), -8.0, B("NTH", 0, 1), A.mult, A.add, n=1)
-        proofs(t)
-    op(Y, "sow", "ysd", 0.1, lambda q: q.dma_start(T.ys[:], T.sow[:, 0:512]), lat=2.5, sem="out6", val=16)
+            col = lambda n, j: B(n, j, j + 1)
+            for h in range(0, NH_, 2):
+                j = NH_ * t + h
+                two = h + 1 < NH_
+                ts("AS ACN%d%d" % (t, h) + (" ACN%d%d" % (t, h + 1) if two else ""), "AS", col("AS", 0), col("ACN", j), col("ACN", j + 1) if two else 0.0, col("AS", 0), A.add, A.add, n=1)
+            cp("AS", "AI", col("AI", 0), col("AS", 0), n=1)
+            ts("AI", "AI2", col("AI2", 0), col("AI", 0), 31, None, A.bitwise_and, n=1)
+            ts("AI2 NTH", "NLIM", col("NLIM", 0), col("AI2", 0), -0.5, col("NTH", 0), A.mult, A.add, n=1)
+            ts("BK NLIM", "CMb%d" % ((t + 1) % 2), B("CM%d" % ((t + 1) % 2), 128, 256), B("BK"), col("NLIM", 0), None, A.mult, n=128)
+        for h in range(NH_):
+            proofs(t, h)
+            writes(t, h)
+    op(Y, "scw", "ysd", 0.1, lambda q: q.dma_start(T.ys[:], T.scw[:, 0:512]), lat=2.5, sem="out%d" % (NOUT - 1), val=16)
     return ops
 
 
@@ -365,22 +410,6 @@ def depend(ops):
     return ops
 
 
-def shifts(ops):
-    off = [-3.0 * o["h"] for o in ops]
-    kind = [(o["e"] + o["w"][0].rstrip("0123456789_"), o["h"]) for o in ops]
-    names = sorted(set(kind))
-    for i in SHIFTS:
-        rng = np.random.default_rng(i)
-        u, a, w, d = rng.random(), int(rng.integers(1 << 30)), int(rng.integers(4)), float(rng.normal())
-        if u < .5:
-            which, size = [j for j, k in enumerate(kind) if k == names[a % len(names)]], 3
-        else:
-            a %= len(ops)
-            which, size = range(a, min(len(ops), a + (1, 5, 20, 60)[w])), 4
-        for j in which: off[j] += size * d
-    return off
-
-
 def schedule(ops, off):
     n, wake = len(ops), K["wake"]
     deps = [set(o["d"]) for o in ops]
@@ -389,12 +418,13 @@ def schedule(ops, off):
     for o in ops:
         for i in o["d"]:
             succ[i].append(o["i"]); left[o["i"]] += 1
+    gap = lambda i, j: 0.0 if ops[i]["e"] == ops[j]["e"] == "t" else wake
     pri = [0.0] * n
     for o in reversed(ops):
-        pri[o["i"]] = o["c"] + o["lat"] + max([pri[j] + wake for j in succ[o["i"]]] or [0.0])
+        pri[o["i"]] = o["c"] + o["lat"] + max([pri[j] + gap(o["i"], j) for j in succ[o["i"]]] or [0.0])
     pri = [a + b for a, b in zip(pri, off)]
     free, bank, end, base, order = {}, {}, [0.0] * n, {}, []
-    banks, given = [[0.0, None] for _ in range(3)], {}
+    banks, given = [[0.0, None] for _ in range(NPOOL)], {}
     ready = [o["i"] for o in ops if not left[o["i"]]]
     def est(i):
         o = ops[i]
@@ -417,14 +447,14 @@ def schedule(ops, off):
         end[i] = x + o["c"] + o["lat"]
         for k in o["b"]: bank[k] = (o["e"], x + o["c"])
         if o["get"]:
-            j = min(range(3), key=lambda j: banks[j][0])
+            j = min(range(NPOOL), key=lambda j: banks[j][0])
             if banks[j][1] is not None: deps[i].add(banks[j][1])
             given[o["get"]] = j
             banks[j][0] = 1e9
         if o["put"]: banks[given[o["put"]]] = [x + o["c"], i]
         order.append(i)
         for j in succ[i]:
-            base[j] = max(base.get(j, 0.0), end[i] + wake)
+            base[j] = max(base.get(j, 0.0), end[i] + gap(i, j))
             left[j] -= 1
             if not left[j]: ready.append(j)
     prev = {}
@@ -435,7 +465,13 @@ def schedule(ops, off):
             for e, j in p.items():
                 if e != o["e"]: deps[i].add(j)
             p[o["e"]] = i
-    return order, max(end), given, deps
+    return order, max(end), given, deps, end
+
+
+def plan(ops):
+    if "order" not in PLAN:
+        depend(ops)
+        PLAN["order"], PLAN["time"], PLAN["bank"], PLAN["d"], PLAN["end"] = schedule(ops, [-K["lag"] * o["h"] for o in ops])
 
 
 def rank_program(g, core, T, topo):
@@ -443,9 +479,7 @@ def rank_program(g, core, T, topo):
     if rank is None:
         return
     ops = build(T)
-    if "order" not in PLAN:
-        depend(ops)
-        PLAN["order"], PLAN["time"], PLAN["bank"], PLAN["d"] = schedule(ops, shifts(ops))
+    plan(ops)
     queue = {"v": g.vector, "s": g.scalar, "t": g.tensor, "g": g, "y": g.sync}
     know = {e: {} for e in queue}
     count, clock = {}, {}
@@ -455,6 +489,8 @@ def rank_program(g, core, T, topo):
         e, q = o["e"], queue[o["e"]]
         kn = know[e]
         for j in sorted(PLAN["d"][i], key=lambda j: -clock[j][2]):
+            if e == ops[j]["e"] == "t":
+                continue
             s, v, _, c = clock[j]
             if kn.get(s, 0) < v:
                 q.wait_ge(T.sem[s], v)
@@ -462,13 +498,13 @@ def rank_program(g, core, T, topo):
                     if kn.get(k, 0) < w: kn[k] = w
                 kn[s] = max(kn.get(s, 0), v)
         if isinstance(o["f"], tuple):
-            _, t, h = o["f"]
-            dst = T.cores[(rank + HOPS[t]) % N]
+            _, hop, out, src = o["f"]
+            dst = T.cores[(rank + hop) % N]
             rid, pid, _ = topo.addr(dst)
             mask = sum(1 << x for x in topo.engines(core, dst)[:NENG])
-            g.remote_dma(T["m%d%d" % (t + 1, h)][:], T["o%d%d" % (t, h)][:], T.sem[o["sem"]], T.sem.loc, pid, rid, mask)
+            g.remote_dma(out, src, T.sem[o["sem"]], T.sem.loc, pid, rid, mask)
             sends += NENG
-            clock[i] = (o["sem"], o["val"], len(clock), dict(kn))
+            clock[i] = (o["sem"], o["val"], len(clock), {})
             continue
         x = o["f"](q)
         if o["sem"]:
@@ -485,6 +521,8 @@ def rank_program(g, core, T, topo):
     for i in range(NOUT):
         g.wait_ge(T.sem["out%d" % i], 16)
     g.wait_ge(T.sem.loc, sends)
+    for s in SEMAPHORES:
+        if s[0] == "k": g.wait_ge(T.sem[s], 16)
     for t in (1, 2, 3):
-        for h in (0, 1):
+        for h in range(NH_):
             g.wait_ge(T.sem["a%d%d" % (t, h)], NENG)

@@ -1,3 +1,4 @@
+import math
 import numpy as np
 from concourse.mybir import dt, AluOpType as A, ActivationFunctionType as F
 
@@ -14,7 +15,7 @@ EQ = 3 / 128
 H, BF, F4, I4, U2 = "float16", "bfloat16", "float32", "int32", "uint16"
 PER = {
     "OFT": (U2, C), "OFX": (U2, C), "OFN": (U2, 8), "OFV": (U2, 2 * NC), "OFW": (U2, 2 * NC), "LI": (I4, 2 * C), "VI": (I4, 2 * NC), "VI2": (I4, 2 * NC),
-    "ZSS": (H, L), "ZE": (H, L), "GD": (H, L), "GN": (H, L), "XT": (H, L), "TP": (H, L),
+    "ZE": (H, L), "GD": (H, L), "GN": (H, L), "XT": (H, L), "TP": (H, L),
     "EQ0": (BF, L), "EQ1": (BF, L), "EQ2": (BF, L),
     "FL": (H, 2 * C), "FK": (H, 2 * C), "NH": (H, C), "OH": (H, 128), "NF": (H, 128), "FAR": (BF, C), "R0": (H, 2 * C), "R1": (BF, 2 * C),
     "DT1": (H, 2 * C), "M1": (H, 2 * C), "SA": (H, 2 * C), "SB": (H, 2 * C),
@@ -26,9 +27,8 @@ SCALED = {"IDN": -1, "I3N": -3, "I4": 4, "I128N": -128, "I512": 512, "I512N": -5
 ONE = {
     "SEI": (BF, 2048), "GG": (BF, 2048), "SX": (BF, 2000), "DF": (BF, 1024), "PP": (BF, 192), "ON1": (BF, 1024),
     "ID": (BF, 128), "BK": (BF, 128), "BKN": (BF, 128), "BKC": (BF, 128), "W16": (BF, 16),
-    "RSTB": (BF, L), "RST0": (BF, C), "CZ": (BF, C), "CY": (BF, 2 * C), "C3": (BF, 3 * C), "LC": (BF, 2 * NC), "TRI": (BF, C), "TR1": (BF, C), "Z0": (BF, M),
-    "CM0": (H, 256), "CM1": (H, 256), "CB": (F4, 8),
-    "IA": (I4, C), "IB": (I4, 128), "IC": (I4, C), "ID4": (I4, C),
+    "RSTB": (BF, L), "RST0": (BF, C), "CZ": (BF, C), "CY": (BF, 2 * C), "C3": (BF, 3 * C), "LC": (BF, 2 * NC), "TRI": (BF, C), "LK": (BF, 128), "Z0": (BF, M), "ZR": (BF, 1024), "IB": (BF, 128),
+    "ZSS": (H, L), "CM0": (H, 256), "CM1": (H, 256), "CB": (F4, 8), "IA": (I4, 8), "IC": (I4, 8),
     "THR": (I4, 8), "TH1": (I4, 8), "TH2": (I4, 8), "NTH": (F4, 8), "NLIM": (F4, 8), "ACN": (F4, 16), "AS": (F4, 8), "AI": (I4, 8), "AI2": (I4, 8), "SP": (F4, 8),
     "SI": (I4, 1024),
 }
@@ -48,27 +48,31 @@ for _h in range(NH_):
         SCRATCH["m%d%d" % (_t, _h)] = ("sbuf", [128, 4 * C], H)
         if _t < 3:
             SCRATCH["o%d%d" % (_t, _h)] = ("sbuf", [128, 3 * C], H)
-NPOOL = 3
-for _b in ("cm0", "cm1", "cm2", "bm", "bx0", "bx1", "by0", "by1"):
+SENDS = [[0, 1, 2]]
+LAST = [[2], [0, 1]]
+NPOOL = 4
+for _b in ("cm0", "cm1", "cm2", "cm3", "bx0", "bx1", "by0", "by1"):
     SCRATCH[_b] = ("psum", [128, 512], F4)
-NLOAD, NOUT = 2 * NH_ + 6, 3 * NH_ + 1
-SEMAPHORES = ["v", "s", "t", "g", "loc"] + ["l%d" % i for i in range(NLOAD)] + ["a%d%d" % (t, h) for t in (1, 2, 3) for h in range(NH_)] + ["out%d" % i for i in range(NOUT)]
+NLOAD, NOUT = 2 * NH_ + 10, 3 * NH_ + 1
+SEMAPHORES = ["v", "s", "t", "g", "loc"] + ["l%d" % i for i in range(NLOAD)] + ["a%d%d%d" % (t, h, js[0]) for t in (1, 2, 3) for h in range(NH_) for js in SENDS] + ["out%d" % i for i in range(NOUT)]
 SEMAPHORES += ["k%d%d%d" % (t, h, j) for t in range(4) for h in range(NH_) for j in range(4)]
 MAGIC = 1.5 * 2.0 ** 30
 
-K = {"v": 1.0e-3, "t": 0.5e-3, "fix": 0.06, "wake": 0.08, "gat": 1.56, "sca": 3.8, "hop": 3.5, "lag": 9.0}
+K = {"v": 0.9e-3, "t": 0.45e-3, "fix": 0.06, "wake": 0.08, "gat": 1.56, "sca": 3.8, "hop": 3.5, "lag": 8.0}
 def cv(n, k=1.0): return K["fix"] + K["v"] * max(64, n * k)
 def ct(*ns): return sum(K["t"] * max(64, n) for n in ns) + 0.03
 
 MODES = "SSSS" "SSSS" "SSSS"
 ON = {"ZSS": "s", "FAR": "s", "FKD": "s", "FKT": "s"}
+PARTS = {"ZE": 1, "GD": 2, "GN": 1, "XT": 2, "TP": 1}
+ROUNDS, SEED = (800, 25000), 0
 NENG = 8
 PLAN = {}
 
 
 def build(T):
     ops = []
-    now = [0]
+    now = [0, -1]
 
     def B(name, lo=0, hi=None, step=1, p=None):
         d, a, w = WHERE[name]
@@ -82,7 +86,7 @@ def build(T):
         return T["p_" + d][slice(*p), a + n - 1:(a - 1 if a else None):-1]
 
     def op(eng, rd, wr, cost, fn, banks=(), lat=0.0, sem=None, val=1, get=None, put=None):
-        ops.append(dict(h=now[0], e=eng, r=rd.split(), w=wr.split(), c=cost, f=fn, lat=lat, sem=sem, val=val, b=list(banks), i=len(ops), get=get, put=put))
+        ops.append(dict(h=now[0], t=now[1], e=eng, r=rd.split(), w=wr.split(), c=cost, f=fn, lat=lat, sem=sem, val=val, b=list(banks), i=len(ops), get=get, put=put))
 
     def mm(calls):
         def f(q):
@@ -128,27 +132,34 @@ def build(T):
             load("THR", B("THR", 0, 1), T.th[:], kb=1)
     load("SIc", B("SI", 0, 512), T.sc[:], kb=260)
     load("SIt", B("SI", 512, 1024), T.st[:], kb=260)
-    op(V, "", "tabm", cv(16), lambda q: q.memset(T.tab[:, 0:16], -1.0))
     TAB = "taba tabb tabm"
     tab = T.tab[:, 0:4112]
 
-    def ms(name, c, lo=0, hi=None, step=1, p=None, key=None, rd=""):
+    def ms(name, c, lo=0, hi=None, step=1, p=None, key=None, eng=S):
         n = len(range(lo, WHERE[name][2] if hi is None else hi, step))
-        op(V, rd, key or name, cv(n, 0.5), lambda q: q.memset(B(name, lo, hi, step, p), c))
+        if eng == V:
+            op(V, "", key or name, cv(n, 0.5), lambda q: q.memset(B(name, lo, hi, step, p), c))
+        else:
+            act("ON1", key or name, B(name, lo, hi, step, p), B("ON1", 0, n, p=p), F.Copy, n=n, scale=float(c))
     def iota(name, n, pat, base, cmul):
-        op(G, "", name, 0.13 + 2 * K["v"] * n, lambda q: q.iota(B(name, 0, n), pat, base, cmul))
+        op(G, "", name, 0.13 + 2 * K["v"] * n, lambda q: q.iota(B(name, 0, n), pat, base, cmul, allow_small_or_imprecise_dtypes=True))
     def aff(out, src, n, pat, cmp, base, cmul, fill=0.0, at=0, p=None, key=""):
         a = at if src == out else 0
-        op(G, src + (key if src == out else ""), out + key, 0.17 + 2 * K["v"] * n, lambda q: q.affine_select(B(out, at, at + n, p=p), B(src, a, a + n, p=p), pat, cmp, fill, base, cmul))
+        op(G, (src + key if src == out else src + " ON2" * (n > 384)), out + key, 0.17 + 2 * K["v"] * n, lambda q: q.affine_select(B(out, at, at + n, p=p), B(src, a, a + n, p=p), pat, cmp, fill, base, cmul))
     LO, HI = (0, 64), (64, 128)
-    ms("ON1", 1.0)
+    ms("ON1", 1.0, 0, 384, eng=V)
+    ms("ON1", 1.0, 384, 1024, key="ON2", eng=V)
+    act("ON1", "tabm", T.tab[:, 0:16], B("ON1", 0, 16), F.Copy, n=16, scale=-1.0)
     aff("ID", "ON1", 128, [[-1, 128]], A.is_equal, 0, 1)
     aff("BKC", "ON1", 128, [[-16, 8], [0, 16]], A.is_ge, 0, 1)
     aff("BK", "BKC", 128, [[16, 8], [0, 16]], A.is_ge, 15, -1)
     aff("DF", "ON1", 1024, [[-1, 16], [-16, 4], [0, 16]], A.is_equal, -64, 1, key="u")
     iota("IB", 128, [[0, 8], [-1, 16]], 15, 0)
-    iota("IA", C, [[0, C]], 0, 1)
-    iota("ID4", C, [[0, NC], [1, 16]], 0, 0)
+    iota("IA", 1, [[0, 1]], 0, 1)
+    aff("LK", "ON1", 128, [[0, 8], [-1, 16]], A.is_equal, 0, 1)
+    iota("TRI", C, [[0, C]], 2048, 0)
+    aff("TRI", "TRI", C, [[0, NC], [1, 16]], A.is_gt, 0, -1, 6144.0)
+    aff("TRI", "TRI", C, [[0, NC], [1, 16]], A.not_equal, 0, -1)
     act("ID DFu", "DFl", B("DF", 0, 64, p=LO), B("ID", 0, 64, p=LO), F.Copy, n=64, scale=-1.0)
     for w in (64, 128, 256, 512):
         act("DFl", "DFl", B("DF", w, 2 * w, p=LO), B("DF", 0, w, p=LO), F.Copy, n=w)
@@ -157,17 +168,19 @@ def build(T):
         aff("SEI", "ON1", 512, [[-1, 4], [-16, 8], [0, 16]], A.is_equal, -4 * j, 1, at=512 * j, key=k)
         aff("SEI", "SEI", 512, [[0, 4], [-1, 128]], A.not_equal, 0, 1, -1.0, at=512 * j, key=k)
         aff("SEI", "SEI", 512, [[-1, 4], [-512, 8], [-31, 16]], A.not_equal, -4 * j, 32, at=512 * j, key=k)
-    ms("RSTB", BIG)
-    ms("RSTB", -BIG, 0, L, 16)
-    for h in range(NH_):
-        ms("ZSS%d" % h, 0.0)
-    ms("SX", 0.0)
-    ms("GG", 0.0)
+    ms("RSTB", BIG, eng=V)
+    ms("RSTB", -BIG, 0, L, 16, eng=V)
+    ms("ZSS", 0.0, eng=V)
+    ms("ZR", 0.0, eng=V)
+    for name in ("SX", "GG"):
+        for j in (0, 1):
+            hi = min(1024 * j + 1024, WHERE[name][2])
+            load(name + str(j), B(name, 1024 * j, hi), B("ZR", 0, hi - 1024 * j), rd="ZR", kb=260)
     ms("PP", 0.0)
     for g in range(8):
         a = 64 * (g % 2) + 16 * (g // 2)
-        act("BK SX", "SXg%d" % g, B("SX", 16 * (g // 2) + g % 2, 2000, 130), B("BK", a, a + 16), F.Copy, n=16, scale=-128.0)
-        act("BK GG", "GGg%d" % g, B("GG", 16 * g, 2048, 129), B("BK", 16 * g, 16 * g + 16), F.Copy, n=16, scale=-128.0)
+        act("BK SX0 SX1", "SXg%d" % g, B("SX", 16 * (g // 2) + g % 2, 2000, 130), B("BK", a, a + 16), F.Copy, n=16, scale=-128.0)
+        act("BK GG0 GG1", "GGg%d" % g, B("GG", 16 * g, 2048, 129), B("BK", 16 * g, 16 * g + 16), F.Copy, n=16, scale=-128.0)
     act("ID PP", "PPa", B("PP", 64, 128, p=LO), B("ID", 0, 64, p=LO), F.Copy, n=64, scale=-128.0)
     act("ID PP", "PPb", B("PP", 64, 128, p=HI), B("ID", 64, 128, p=HI), F.Copy, n=64, scale=-128.0)
     GGK = " ".join("GGg%d" % g for g in range(8))
@@ -199,12 +212,8 @@ def build(T):
     ms("CB", -3072.0, 3, 4, key="CB3")
     ms("CB", 32.0, 4, 5, key="CB4")
     for j in (0, 1):
-        ts("IB", "CMa%d" % j, B("CM%d" % j, 0, 128), B("IB"), 1 / 2048, None, A.mult, n=128)
-    ts("IA", "IC", B("IC"), B("IA"), 15, None, A.bitwise_and)
-    tt("ID4 IC", "TR1", B("TR1"), B("ID4"), B("IC"), A.subtract)
-    ts("TR1", "TRI", B("TRI"), B("TR1"), 0.0, 4096.0, A.is_lt, A.mult)
-    ts("TR1", "TR1", B("TR1"), B("TR1"), 0.0, 2048.0, A.not_equal, A.mult)
-    tt("TR1 TRI", "TRI", B("TRI"), B("TRI"), B("TR1"), A.add)
+        act("IB", "CMa%d" % j, B("CM%d" % j, 0, 128), B("IB"), F.Copy, n=128, scale=1 / 2048)
+    ts("IA", "IC", B("IC", 0, 1), B("IA", 0, 1), 15, None, A.bitwise_and, n=1)
     ts("IC", "SP", B("SP", 0, 1), B("IC", 0, 1), 512.0, None, A.add, n=1)
     ms("AS", 0.0)
     tt("THR IC", "TH1", B("TH1", 0, 1), B("THR", 0, 1), B("IC", 0, 1), A.add, n=1)
@@ -214,16 +223,22 @@ def build(T):
 
     for h in range(NH_):
         m = T["m0%d" % h]
-        ts("LIt%d LId%d" % (h, h), "m0%d" % h, m[:, 0:2 * C], B("LI%d" % h), 1 / 2048, -2047 / 2048, A.mult, A.add, n=2 * C)
+        ts("LIt%d LId%d" % (h, h), "m0%dd m0%dt" % (h, h), m[:, 0:2 * C], B("LI%d" % h), 1 / 2048, -2047 / 2048, A.mult, A.add, n=2 * C)
         act("Z0", "m0%dz" % h, m[:, 2 * C:3 * C], B("Z0", C * h, C * h + C), F.Copy, bias=ZO)
-    cp("SIc", "scw", T.scw[:, 0:512], B("SI", 0, 512), n=512)
-    cp("SIt", "stw", T.stw[:, 0:512], B("SI", 512, 1024), n=512)
-    op(V, "", "scwd", cv(16), lambda q: q.memset(T.scw[:, 512:528], 0.0))
+    act("SIc", "scw", T.scw[:, 0:512], B("SI", 0, 512), F.Copy, n=512)
+    act("SIt", "stw", T.stw[:, 0:512], B("SI", 512, 1024), F.Copy, n=512)
+    act("ON1", "scwd", T.scw[:, 512:528], B("ON1", 0, 16), F.Copy, n=16)
 
     nblk = [0]
     def newbank():
         nblk[0] += 1
         return "blk%d" % nblk[0]
+
+    def parts(name):
+        k = PARTS[name]
+        return [(L * i // k, L * (i + 1) // k, (C * i // k, C * (i + 1) // k), "%d_" % i) for i in range(k)]
+    def need(name, a=0, e=L):
+        return " ".join("." + name + k for a1, e1, o, k in parts(name) if a1 < e and a < e1)
 
     def chunk(t, h):
         now[0] = h
@@ -231,11 +246,11 @@ def build(T):
         X = lambda n: n + str(h)
         b = lambda n, *a, **k: B(X(n), *a, **k)
         D, TT, Z, DT = m[:, 0:C], m[:, C:2 * C], m[:, 2 * C:3 * C], m[:, 0:2 * C]
-        km = "m%d%d" % (t, h)
-        kz = km + "z" if t == 0 else km
+        kd, kt, kz = ("m%d%d%s" % (t, h, j) for j in "dtz")
+        km = kd + " " + kt
         x = lambda s: " ".join(X(w[1:]) if w[0] == "." else w for w in s.split())
         nx, ny = "bx%d" % (h % 2), "by%d" % (h % 2)
-        bm, bx, by = T.bm, T[nx], T[ny]
+        bx, by = T[nx], T[ny]
         kx = lambda *js: " ".join(nx + str(j) for j in js)
         ky = lambda *js: " ".join(ny + str(j) for j in js)
         c = lambda bank, i, j=None: bank[:, C * i:C * (i + 1 if j is None else j)]
@@ -247,37 +262,6 @@ def build(T):
         stack(1, ".SAl", b("SA", 0, C, p=LO), m[0:64, C:2 * C])
         stack(2, ".SBl", b("SB", p=LO), m[64:128, 0:2 * C])
         stack(3, ".SBu", b("SB", 0, C, p=HI), m[64:128, C:2 * C])
-        ts(km, x(".OFT"), b("OFT"), TT, 2048.0, 2063.0, A.mult, A.add, k=.5)
-        if ON["ZSS"] == V:
-            cp(x(kz + " .ZSS"), x(".ZSS"), b("ZSS", 0, L, 16), Z, k=.5)
-        else:
-            act(x(kz + " .ZSS"), x(".ZSS"), b("ZSS", 0, L, 16), Z, F.Copy)
-        scan(x(".ZSS RSTB"), x(".ZE"), b("ZE"), B("RSTB"), b("ZSS"), A.min, A.max, n=L, k=.5)
-        tt(x(TAB + " .OFT .ZE"), x(".GD"), b("GD"), tab.indirect(b("OFT")), b("ZE"), A.subtract, n=L, k=K["gat"])
-        ts(x(".GD"), x(".GN"), b("GN"), b("GD"), ZO, 0.0, A.add, A.min, n=L, k=.5)
-        ts(km, x(".FL"), b("FL"), DT, -1.0, None, A.is_gt, n=2 * C, k=.5)
-        pe(x("BK .FL"), kx(4, "o"), group(c(bx, 4), [(B("BK"), b("FL", C, 2 * C))]), nx, C)
-        act(kx(4) + " CB4", x(".NH"), b("NH"), c(bx, 4), F.Relu, banks=[nx], bias=B("CB", 4, 5), scale=-32.0)
-        cm = "CM%d" % (t % 2)
-        calls = [(B("ON1", 0, C), B(cm), bm[0:C, 0:256]), (b("FL", C, 2 * C), B("I8K"), bm[0:C, 128:256])]
-        calls += [(b("GD", p, L, 16), B("W16", 0, 8), bm[0:C, 128 + p:256:16]) for p in range(16)]
-        calls += [(b("GN", p, L, 16), B("W16"), bm[0:C, p:256:16]) for p in range(16)]
-        pe(x("ON1 CMa%d CMb%d I8K W16a W16b .FL .GD .GN" % (t % 2, t % 2)), "psK psD", group(None, calls), "bm", 256, 128, *[64] * 32)
-        scan("psK RSTB", x(".MX"), b("MX", p=P), B("RSTB", 0, 128, p=P), bm[0:C, 0:128], A.min, A.max, n=128, banks=["bm"])
-        act("psD CB0", x(".NF"), b("NF", p=P), bm[0:C, 128:256], F.Sigmoid, n=128, banks=["bm"], bias=B("CB", 0, 1, p=P), scale=-4096.0)
-        scan(x(".MX RSTB"), x(".SM"), back(X("SM"), 128, P), B("RSTB", 0, 128, p=P), back(X("MX"), 128, P), A.min, A.max, n=128)
-        tt(x("psK .SM"), x(".OH"), b("OH", p=P), bm[0:C, 0:128], b("SM", p=P), A.is_equal, n=128, k=1, banks=["bm"])
-        pe(x(".OH I2K"), "psO", group(bm[:, 256:256 + C], [(b("OH", p=P), B("I2K", 0, C, p=P))]), "bm", C)
-        tt("psO " + km, x(".TH"), m[:, 3 * C:4 * C], bm[:, 256:256 + C], TT, A.mult, k=1, banks=["bm"])
-        pl = bm[:, 352:352 + 2 * NC]
-        pe(x(GGK + " ID LC .TH " + kz), "psN", group(pl, [(B("ID"), B("LC"))] + [(sel(r, "GG"), m[:, 2 * C + r:4 * C:16]) for r in range(16)]), "bm", *[64] * 17)
-        ts("psN", x(".VI"), b("VI"), pl, -1 / 128, None, A.mult, n=2 * NC, banks=["bm"])
-        ts("psN", x(".OFN"), b("OFN", 0, NC), bm[:, 352 + NC:352 + 2 * NC], -1 / 128, 2064.0, A.mult, A.add, n=NC, banks=["bm"])
-        ts(x(".VI"), x(".VI2"), b("VI2"), b("VI"), 511, None, A.bitwise_and, n=2 * NC)
-        cp(x(".VI2"), x(".OFV"), b("OFV"), b("VI2"), n=2 * NC)
-        for j, (win, kw, a) in enumerate(((T.scw, "scw", NC), (T.stw, "stw", NC), (T.scw, "scw", 0), (T.stw, "stw", 0))):
-            act(x(kw + " .OFV"), x(".CV%d_" % j), b("CV", C * j, C * j + C), win[:, 0:512].indirect(b("OFV", a, a + NC)), F.Copy, k=K["gat"], scale=1 / 2048, bias=-2047 / 2048)
-        act(x(TAB + " .OFN"), x(".YK"), b("YK"), tab.indirect(b("OFN", 0, NC)), F.Relu, k=K["gat"])
         def compare(j, col, to, kt, bank_to, last, also=None):
             for k in range(NB):
                 bank, w, up = newbank(), LB * C, k >= NB // 2
@@ -298,8 +282,43 @@ def build(T):
                     calls.append(((two if up else one)(s), e, to))
                     if also is not None: calls.append(((one if up else two)(s), e, also))
                 pe(SXK + " " + ke, kt, group(None, calls, False, last and k == NB - 1), bank_to, *[C] * len(calls))
+        ts(kt, x(".OFT"), b("OFT"), TT, 2048.0, 2063.0, A.mult, A.add, k=.5)
+        if ON["ZSS"] == V:
+            cp(kz, "ZSS", B("ZSS", 0, L, 16), Z, k=.5)
+        else:
+            act(kz, "ZSS", B("ZSS", 0, L, 16), Z, F.Copy)
+        for a, e, o, k in parts("ZE"):
+            scan("ZSS RSTB", x(".ZE" + k), b("ZE", a, e), B("RSTB", 0, e - a), B("ZSS", a, e), A.min, A.max, n=e - a, k=.5)
+        for a, e, o, k in parts("GD"):
+            tt(x(TAB + " .OFT " + need("ZE", a, e)), x(".GD" + k), b("GD", a, e), tab.indirect(b("OFT", *o)), b("ZE", a, e), A.subtract, n=e - a, k=K["gat"])
+        for a, e, o, k in parts("GN"):
+            ts(x(need("GD", a, e)), x(".GN" + k), b("GN", a, e), b("GD", a, e), ZO, 0.0, A.add, A.min, n=e - a, k=.5)
+        ts(km, x(".FL"), b("FL"), DT, -1.0, None, A.is_gt, n=2 * C, k=.5)
+        pe(x("BK .FL " + kx("o")), kx(4), group(c(bx, 4), [(B("BK"), b("FL", C, 2 * C))]), nx, C)
+        act(kx(4) + " CB4", x(".NH"), b("NH"), c(bx, 4), F.Relu, banks=[nx], bias=B("CB", 4, 5), scale=-32.0)
         pe("ID " + km, kx(0, 1, "o"), group(c(bx, 0, 2), [(B("ID"), DT)], True, False), nx, 2 * C)
         compare(0, 0, c(bx, 1), kx(0, 1, "o"), nx, True, c(bx, 0))
+        cm = "CM%d" % (t % 2)
+        calls = [(B("ON1", 0, C), B(cm), by[0:C, 0:256]), (b("FL", C, 2 * C), B("I8K"), by[0:C, 128:256])]
+        calls += [(b("GD", p, L, 16), B("W16", 0, 8), by[0:C, 128 + p:256:16]) for p in range(16)]
+        pe(x("ON1 CMa%d CMb%d I8K W16a .FL " % (t % 2, t % 2) + need("GD")), ky(0, 1, 2, "o"), group(None, calls, True, False), ny, 256, 128, *[64] * 16)
+        calls = [(b("GN", p, L, 16), B("W16"), by[0:C, p:256:16]) for p in range(16)]
+        pe(x("W16a W16b " + need("GN")), ky(0, 1, 2, "o"), group(None, calls, False, True), ny, *[64] * 16)
+        scan(ky(0, 1) + " RSTB", x(".MX"), b("MX", p=P), B("RSTB", 0, 128, p=P), by[0:C, 0:128], A.min, A.max, n=128, banks=[ny])
+        act(ky(1, 2) + " CB0", x(".NF"), b("NF", p=P), by[0:C, 128:256], F.Sigmoid, n=128, banks=[ny], bias=B("CB", 0, 1, p=P), scale=-4096.0)
+        scan(x(".MX RSTB"), x(".SM"), back(X("SM"), 128, P), B("RSTB", 0, 128, p=P), back(X("MX"), 128, P), A.min, A.max, n=128)
+        tt(x(ky(0, 1) + " .SM"), x(".OH"), b("OH", p=P), by[0:C, 0:128], b("SM", p=P), A.is_equal, n=128, k=1, banks=[ny])
+        pe(x(".OH I2K " + kx("o")), kx(2), group(c(bx, 2), [(b("OH", p=P), B("I2K", 0, C, p=P))]), nx, C)
+        tt(kx(2) + " " + kt, x(".TH"), m[:, 3 * C:4 * C], c(bx, 2), TT, A.mult, k=1, banks=[nx])
+        pl = bx[:, 5 * C:5 * C + 2 * NC]
+        pe(x(GGK + " ID LC .TH " + kz + " " + kx("o")), kx(5), group(pl, [(B("ID"), B("LC"))] + [(sel(r, "GG"), m[:, 2 * C + r:4 * C:16]) for r in range(16)]), nx, *[64] * 17)
+        ts(kx(5), x(".VI"), b("VI"), pl, -1 / 128, None, A.mult, n=2 * NC, banks=[nx])
+        ts(kx(5), x(".OFN"), b("OFN", 0, NC), bx[:, 5 * C + NC:5 * C + 2 * NC], -1 / 128, 2064.0, A.mult, A.add, n=NC, banks=[nx])
+        ts(x(".VI"), x(".VI2"), b("VI2"), b("VI"), 511, None, A.bitwise_and, n=2 * NC)
+        cp(x(".VI2"), x(".OFV"), b("OFV"), b("VI2"), n=2 * NC)
+        for j, (win, kw, a) in enumerate(((T.scw, "scw", NC), (T.stw, "stw", NC), (T.scw, "scw", 0), (T.stw, "stw", 0))):
+            act(x(kw + " .OFV"), x(".CV%d_" % j), b("CV", C * j, C * j + C), win[:, 0:512].indirect(b("OFV", a, a + NC)), F.Copy, k=K["gat"], scale=1 / 2048, bias=-2047 / 2048)
+        act(x(TAB + " .OFN"), x(".YK"), b("YK"), tab.indirect(b("OFN", 0, NC)), F.Relu, k=K["gat"])
         ts(kx(0, 1), x(".R0"), b("R0"), c(bx, 0, 2), MAGIC, -MAGIC, A.add, A.add, n=2 * C, banks=[nx])
         tt(x(kx(0, 1) + " .R0"), x(".DT1"), b("DT1"), c(bx, 0, 2), b("R0"), A.subtract, n=2 * C, k=1, banks=[nx])
         D1, T1 = b("DT1", 0, C), b("DT1", C, 2 * C)
@@ -310,52 +329,69 @@ def build(T):
             else:
                 act(key + " CB2", x(".FK%d_" % j), b("FK", C * j, C * j + C), src, F.Sigmoid, banks=banks, bias=B("CB", 2, 3), scale=2.0 ** 23)
         filled(0, x(".DT1"), D1, .5, [])
-        act(x(TAB + " .OFX"), x(".XT"), b("XT"), tab.indirect(b("OFX")), F.Copy, n=L, k=K["gat"])
-        scan(x(".XT RSTB"), x(".TP"), b("TP"), B("RSTB"), b("XT"), A.min, A.max, n=L, k=.5)
+        for a, e, o, k in parts("XT"):
+            act(x(TAB + " .OFX"), x(".XT" + k), b("XT", a, e), tab.indirect(b("OFX", *o)), F.Copy, n=e - a, k=K["gat"])
+        for a, e, o, k in parts("TP"):
+            scan(x("RSTB " + need("XT", a, e)), x(".TP" + k), b("TP", a, e), B("RSTB", 0, e - a), b("XT", a, e), A.min, A.max, n=e - a, k=.5)
         oh = (b("OH", p=P), B("I3N", 0, C, p=P))
-        pe(x(".NF .DT1 I128N IDN"), kx(3, "o"), group(c(bx, 3), [(B("IDN"), T1), (b("NF", p=P), B("I128N", 0, C, p=P))]), nx, C, C)
+        pe(x(".NF .DT1 I128N IDN " + kx("o")), kx(3), group(c(bx, 3), [(B("IDN"), T1), (b("NF", p=P), B("I128N", 0, C, p=P))]), nx, C, C)
         act(kx(3) + " CB3", x(".FAR"), b("FAR"), c(bx, 3), F.Relu, banks=[nx], scale=2048.0, bias=B("CB", 3, 4))
-        pe(x(".OH .DT1 I3N ID"), kx(4, "o"), group(c(bx, 4), [(B("ID"), T1), oh]), nx, C, C)
+        pe(x(".OH .DT1 I3N ID " + kx("o")), kx(4), group(c(bx, 4), [(B("ID"), T1), oh]), nx, C, C)
         filled(1, kx(4), c(bx, 4), 1, [nx])
         act(kx(4) + " CB0", x(".TN"), b("TN"), c(bx, 4), F.Relu, banks=[nx], bias=B("CB", 0, 1), scale=2048.0)
         far, left, nh = b("FAR"), b("FK", 0, C), b("NH")
         ng = b("NG", 0, C)
-        pe(x("ID IDN BK BKN .FAR .FK0_ .NH"), ky(2, 3, 4, "o"), group(c(by, 2), [(B("BKN"), left), (B("ID"), nh), (B("BK"), far)]) +
+        if t < 3:
+            pe(x("BK BKN .FL .FK0_ .FAR " + kx("o")), kx(3), group(c(bx, 3), [(B("BK"), b("FL", 0, C)), (B("BKN"), left), (B("BKN"), far)]), nx, C, C, C)
+            act(kx(3), x(".JK ACN%d%d" % (t, h)), b("JK"), c(bx, 3), F.Relu, banks=[nx], accum_out=B("ACN", NH_ * t + h, NH_ * t + h + 1))
+        pe(x("ID IDN BK BKN .FAR .FK0_ .NH " + ky("o")), ky(2, 3, 4), group(c(by, 2), [(B("BKN"), left), (B("ID"), nh), (B("BK"), far)]) +
            group(c(by, 3), [(B("BKN"), left), (B("IDN"), nh), (B("BKN"), far)]) + group(c(by, 4), [(B("BK"), far)]), ny, *[C] * 7)
         act(ky(2, 3) + " CB0", x(".NG"), b("NG"), c(by, 2, 4), F.Sigmoid, n=2 * C, banks=[ny], bias=B("CB", 0, 1), scale=4096.0)
         tt(x(ky(4) + " .YK"), x(".YM"), b("YM"), c(by, 4), b("YK"), A.min, k=1, banks=[ny])
-        pe(x("ID IDN I512 .YM .NG " + kz), kx(3, "o"), group(c(bx, 3), [(B("ID"), Z), (B("I512"), ng), (B("IDN"), b("YM"))]), nx, C, C, C)
-        act(kx(3), x(".A2z"), b("A2", 2 * C, 3 * C), c(bx, 3), F.Copy, banks=[nx], bias=-512.0)
-        pe(x("ID IDN I3N I512N ON1 CZ .DT1 .OH .YM .NG " + kz), kx(0, 1, 2, "o"), group(None, [(B("ID"), b("DT1"), c(bx, 0, 2)), oh + (c(bx, 1),), (B("I512N"), ng, c(bx, 0)), (B("I512N"), ng, c(bx, 1))]) +
+        pe(x("ID IDN I512 .YM .NG %s %s" % (kz, kx("o"))), kx(3), group(c(bx, 3), [(B("ID"), Z), (B("I512"), ng), (B("IDN"), b("YM"))]), nx, C, C, C)
+        act(kx(3), x(".A22_"), b("A2", 2 * C, 3 * C), c(bx, 3), F.Copy, banks=[nx], bias=-512.0)
+        pe(x("ID IDN I3N I512N ON1 CZ .DT1 .OH .YM .NG %s %s" % (kz, kx("o"))), kx(0, 1, 2), group(None, [(B("ID"), b("DT1"), c(bx, 0, 2)), oh + (c(bx, 1),), (B("I512N"), ng, c(bx, 0)), (B("I512N"), ng, c(bx, 1))]) +
            group(c(bx, 2), [(ones, B("CZ")), (B("IDN"), Z), (B("ID"), b("YM"))]), nx, 2 * C, *[C] * 6)
         cp(x(".CV0_ .CV1_"), x(".SAl .SA2"), b("SA", p=LO), b("CV", 0, 2 * C, p=LO), n=2 * C, k=.5)
         cp(x(".CV0_ .CV1_"), x(".SBu .SB2"), b("SB", p=HI), b("CV", 0, 2 * C, p=HI), n=2 * C, k=.5)
-        pe(x("ON1 CY I3N .FK0_ .FK1_"), ky(0, 1, "o"), group(c(by, 0, 2), [(ones, B("CY")), (B("I3N"), b("FK"))], True, False), ny, 2 * C, 2 * C)
-        compare(1, 0, c(by, 0), ky(0, 1, "o"), ny, False)
-        compare(2, 1, c(by, 1), ky(0, 1, "o"), ny, True)
-        act(ky(0, 1), x(".R1"), b("R1"), c(by, 0, 2), F.Copy, n=2 * C, banks=[ny], bias=24.0)
-        tt(x(ky(0, 1) + " .R1"), x(".M1"), b("M1"), c(by, 0, 2), b("R1"), A.subtract, n=2 * C, k=1, banks=[ny])
-        pe(x("ID I512N BK .M1 .NG .FAR"), ky(0, 1, "o"), group(None, [(B("ID"), b("M1"), c(by, 0, 2))] + [(w, y, c(by, j)) for j in (0, 1) for w, y in ((B("I512N"), ng), (B("BK"), far))]), ny, 2 * C, *[C] * 4)
-        tt(x(ky(0, 1) + " .CV0_ .CV1_"), x(".A2"), b("A2", 0, 2 * C), c(by, 0, 2), b("CV", 0, 2 * C), A.min, n=2 * C, k=1, banks=[ny])
-        tt(x(kx(0, 1, 2) + " .A2 .A2z"), x(".A3"), b("A3"), c(bx, 0, 3), b("A2"), A.max, n=3 * C, k=1, banks=[nx])
-        bank = newbank()
-        op(TE, x("ON1 C3 ID I4 BKN IH I512N .CV2_ .CV3_ .NG .FAR .YK .TP"), bank, ct(3 * C, 2 * C, *[C] * 7), mm(lambda: group(None, [
-            (ones, B("C3"), c(pool(bank), 0, 3)), (B("ID"), b("CV", 2 * C, 4 * C), c(pool(bank), 0, 2))] +
-            [(w, y, c(pool(bank), j)) for j in (0, 1) for w, y in ((B("I4"), ng), (B("BKN"), far))] +
-            [(w, y, c(pool(bank), 2)) for w, y in ((B("I512N"), ng), (B("IH"), b("YK")), (B("IH"), b("TP", 15, L, 16)))])), get=bank)
-        ko, out = ("o%d%d" % (t, h), T["o%d%d" % (t, h)][:]) if t < 3 else (x(".FIN"), b("FIN"))
-        op(V, x(bank + " .A3"), ko, cv(3 * C), lambda q: q.tensor_tensor(out, c(pool(bank), 0, 3), b("A3"), A.max), put=bank)
-        if t < 3:
-            op(G, ko, "m%d%d" % (t + 1, h), 1.0, ("send", HOPS[t], T["m%d%d" % (t + 1, h)][:, 0:3 * C], out), lat=K["hop"], sem="a%d%d" % (t + 1, h), val=NENG)
-            pe(x("BK BKN .FL .FK0_ .FAR"), "psS", group(bm[:, 384:384 + C], [(B("BK"), b("FL", 0, C)), (B("BKN"), left), (B("BKN"), far)]), "bm", C, C, C)
-            act("psS", x(".JK ACN%d%d" % (t, h)), b("JK"), bm[:, 384:384 + C], F.Relu, banks=["bm"], accum_out=B("ACN", NH_ * t + h, NH_ * t + h + 1))
-        else:
-            ts(ko, x(".R0"), b("R0"), b("FIN", 0, 2 * C), -1.0, None, A.max, n=2 * C, k=.5)
-            act(x(".R0"), x(".OUTa"), b("OUT", 0, 2 * C), b("R0"), F.Copy, n=2 * C, scale=2048.0, bias=2047.0)
-            ts(ko, x(".OUTz"), b("OUT", 2 * C, 3 * C), b("FIN", 2 * C, 3 * C), -ZO, None, A.add)
-            s = slice(C * h, C * h + C)
-            for j, (y, k) in enumerate(((T.yd, ".OUTa"), (T.yt, ".OUTa"), (T.yz, ".OUTz"))):
-                op(Y, x(k), "y%d%d" % (j, h), 0.1, (lambda y, j: lambda q: q.dma_start(y[:, s], b("OUT", C * j, C * j + C)))(y, j), lat=2.2, sem="out%d" % (3 * h + j), val=16)
+        part = lambda n, i, j=None: b(n, C * i, C * (i + 1 if j is None else j))
+        keys = lambda n, js: " ".join(x(".%s%d_" % (n, j)) for j in js)
+        def refill(js):
+            i, e, n = js[0], js[-1] + 1, C * len(js)
+            pe(x("ON1 CY I3N " + keys("FK", js)), ky(*js, "o"), group(c(by, i, e), [(ones, B("CY", 0, n)), (B("I3N"), part("FK", i, e))], True, False), ny, n, n)
+            for j in reversed(js):
+                compare(1 + j, j, c(by, j), ky(*js, "o"), ny, j == i)
+            act(ky(*js), keys("R1", js), part("R1", i, e), c(by, i, e), F.Copy, n=n, banks=[ny], bias=24.0)
+            tt(ky(*js) + " " + keys("R1", js), keys("M1", js), part("M1", i, e), c(by, i, e), part("R1", i, e), A.subtract, n=n, k=1, banks=[ny])
+            nb, to, a, kb = (ny, by, 0, ky) if i == 0 else (nx, bx, 4, kx)
+            pe(x("ID I512N BK .NG .FAR %s %s" % (keys("M1", js), kb("o"))), kb(*range(a, a + len(js))), group(None, [(B("ID"), part("M1", i, e), c(to, a, a + len(js)))] + [
+                (w, y, c(to, a + j - i)) for j in js for w, y in ((B("I512N"), ng), (B("BK"), far))]), nb, n, *[C] * (2 * len(js)))
+            tt(kb(*range(a, a + len(js))) + " " + keys("CV", js), keys("A2", js), part("A2", i, e), c(to, a, a + len(js)), part("CV", i, e), A.min, n=n, k=1, banks=[nb])
+        def finish(js):
+            i, e, n = js[0], js[-1] + 1, C * len(js)
+            tt(kx(*js) + " " + keys("A2", js), keys("A3", js), part("A3", i, e), c(bx, i, e), part("A2", i, e), A.max, n=n, k=1, banks=[nx])
+            bank = newbank()
+            terms = lambda j: ((B("ID"), part("CV", 2 + j)), (B("I4"), ng), (B("BKN"), far)) if j < 2 else ((B("I512N"), ng), (B("IH"), b("YK")), (B("IH"), b("TP", 15, L, 16)))
+            op(TE, x("ON1 C3 ID I4 BKN IH I512N .NG .FAR " + keys("CV", [2 + j for j in js if j < 2]) + (" .YK " + need("TP") if 2 in js else "")), bank, ct(n, *[C] * (3 * len(js))), mm(lambda: group(None, [
+                (ones, B("C3", C * i, C * e), c(pool(bank), i, e))] + [(w, y, c(pool(bank), j)) for j in js for w, y in terms(j)])), get=bank)
+            ko = "o%d%d%d" % (t, h, i)
+            out = T["o%d%d" % (t, h)][:, C * i:C * e] if t < 3 else part("FIN", i, e)
+            op(V, x(bank + " " + keys("A3", js)), ko, cv(n), lambda q: q.tensor_tensor(out, c(pool(bank), i, e), part("A3", i, e), A.max), put=bank)
+            if t < 3:
+                op(G, ko, " ".join("m%d%d%s" % (t + 1, h, "dtz"[j]) for j in js), 1.0, ("send", HOPS[t], T["m%d%d" % (t + 1, h)][:, C * i:C * e], out), lat=K["hop"], sem="a%d%d%d" % (t + 1, h, i), val=NENG)
+                return
+            ls = [j for j in js if j < 2]
+            if ls:
+                i, e, n = ls[0], ls[-1] + 1, C * len(ls)
+                ts(ko, keys("R0", ls) + x(" .R0"), part("R0", i, e), part("FIN", i, e), -1.0, None, A.max, n=n, k=.5)
+                act(keys("R0", ls), keys("OUT", ls), part("OUT", i, e), part("R0", i, e), F.Copy, n=n, scale=2048.0, bias=2047.0)
+            if 2 in js:
+                ts(ko, keys("OUT", [2]), part("OUT", 2), part("FIN", 2), -ZO, None, A.add)
+            for j in js:
+                op(Y, keys("OUT", [j]), "y%d%d" % (j, h), 0.1, (lambda j: lambda q: q.dma_start((T.yd, T.yt, T.yz)[j][:, C * h:C * h + C], part("OUT", j)))(j), lat=2.2, sem="out%d" % (3 * h + j), val=16)
+        for js in (SENDS if t < 3 else LAST):
+            if js[0] < 2: refill([j for j in js if j < 2])
+            finish(js)
 
     def proofs(t, h):
         now[0] = h
@@ -364,7 +400,7 @@ def build(T):
         x = lambda s: " ".join(X(w[1:]) if w[0] == "." else w for w in s.split())
         bank = newbank()
         cp(x(".VI2"), x(".VL"), b("VL"), b("VI2", NC, 2 * NC), n=NC)
-        op(TE, x("ID TRI SEIq0 SEIq1 SEIq2 SEIq3 I2KN .VL .NG"), bank, ct(C, C, *[64] * 16), mm(lambda: group(None, [(B("ID"), B("TRI"), pool(bank)[:, 0:C])] + [
+        op(TE, x("LK TRI SEIq0 SEIq1 SEIq2 SEIq3 I2KN .VL .NG"), bank, ct(C, C, *[64] * 16), mm(lambda: group(None, [(B("LK"), B("TRI"), pool(bank)[:, 0:C])] + [
             (sel(r, "SEI"), b("VL"), pool(bank)[:, r:C:16]) for r in range(16)] + [(B("I2KN"), b("NG", C, 2 * C), pool(bank)[:, 0:C])])), get=bank)
         op(V, bank + " SP", x(".EP"), cv(C), lambda q: q.tensor_scalar(b("EP"), pool(bank)[:, 0:C], 0.0, B("SP", 0, 1), A.is_equal, A.mult), put=bank)
         scan(x(".EP RST0"), x(".LS"), b("LS"), B("RST0"), b("EP"), A.mult, A.max, k=.5)
@@ -377,9 +413,10 @@ def build(T):
             ts("OFW%d TN%d scwd" % (h, h), "scw", T.scw[:, 0:528].indirect(B("OFW%d" % h, 2 * j, 2 * j + 1)), B("TN%d" % h, 16 * j, 16 * j + 16), 1.0, -1.0, A.mult, A.add, n=16, k=K["sca"])
 
     for t in range(4):
+        now[1] = t
         for h in range(NH_):
             chunk(t, h)
-        now[0] = 0
+        now[0] = NH_ - 1
         if t < 3:
             col = lambda n, j: B(n, j, j + 1)
             for h in range(0, NH_, 2):
@@ -412,7 +449,6 @@ def depend(ops):
 
 def schedule(ops, off):
     n, wake = len(ops), K["wake"]
-    deps = [set(o["d"]) for o in ops]
     succ = [[] for _ in ops]
     left = [0] * n
     for o in ops:
@@ -448,7 +484,6 @@ def schedule(ops, off):
         for k in o["b"]: bank[k] = (o["e"], x + o["c"])
         if o["get"]:
             j = min(range(NPOOL), key=lambda j: banks[j][0])
-            if banks[j][1] is not None: deps[i].add(banks[j][1])
             given[o["get"]] = j
             banks[j][0] = 1e9
         if o["put"]: banks[given[o["put"]]] = [x + o["c"], i]
@@ -457,21 +492,118 @@ def schedule(ops, off):
             base[j] = max(base.get(j, 0.0), end[i] + gap(i, j))
             left[j] -= 1
             if not left[j]: ready.append(j)
-    prev = {}
+    return order, max(end)
+
+
+def timer(ops):
+    n, wake = len(ops), K["wake"]
+    E, cost, lat = [o["e"] for o in ops], [o["c"] for o in ops], [o["lat"] for o in ops]
+    D = [[(j, 0.0 if E[j] == o["e"] == "t" else wake) for j in o["d"]] for o in ops]
+    BK, get, put = [o["b"] for o in ops], [o["get"] for o in ops], [o["put"] for o in ops]
+    def times(order):
+        end, why, res = [0.0] * n, [-1] * n, [False] * n
+        free, bank, given, before = {}, {}, {}, {}
+        banks = [[0.0, -1, j] for j in range(NPOOL)]
+        for i in order:
+            x, w, r = 0.0, -1, False
+            for j, g in D[i]:
+                if end[j] + g > x: x, w = end[j] + g, j
+            e = E[i]
+            f = free.get(e)
+            if f and f[0] > x: x, w, r = f[0], f[1], True
+            for k in BK[i]:
+                for e2, (tm, j) in bank.get(k, {}).items():
+                    if e2 != e and tm + wake > x: x, w, r = tm + wake, j, True
+            if get[i]:
+                q = min(banks)
+                if q[0] > 1e8: return None
+                if q[1] >= 0:
+                    before[i] = q[1]
+                    if q[0] + wake > x: x, w, r = q[0] + wake, q[1], True
+                given[get[i]] = q
+                q[0] = 1e9
+            y = x + cost[i]
+            free[e] = (y, i)
+            for k in BK[i]: bank.setdefault(k, {})[e] = (y, i)
+            if put[i]: given[put[i]][0:2] = [y, i]
+            end[i], why[i], res[i] = y + lat[i], w, r
+        return end, why, res, {k: q[2] for k, q in given.items()}, before
+    return times
+
+
+def shift(ops, rng, rounds):
+    kind = [(o["e"] + o["w"][0].rstrip("0123456789_") + str(round(o["c"], 2)), o["h"]) for o in ops]
+    same = [[j for j, x in enumerate(kind) if x == k] for k in sorted(set(kind))]
+    off = np.array([-K["lag"] * o["h"] for o in ops])
+    order, cur = schedule(ops, list(off))
+    for it in range(rounds):
+        new = off.copy()
+        if rng.random() < .5:
+            new[same[rng.integers(len(same))]] += 3 * rng.normal()
+        else:
+            a = rng.integers(len(ops))
+            new[a:a + (1, 5, 20, 60)[rng.integers(4)]] += 3 * rng.normal()
+        p, x = schedule(ops, list(new))
+        if x <= cur: off, cur, order = new, x, p
+    return order
+
+
+def swap(ops, order, rng, rounds, hot=0.15, cold=0.01):
+    n, times = len(ops), timer(ops)
+    pre, suc = [o["d"] for o in ops], [set() for _ in ops]
+    for o in ops:
+        for j in o["d"]: suc[j].add(o["i"])
+    cur = times(order)
+    c = best = max(cur[0])
+    keep = order
+    for it, (u, v, w, z) in enumerate(rng.random((rounds, 4)).tolist()):
+        end, why, res = cur[:3]
+        i, arcs = end.index(c), []
+        while why[i] >= 0:
+            if res[i]: arcs.append((why[i], i))
+            i = why[i]
+        j, i = arcs[int(u * len(arcs))]
+        a, b, more = order.index(j), order.index(i), (0, 0, 0, 3, 10)[int(5 * w)]
+        if v < .5:
+            a = max(0, a - more)
+            seg, S = order[a:b + 1], {i}
+            for x in reversed(seg[:-1]):
+                if suc[x] & S: S.add(x)
+            if j in S: continue
+            new = [x for x in seg if x in S] + [x for x in seg if x not in S]
+        else:
+            seg, S = order[a:b + 1 + more], {j}
+            for x in seg[1:]:
+                if pre[x] & S: S.add(x)
+            if i in S: continue
+            new = [x for x in seg if x not in S] + [x for x in seg if x in S]
+        p = order[:a] + new + order[a + len(seg):]
+        d = times(p)
+        if d is None: continue
+        y = max(d[0])
+        if y <= c or z < math.exp((c - y) / (hot * (cold / hot) ** (it / rounds))):
+            order, cur, c = p, d, y
+            if y < best: best, keep = y, p
+    return keep
+
+
+def plan(ops):
+    if "order" in PLAN:
+        return
+    depend(ops)
+    rng = np.random.default_rng(SEED)
+    order = swap(ops, shift(ops, rng, ROUNDS[0]), rng, ROUNDS[1])
+    end, _, _, given, before = timer(ops)(order)
+    deps, prev = [set(o["d"]) for o in ops], {}
     for i in order:
         o = ops[i]
+        if i in before: deps[i].add(before[i])
         for k in o["b"]:
             p = prev.setdefault(k, {})
             for e, j in p.items():
                 if e != o["e"]: deps[i].add(j)
             p[o["e"]] = i
-    return order, max(end), given, deps, end
-
-
-def plan(ops):
-    if "order" not in PLAN:
-        depend(ops)
-        PLAN["order"], PLAN["time"], PLAN["bank"], PLAN["d"], PLAN["end"] = schedule(ops, [-K["lag"] * o["h"] for o in ops])
+    PLAN.update(order=order, time=max(end), bank=given, d=deps, end=end)
 
 
 def rank_program(g, core, T, topo):
@@ -523,6 +655,5 @@ def rank_program(g, core, T, topo):
     g.wait_ge(T.sem.loc, sends)
     for s in SEMAPHORES:
         if s[0] == "k": g.wait_ge(T.sem[s], 16)
-    for t in (1, 2, 3):
-        for h in range(NH_):
-            g.wait_ge(T.sem["a%d%d" % (t, h)], NENG)
+    for s in SEMAPHORES:
+        if s[0] == "a": g.wait_ge(T.sem[s], NENG)

@@ -14,23 +14,22 @@ EQ = 3 / 128
 
 H, BF, F4, I4, U2 = "float16", "bfloat16", "float32", "int32", "uint16"
 PER = {
-    "OFT": (U2, C), "OFX": (U2, C), "OFN": (U2, 8), "OFV": (U2, 2 * NC), "OFW": (U2, 2 * NC), "LI": (I4, 2 * C), "VI": (I4, 2 * NC), "VI2": (I4, 2 * NC),
-    "ZE": (H, L), "GD": (H, L), "GN": (H, L), "XT": (H, L), "TP": (H, L),
+    "OFT": (U2, C), "OFX": (U2, C), "OFN": (U2, 8), "OFV": (U2, 2 * NC), "LI": (I4, 2 * C), "VI": (I4, 2 * NC), "VI2": (I4, 2 * NC),
+    "ZE": (H, L // 2), "GD": (H, L), "GN": (H, L), "XT": (H, L), "TP": (H, L),
     "EQ0": (BF, L), "EQ1": (BF, L), "EQ2": (BF, L),
     "FL": (H, 2 * C), "FK": (H, 2 * C), "NH": (H, C), "OH": (H, 128), "NF": (H, 128), "FAR": (BF, C), "R0": (H, 2 * C), "R1": (BF, 2 * C),
-    "DT1": (H, 2 * C), "M1": (H, 2 * C), "SA": (H, 2 * C), "SB": (H, 2 * C),
+    "DT1": (H, 2 * C), "SA": (H, 2 * C), "SB": (H, 2 * C),
     "CV": (H, 4 * C), "YK": (H, C), "YM": (H, C), "NG": (H, 2 * C), "A2": (H, 3 * C), "A3": (H, 3 * C), "FIN": (H, 3 * C),
-    "VL": (H, NC), "EP": (H, C), "LS": (H, C), "WO": (H, NC),
     "MX": (F4, 128), "SM": (F4, 128), "JK": (F4, C), "TN": (F4, C), "OUT": (F4, 3 * C),
 }
-SCALED = {"IDN": -1, "I3N": -3, "I4": 4, "I128N": -128, "I512": 512, "I512N": -512, "I2K": 2048, "I2KN": -2048, "I8K": 8192, "IH": 0.5}
+SCALED = {"IDN": -1, "I3N": -3, "I4": 4, "I56N": -56, "I512": 512, "I512N": -512, "I2K": 2048, "I8K": 8192, "IH": 0.5}
 ONE = {
-    "SEI": (BF, 2048), "GG": (BF, 2048), "SX": (BF, 2000), "DF": (BF, 1024), "PP": (BF, 192), "ON1": (BF, 1024),
+    "SEI": (BF, 2048), "GG": (BF, 2048), "SX": (BF, 1024), "DF": (BF, 1024), "ON1": (BF, 1024),
     "ID": (BF, 128), "BK": (BF, 128), "BKN": (BF, 128), "BKC": (BF, 128), "W16": (BF, 16),
-    "RSTB": (BF, L), "RST0": (BF, C), "CZ": (BF, C), "CY": (BF, 2 * C), "C3": (BF, 3 * C), "LC": (BF, 2 * NC), "TRI": (BF, C), "LK": (BF, 128), "Z0": (BF, M), "ZR": (BF, 1024), "IB": (BF, 128),
-    "ZSS": (H, L), "CM0": (H, 256), "CM1": (H, 256), "CB": (F4, 8), "IA": (I4, 8), "IC": (I4, 8),
+    "RSTB": (BF, L), "RST8": (BF, L // 2), "PQ": (BF, 512), "RST0": (BF, M), "CZ": (BF, 2 * C), "CY": (BF, 2 * C), "LC": (BF, 2 * NC), "TRI": (BF, M), "LK": (BF, 128), "SH": (BF, 256), "ILO": (BF, 128), "IHI": (BF, 128), "Z0": (BF, M), "ZR": (BF, 1024), "IB": (BF, 128),
+    "ZSS": (H, L // 2), "CM0": (H, 256), "CM1": (H, 256), "CB": (F4, 8), "IA": (I4, 8), "IC": (I4, 8),
     "THR": (I4, 8), "TH1": (I4, 8), "TH2": (I4, 8), "NTH": (F4, 8), "NLIM": (F4, 8), "ACN": (F4, 16), "AS": (F4, 8), "AI": (I4, 8), "AI2": (I4, 8), "SP": (F4, 8),
-    "SI": (I4, 1024),
+    "SI": (I4, 512), "VL": (H, M // 16), "EP": (H, M), "LS": (H, M), "WO": (H, M // 16), "OFW": (U2, M // 8),
 }
 ONE.update({_n: (BF, 128) for _n in SCALED})
 WHERE = {}
@@ -42,7 +41,7 @@ for _n, (_d, _w) in [(n + str(h), x) for n, x in PER.items() for h in range(NH_)
 SCRATCH = {"p_" + _d: ("sbuf", [128, _w], _d) for _d, _w in _tot.items()}
 SCRATCH["tab"] = ("sbuf", [128, 4112], BF)
 SCRATCH["scw"] = ("sbuf", [128, 528], F4)
-SCRATCH["stw"] = ("sbuf", [128, 512], F4)
+SCRATCH["stw"] = ("sbuf", [128, 512], I4)
 for _h in range(NH_):
     for _t in range(4):
         SCRATCH["m%d%d" % (_t, _h)] = ("sbuf", [128, 4 * C], H)
@@ -53,19 +52,20 @@ LAST = [[2], [0, 1]]
 NPOOL = 4
 for _b in ("cm0", "cm1", "cm2", "cm3", "bx0", "bx1", "by0", "by1"):
     SCRATCH[_b] = ("psum", [128, 512], F4)
-NLOAD, NOUT = 2 * NH_ + 10, 3 * NH_ + 1
+NLOAD, NOUT = 2 * NH_ + 14, 3 * NH_ + 1
 SEMAPHORES = ["v", "s", "t", "g", "loc"] + ["l%d" % i for i in range(NLOAD)] + ["a%d%d%d" % (t, h, js[0]) for t in (1, 2, 3) for h in range(NH_) for js in SENDS] + ["out%d" % i for i in range(NOUT)]
-SEMAPHORES += ["k%d%d%d" % (t, h, j) for t in range(4) for h in range(NH_) for j in range(4)]
 MAGIC = 1.5 * 2.0 ** 30
 
-K = {"v": 0.9e-3, "t": 0.45e-3, "fix": 0.06, "wake": 0.08, "gat": 1.56, "sca": 3.8, "hop": 3.5, "lag": 8.0}
+K = {"v": 0.87e-3, "t": 0.435e-3, "fix": 0.05, "wake": 0.13, "gat": 1.56, "sca": 3.8, "hop": 4.0, "lag": 8.0}
 def cv(n, k=1.0): return K["fix"] + K["v"] * max(64, n * k)
 def ct(*ns): return sum(K["t"] * max(64, n) for n in ns) + 0.03
 
-MODES = "SSSS" "SSSS" "SSSS"
-ON = {"ZSS": "s", "FAR": "s", "FKD": "s", "FKT": "s"}
-PARTS = {"ZE": 1, "GD": 2, "GN": 1, "XT": 2, "TP": 1}
-ROUNDS, SEED = (800, 25000), 0
+ALL, FIRST, END = "SSSS" "SSSV" "SSSS", "SSSS" "SSSV" "SSSS", "SSSS" "SVSV" "SVSV"
+MODES = [[FIRST, FIRST], [ALL, ALL], [ALL, ALL], [ALL, END]]
+ON = {"ZSS": "s", "FKD": "s", "FKT": "s"}
+SEMAPHORES += ["k%d%d%d" % (t, h, j) for t in range(4) for h in range(NH_) for j in range(4)]
+PARTS = {"XT": 2, "TP": 1}
+ROUNDS, SEED = (200, 150000), 0
 NENG = 8
 PLAN = {}
 
@@ -131,7 +131,7 @@ def build(T):
             load("tabb", T.tab[:, 2064:4112], T.clk[:, 2048:4096], eng=S, kb=520)
             load("THR", B("THR", 0, 1), T.th[:], kb=1)
     load("SIc", B("SI", 0, 512), T.sc[:], kb=260)
-    load("SIt", B("SI", 512, 1024), T.st[:], kb=260)
+    load("stw", T.stw[:], T.st[:], kb=260)
     TAB = "taba tabb tabm"
     tab = T.tab[:, 0:4112]
 
@@ -150,41 +150,52 @@ def build(T):
     ms("ON1", 1.0, 0, 384, eng=V)
     ms("ON1", 1.0, 384, 1024, key="ON2", eng=V)
     act("ON1", "tabm", T.tab[:, 0:16], B("ON1", 0, 16), F.Copy, n=16, scale=-1.0)
+    for q in (0, 1):
+        for a in (0, 1):
+            aff("PQ", "ON1", 128, [[-16, 8], [992, 2], [-1, 8]], A.is_equal, -8 * (q - a) - 1000 * a, 1, at=128 * (2 * q + a), key=str(2 * q + a))
     aff("ID", "ON1", 128, [[-1, 128]], A.is_equal, 0, 1)
     aff("BKC", "ON1", 128, [[-16, 8], [0, 16]], A.is_ge, 0, 1)
     aff("BK", "BKC", 128, [[16, 8], [0, 16]], A.is_ge, 15, -1)
     aff("DF", "ON1", 1024, [[-1, 16], [-16, 4], [0, 16]], A.is_equal, -64, 1, key="u")
+    aff("SH", "ON1", 256, [[-1, 256]], A.is_equal, 64, 1)
+    aff("ILO", "ID", 128, [[0, 128]], A.is_ge, 63, -1)
+    aff("IHI", "ID", 128, [[0, 128]], A.is_ge, -64, 1)
     iota("IB", 128, [[0, 8], [-1, 16]], 15, 0)
     iota("IA", 1, [[0, 1]], 0, 1)
     aff("LK", "ON1", 128, [[0, 8], [-1, 16]], A.is_equal, 0, 1)
-    iota("TRI", C, [[0, C]], 2048, 0)
-    aff("TRI", "TRI", C, [[0, NC], [1, 16]], A.is_gt, 0, -1, 6144.0)
-    aff("TRI", "TRI", C, [[0, NC], [1, 16]], A.not_equal, 0, -1)
+    iota("TRI", M, [[0, M]], 1024, 0)
+    aff("TRI", "TRI", M, [[0, M // 16], [1, 16]], A.is_gt, 0, -1, 2048.0)
+    aff("TRI", "TRI", M, [[0, M // 16], [1, 16]], A.not_equal, 0, -1, 512.0)
     act("ID DFu", "DFl", B("DF", 0, 64, p=LO), B("ID", 0, 64, p=LO), F.Copy, n=64, scale=-1.0)
-    for w in (64, 128, 256, 512):
+    for w in (64, 128):
         act("DFl", "DFl", B("DF", w, 2 * w, p=LO), B("DF", 0, w, p=LO), F.Copy, n=w)
+    for j in (1, 2, 3):
+        load("DF%d" % j, B("DF", 256 * j, 256 * j + 256, p=LO), B("DF", 0, 256, p=LO), rd="DFl", kb=30)
     for j in range(4):
         k = "q%d" % j
         aff("SEI", "ON1", 512, [[-1, 4], [-16, 8], [0, 16]], A.is_equal, -4 * j, 1, at=512 * j, key=k)
         aff("SEI", "SEI", 512, [[0, 4], [-1, 128]], A.not_equal, 0, 1, -1.0, at=512 * j, key=k)
         aff("SEI", "SEI", 512, [[-1, 4], [-512, 8], [-31, 16]], A.not_equal, -4 * j, 32, at=512 * j, key=k)
+    ms("RST8", BIG, eng=V)
+    ms("RST8", -BIG, 0, L // 2, 8, eng=V)
     ms("RSTB", BIG, eng=V)
     ms("RSTB", -BIG, 0, L, 16, eng=V)
     ms("ZSS", 0.0, eng=V)
     ms("ZR", 0.0, eng=V)
-    for name in ("SX", "GG"):
-        for j in (0, 1):
-            hi = min(1024 * j + 1024, WHERE[name][2])
-            load(name + str(j), B(name, 1024 * j, hi), B("ZR", 0, hi - 1024 * j), rd="ZR", kb=260)
-    ms("PP", 0.0)
+    for j in (0, 1):
+        load("GG%d" % j, B("GG", 1024 * j, 1024 * j + 1024), B("ZR"), rd="ZR", kb=260)
+    ms("SX", 0.0, 64, 128)
+    act("ID", "SX", B("SX", 0, 64, p=LO), B("ID", 0, 64, p=LO), F.Copy, n=64, scale=-128.0)
+    act("ID", "SX", B("SX", 0, 64, p=HI), B("ID", 64, 128, p=HI), F.Copy, n=64, scale=-128.0)
+    act("SX", "SX", B("SX", 128, 256), B("SX", 0, 128), F.Copy, n=128)
+    for j in (1, 2, 3):
+        load("SX%d" % j, B("SX", 256 * j, 256 * j + 256), B("SX", 0, 256), rd="SX", kb=60)
     for g in range(8):
         a = 64 * (g % 2) + 16 * (g // 2)
-        act("BK SX0 SX1", "SXg%d" % g, B("SX", 16 * (g // 2) + g % 2, 2000, 130), B("BK", a, a + 16), F.Copy, n=16, scale=-128.0)
+        act("BK SX1 SX2 SX3", "SXg%d" % g, B("SX", 64 + 16 * (g // 2) + g % 2, 1024, 130), B("BK", a, a + 8), F.Copy, n=8, scale=-128.0)
         act("BK GG0 GG1", "GGg%d" % g, B("GG", 16 * g, 2048, 129), B("BK", 16 * g, 16 * g + 16), F.Copy, n=16, scale=-128.0)
-    act("ID PP", "PPa", B("PP", 64, 128, p=LO), B("ID", 0, 64, p=LO), F.Copy, n=64, scale=-128.0)
-    act("ID PP", "PPb", B("PP", 64, 128, p=HI), B("ID", 64, 128, p=HI), F.Copy, n=64, scale=-128.0)
     GGK = " ".join("GGg%d" % g for g in range(8))
-    SXK = " ".join("SXg%d" % g for g in range(8)) + " PPa PPb"
+    SXK = " ".join("SXg%d" % g for g in range(8))
     for out, k in SCALED.items():
         act("ID", out, B(out), B("ID"), F.Copy, n=128, scale=float(k))
     act("BK", "BKN", B("BKN"), B("BK"), F.Copy, n=128, scale=-1.0)
@@ -199,18 +210,17 @@ def build(T):
                 ms(name, hi / 64, a, a + w, p=LO)
                 ms(name, lo / 64, a, a + w, p=HI)
             a += w
-    sums("CZ", [(C, 2 * ZO, None)])
-    sums("CY", [(2 * C, 24576, 1)])
-    sums("C3", [(2 * C, -4, None), (C, ZO, -0.25)])
+    sums("CZ", [(C, 2 * ZO, None), (C, -512, None)])
+    sums("CY", [(2 * C, 24576, 57)])
     ms("LC", 0.0)
     ms("LC", 128.0, NC, 2 * NC)
     ms("RST0", 1.0)
-    ms("RST0", 0.0, 0, C, 16)
+    ms("RST0", 0.0, 0, M, 16)
     ms("CB", 2048.0, 0, 1, key="CB0")
     ms("CB", float(np.log(EQ / (1 - EQ))), 1, 2, key="CB1")
     ms("CB", 4096 * 2047.5, 2, 3, key="CB2")
     ms("CB", -3072.0, 3, 4, key="CB3")
-    ms("CB", 32.0, 4, 5, key="CB4")
+    ms("CB", 512.0, 4, 5, key="CB4")
     for j in (0, 1):
         act("IB", "CMa%d" % j, B("CM%d" % j, 0, 128), B("IB"), F.Copy, n=128, scale=1 / 2048)
     ts("IA", "IC", B("IC", 0, 1), B("IA", 0, 1), 15, None, A.bitwise_and, n=1)
@@ -226,7 +236,6 @@ def build(T):
         ts("LIt%d LId%d" % (h, h), "m0%dd m0%dt" % (h, h), m[:, 0:2 * C], B("LI%d" % h), 1 / 2048, -2047 / 2048, A.mult, A.add, n=2 * C)
         act("Z0", "m0%dz" % h, m[:, 2 * C:3 * C], B("Z0", C * h, C * h + C), F.Copy, bias=ZO)
     act("SIc", "scw", T.scw[:, 0:512], B("SI", 0, 512), F.Copy, n=512)
-    act("SIt", "stw", T.stw[:, 0:512], B("SI", 512, 1024), F.Copy, n=512)
     act("ON1", "scwd", T.scw[:, 512:528], B("ON1", 0, 16), F.Copy, n=16)
 
     nblk = [0]
@@ -258,56 +267,59 @@ def build(T):
         ones = B("ON1", 0, 128)
         def stack(j, wr, out, src):
             op(Y, km, x(wr), 0.1, lambda q: q.dma_start(out, src), lat=2.1, sem="k%d%d%d" % (t, h, j), val=16)
-        stack(0, ".SAu", b("SA", p=HI), m[0:64, 0:2 * C])
-        stack(1, ".SAl", b("SA", 0, C, p=LO), m[0:64, C:2 * C])
-        stack(2, ".SBl", b("SB", p=LO), m[64:128, 0:2 * C])
-        stack(3, ".SBu", b("SB", 0, C, p=HI), m[64:128, C:2 * C])
-        def compare(j, col, to, kt, bank_to, last, also=None):
+        stack(0, ".SAd .SAt", b("SA", p=HI), m[0:64, 0:2 * C])
+        stack(1, ".SAc", b("SA", 0, C, p=LO), m[0:64, C:2 * C])
+        stack(2, ".SBd .SBt", b("SB", p=LO), m[64:128, 0:2 * C])
+        stack(3, ".SBc", b("SB", 0, C, p=HI), m[64:128, C:2 * C])
+        def compare(j, col, kt=None, last=True):
             for k in range(NB):
                 bank, w, up = newbank(), LB * C, k >= NB // 2
                 ss = range(LB * k % 8, LB * k % 8 + LB)
-                src, ks = b("SB" if up else "SA", C * col, C * col + C), (".SBl .SBu" if up else ".SAu .SAl") + (" .SB2" if up else " .SA2") * col
-                op(TE, x("DFu DFl " + ks), bank, ct(*[C] * LB), mm((lambda bank, ss, src: lambda: [
+                src, ks = b("SB" if up else "SA", C * col, C * col + C), (".SBd .SBc", ".SBt .SB2")[col] if up else (".SAd .SAc", ".SAt .SA2")[col]
+                op(TE, x("DFu DFl DF1 DF2 DF3 " + ks), bank, ct(*[C] * LB), mm((lambda bank, ss, src: lambda: [
                     (pool(bank)[:, C * i:C * i + C], sel(s, "DF"), src, True, True) for i, s in enumerate(ss)])(bank, ss, src)), get=bank)
                 eq, ke = b("EQ%d" % j, w * k, w * k + w), x(".EQ%d_%d_" % (j, k))
-                if MODES[(4 * j + k * 4 // NB)] == "V":
+                if MODES[t][h][NB * j + k] == "V":
                     op(V, bank, ke, cv(w), (lambda bank, eq: lambda q: q.tensor_scalar(eq, pool(bank)[:, 0:w], 0.0, EQ, A.is_equal, A.mult))(bank, eq), put=bank)
                 else:
                     op(S, bank + " CB1", ke, cv(w), (lambda bank, eq: lambda q: q.activation(eq, pool(bank)[:, 0:w], F.Sigmoid, bias=B("CB", 1, 2), scale=524288.0))(bank, eq), put=bank)
-                one = lambda s: B("PP", 0, 128) if up else B("PP", 64, 192)
-                two = lambda s: B("SX", 976 * up + 128 * s, 976 * up + 128 * s + 128)
-                calls = []
-                for i, s in enumerate(ss):
-                    e = b("EQ%d" % j, w * k + C * i, w * k + C * i + C)
-                    calls.append(((two if up else one)(s), e, to))
-                    if also is not None: calls.append(((one if up else two)(s), e, also))
-                pe(SXK + " " + ke, kt, group(None, calls, False, last and k == NB - 1), bank_to, *[C] * len(calls))
-        ts(kt, x(".OFT"), b("OFT"), TT, 2048.0, 2063.0, A.mult, A.add, k=.5)
+                e = lambda i: b("EQ%d" % j, w * k + C * i, w * k + C * i + C)
+                if j == 0:
+                    first = k % (NB // 2) == 0
+                    calls = [(B("ID"), src)] * first + [(sel(s, "SX"), e(i)) for i, s in enumerate(ss)]
+                    pe(x("ID %s %s %s" % (SXK, ke, ks * first)), kx(int(up), "o"), group(c(bx, int(up)), calls, first, k % (NB // 2) == NB // 2 - 1), nx, *[C] * len(calls))
+                else:
+                    calls = [(B("SX", 128 * s + 64 * up, 128 * s + 64 * up + 64), e(i)) for i, s in enumerate(ss)]
+                    pe(SXK + " " + ke, kt, group(by[64 * up:64 * up + 64, C * col:C * col + C], calls, False, last and k % (NB // 2) == NB // 2 - 1), ny, *[C] * len(calls))
+        W = L // 2
+        pe("PQ0 PQ1 PQ2 PQ3 %s %s" % (kt, kx("o")), kx(2), [y for q in (0, 1) for y in group(bx[:, 2 * C + C // 2 * q:2 * C + C // 2 * (q + 1)], [
+            (sel(2 * q + a, "PQ"), m[:, C + a:2 * C:2]) for a in (0, 1)])], nx, *[64] * 4)
+        ts(kx(2), x(".OFT"), b("OFT"), c(bx, 2), 2048.0, 2063.0, A.mult, A.add, banks=[nx])
         if ON["ZSS"] == V:
-            cp(kz, "ZSS", B("ZSS", 0, L, 16), Z, k=.5)
+            cp(kz, "ZSS", B("ZSS", 0, W, 8), Z, k=.5)
         else:
-            act(kz, "ZSS", B("ZSS", 0, L, 16), Z, F.Copy)
-        for a, e, o, k in parts("ZE"):
-            scan("ZSS RSTB", x(".ZE" + k), b("ZE", a, e), B("RSTB", 0, e - a), B("ZSS", a, e), A.min, A.max, n=e - a, k=.5)
-        for a, e, o, k in parts("GD"):
-            tt(x(TAB + " .OFT " + need("ZE", a, e)), x(".GD" + k), b("GD", a, e), tab.indirect(b("OFT", *o)), b("ZE", a, e), A.subtract, n=e - a, k=K["gat"])
-        for a, e, o, k in parts("GN"):
-            ts(x(need("GD", a, e)), x(".GN" + k), b("GN", a, e), b("GD", a, e), ZO, 0.0, A.add, A.min, n=e - a, k=.5)
+            act(kz, "ZSS", B("ZSS", 0, W, 8), Z, F.Copy)
+        scan("ZSS RST8", x(".ZE"), b("ZE"), B("RST8"), B("ZSS"), A.min, A.max, n=W, k=.5)
+        for q in (0, 1):
+            a, e = W * q, W * q + W
+            tt(x(TAB + " .OFT .ZE"), x(".GD%d_" % q), b("GD", a, e), tab.indirect(b("OFT", C // 2 * q, C // 2 * (q + 1))), b("ZE"), A.subtract, n=W, k=K["gat"])
+            ts(x(".GD%d_" % q), x(".GN%d_" % q), b("GN", a, e), b("GD", a, e), ZO, 0.0, A.add, A.min, n=W, k=.5)
         ts(km, x(".FL"), b("FL"), DT, -1.0, None, A.is_gt, n=2 * C, k=.5)
         pe(x("BK .FL " + kx("o")), kx(4), group(c(bx, 4), [(B("BK"), b("FL", C, 2 * C))]), nx, C)
-        act(kx(4) + " CB4", x(".NH"), b("NH"), c(bx, 4), F.Relu, banks=[nx], bias=B("CB", 4, 5), scale=-32.0)
-        pe("ID " + km, kx(0, 1, "o"), group(c(bx, 0, 2), [(B("ID"), DT)], True, False), nx, 2 * C)
-        compare(0, 0, c(bx, 1), kx(0, 1, "o"), nx, True, c(bx, 0))
+        act(kx(4) + " CB4", x(".NH"), b("NH"), c(bx, 4), F.Relu, banks=[nx], bias=B("CB", 4, 5), scale=-512.0)
+        compare(0, 0)
         cm = "CM%d" % (t % 2)
         calls = [(B("ON1", 0, C), B(cm), by[0:C, 0:256]), (b("FL", C, 2 * C), B("I8K"), by[0:C, 128:256])]
-        calls += [(b("GD", p, L, 16), B("W16", 0, 8), by[0:C, 128 + p:256:16]) for p in range(16)]
-        pe(x("ON1 CMa%d CMb%d I8K W16a .FL " % (t % 2, t % 2) + need("GD")), ky(0, 1, 2, "o"), group(None, calls, True, False), ny, 256, 128, *[64] * 16)
-        calls = [(b("GN", p, L, 16), B("W16"), by[0:C, p:256:16]) for p in range(16)]
-        pe(x("W16a W16b " + need("GN")), ky(0, 1, 2, "o"), group(None, calls, False, True), ny, *[64] * 16)
+        pe(x("ON1 CMa%d CMb%d I8K .FL" % (t % 2, t % 2)), ky(0, 1, 2, "o"), group(None, calls, True, False), ny, 256, 128)
+        for q in (0, 1):
+            calls = [(b("GD", W * q + p, W * q + W, 8), B("W16", 0, 8), by[0:C, 128 + 8 * q + p:256:16]) for p in range(8)]
+            pe(x("W16a .GD%d_" % q), ky(0, 1, 2, "o"), group(None, calls, False, False), ny, *[64] * 8)
+            calls = [(b("GN", W * q + p, W * q + W, 8), B("W16"), by[0:C, 8 * q + p:256:16]) for p in range(8)]
+            pe(x("W16a W16b .GN%d_" % q), ky(0, 1, 2, "o"), group(None, calls, False, q == 1), ny, *[64] * 8)
         scan(ky(0, 1) + " RSTB", x(".MX"), b("MX", p=P), B("RSTB", 0, 128, p=P), by[0:C, 0:128], A.min, A.max, n=128, banks=[ny])
         act(ky(1, 2) + " CB0", x(".NF"), b("NF", p=P), by[0:C, 128:256], F.Sigmoid, n=128, banks=[ny], bias=B("CB", 0, 1, p=P), scale=-4096.0)
-        scan(x(".MX RSTB"), x(".SM"), back(X("SM"), 128, P), B("RSTB", 0, 128, p=P), back(X("MX"), 128, P), A.min, A.max, n=128)
-        tt(x(ky(0, 1) + " .SM"), x(".OH"), b("OH", p=P), by[0:C, 0:128], b("SM", p=P), A.is_equal, n=128, k=1, banks=[ny])
+        scan(ky(0, 1) + " RSTB", ky(3, 4), by[0:C, 415:287:-1], B("RSTB", 0, 128, p=P), by[0:C, 127::-1], A.min, A.max, n=128, banks=[ny])
+        tt(x(ky(3, 4) + " .MX"), x(".OH"), b("OH", p=P), by[0:C, 288:416], b("MX", p=P), A.is_equal, n=128, k=1, banks=[ny])
         pe(x(".OH I2K " + kx("o")), kx(2), group(c(bx, 2), [(b("OH", p=P), B("I2K", 0, C, p=P))]), nx, C)
         tt(kx(2) + " " + kt, x(".TH"), m[:, 3 * C:4 * C], c(bx, 2), TT, A.mult, k=1, banks=[nx])
         pl = bx[:, 5 * C:5 * C + 2 * NC]
@@ -321,22 +333,25 @@ def build(T):
         act(x(TAB + " .OFN"), x(".YK"), b("YK"), tab.indirect(b("OFN", 0, NC)), F.Relu, k=K["gat"])
         ts(kx(0, 1), x(".R0"), b("R0"), c(bx, 0, 2), MAGIC, -MAGIC, A.add, A.add, n=2 * C, banks=[nx])
         tt(x(kx(0, 1) + " .R0"), x(".DT1"), b("DT1"), c(bx, 0, 2), b("R0"), A.subtract, n=2 * C, k=1, banks=[nx])
-        D1, T1 = b("DT1", 0, C), b("DT1", C, 2 * C)
-        ts(x(".DT1"), x(".OFX"), b("OFX"), D1, 2048.0, 2063.0, A.mult, A.add, k=.5)
+        def home(j, i):
+            lo, hi = (B("SH", 128, 256), B("SH", 0, 128)) if j == 0 else (B("ILO"), B("IHI"))
+            return [(lo, b("DT1", 0, C), c(bx, i)), (hi, b("DT1", C, 2 * C), c(bx, i))]
+        pe(x("SH .DT1 " + kx("o")), kx(4), group(None, home(0, 4)), nx, C, C)
+        ts(kx(4), x(".OFX"), b("OFX"), c(bx, 4), 2048.0, 2063.0, A.mult, A.add, banks=[nx])
         def filled(j, key, src, k, banks):
             if ON["FK" + "DT"[j]] == V:
                 ts(key, x(".FK%d_" % j), b("FK", C * j, C * j + C), src, -1.0, None, A.is_gt, k=k, banks=banks)
             else:
                 act(key + " CB2", x(".FK%d_" % j), b("FK", C * j, C * j + C), src, F.Sigmoid, banks=banks, bias=B("CB", 2, 3), scale=2.0 ** 23)
-        filled(0, x(".DT1"), D1, .5, [])
+        filled(0, kx(4), c(bx, 4), 1, [nx])
         for a, e, o, k in parts("XT"):
             act(x(TAB + " .OFX"), x(".XT" + k), b("XT", a, e), tab.indirect(b("OFX", *o)), F.Copy, n=e - a, k=K["gat"])
         for a, e, o, k in parts("TP"):
             scan(x("RSTB " + need("XT", a, e)), x(".TP" + k), b("TP", a, e), B("RSTB", 0, e - a), b("XT", a, e), A.min, A.max, n=e - a, k=.5)
         oh = (b("OH", p=P), B("I3N", 0, C, p=P))
-        pe(x(".NF .DT1 I128N IDN " + kx("o")), kx(3), group(c(bx, 3), [(B("IDN"), T1), (b("NF", p=P), B("I128N", 0, C, p=P))]), nx, C, C)
-        act(kx(3) + " CB3", x(".FAR"), b("FAR"), c(bx, 3), F.Relu, banks=[nx], scale=2048.0, bias=B("CB", 3, 4))
-        pe(x(".OH .DT1 I3N ID " + kx("o")), kx(4), group(c(bx, 4), [(B("ID"), T1), oh]), nx, C, C)
+        pe(x(".NF .DT1 I512 ILO IHI " + kx("o")), kx(3), group(c(bx, 3), [(b("NF", p=P), B("I512", 0, C, p=P))] + home(1, 3)), nx, C, C, C)
+        act(kx(3) + " CB3", x(".FAR"), b("FAR"), c(bx, 3), F.Relu, banks=[nx], scale=-2048.0, bias=B("CB", 3, 4))
+        pe(x(".OH .DT1 I3N ILO IHI " + kx("o")), kx(4), group(c(bx, 4), [oh] + home(1, 4)), nx, C, C, C)
         filled(1, kx(4), c(bx, 4), 1, [nx])
         act(kx(4) + " CB0", x(".TN"), b("TN"), c(bx, 4), F.Relu, banks=[nx], bias=B("CB", 0, 1), scale=2048.0)
         far, left, nh = b("FAR"), b("FK", 0, C), b("NH")
@@ -344,47 +359,49 @@ def build(T):
         if t < 3:
             pe(x("BK BKN .FL .FK0_ .FAR " + kx("o")), kx(3), group(c(bx, 3), [(B("BK"), b("FL", 0, C)), (B("BKN"), left), (B("BKN"), far)]), nx, C, C, C)
             act(kx(3), x(".JK ACN%d%d" % (t, h)), b("JK"), c(bx, 3), F.Relu, banks=[nx], accum_out=B("ACN", NH_ * t + h, NH_ * t + h + 1))
-        pe(x("ID IDN BK BKN .FAR .FK0_ .NH " + ky("o")), ky(2, 3, 4), group(c(by, 2), [(B("BKN"), left), (B("ID"), nh), (B("BK"), far)]) +
-           group(c(by, 3), [(B("BKN"), left), (B("IDN"), nh), (B("BKN"), far)]) + group(c(by, 4), [(B("BK"), far)]), ny, *[C] * 7)
-        act(ky(2, 3) + " CB0", x(".NG"), b("NG"), c(by, 2, 4), F.Sigmoid, n=2 * C, banks=[ny], bias=B("CB", 0, 1), scale=4096.0)
-        tt(x(ky(4) + " .YK"), x(".YM"), b("YM"), c(by, 4), b("YK"), A.min, k=1, banks=[ny])
-        pe(x("ID IDN I512 .YM .NG %s %s" % (kz, kx("o"))), kx(3), group(c(bx, 3), [(B("ID"), Z), (B("I512"), ng), (B("IDN"), b("YM"))]), nx, C, C, C)
-        act(kx(3), x(".A22_"), b("A2", 2 * C, 3 * C), c(bx, 3), F.Copy, banks=[nx], bias=-512.0)
-        pe(x("ID IDN I3N I512N ON1 CZ .DT1 .OH .YM .NG %s %s" % (kz, kx("o"))), kx(0, 1, 2), group(None, [(B("ID"), b("DT1"), c(bx, 0, 2)), oh + (c(bx, 1),), (B("I512N"), ng, c(bx, 0)), (B("I512N"), ng, c(bx, 1))]) +
-           group(c(bx, 2), [(ones, B("CZ")), (B("IDN"), Z), (B("ID"), b("YM"))]), nx, 2 * C, *[C] * 6)
-        cp(x(".CV0_ .CV1_"), x(".SAl .SA2"), b("SA", p=LO), b("CV", 0, 2 * C, p=LO), n=2 * C, k=.5)
-        cp(x(".CV0_ .CV1_"), x(".SBu .SB2"), b("SB", p=HI), b("CV", 0, 2 * C, p=HI), n=2 * C, k=.5)
+        na = b("NG", C, 2 * C)
+        pe(x("ID BK BKN .FAR .FK0_ .NH " + ky("o")), ky(3, 4), group(c(by, 3), [(B("BKN"), left), (B("ID"), nh), (B("BK"), far)]) + group(c(by, 4), [(B("BKN"), far)]), ny, *[C] * 4)
+        act(ky(3, 4) + " CB0", x(".NG"), b("NG"), c(by, 3, 5), F.Sigmoid, n=2 * C, banks=[ny], bias=B("CB", 0, 1), scale=4096.0)
+        pe(x("BK .FAR " + kx("o")), kx(2), group(c(bx, 2), [(B("BK"), far)]), nx, C)
+        tt(x(kx(2) + " .YK"), x(".YM"), b("YM"), c(bx, 2), b("YK"), A.min, k=1, banks=[nx])
+        pe(x("ON1 CZ ID IDN I512 .YM .NG %s %s" % (kz, ky("o"))), ky(2), group(c(by, 2), [(ones, B("CZ", C, 2 * C)), (B("ID"), Z), (B("I512"), ng), (B("IDN"), b("YM"))]), ny, C, C, C, C)
+        pe(x("SH ILO IHI I3N I512N .DT1 .OH .NG " + kx("o")), kx(0, 1), group(c(bx, 0), [(B("I512N"), ng)] + home(0, 0)) +
+           group(c(bx, 1), [(B("I512N"), ng), oh] + home(1, 1)), nx, *[C] * 7)
+        pe(x("ON1 CZ ID IDN .YM %s %s" % (kz, kx("o"))), kx(2), group(c(bx, 2), [(ones, B("CZ", 0, C)), (B("IDN"), Z), (B("ID"), b("YM"))]), nx, C, C, C)
+        cp(x(".CV0_ .CV1_"), x(".SAc .SA2"), b("SA", p=LO), b("CV", 0, 2 * C, p=LO), n=2 * C, k=.5)
+        cp(x(".CV0_ .CV1_"), x(".SBc .SB2"), b("SB", p=HI), b("CV", 0, 2 * C, p=HI), n=2 * C, k=.5)
         part = lambda n, i, j=None: b(n, C * i, C * (i + 1 if j is None else j))
         keys = lambda n, js: " ".join(x(".%s%d_" % (n, j)) for j in js)
         def refill(js):
             i, e, n = js[0], js[-1] + 1, C * len(js)
-            pe(x("ON1 CY I3N " + keys("FK", js)), ky(*js, "o"), group(c(by, i, e), [(ones, B("CY", 0, n)), (B("I3N"), part("FK", i, e))], True, False), ny, n, n)
+            pe(x("ON1 CY I3N I56N .NG " + keys("FK", js)), ky(*js, "o"), group(None, [(ones, B("CY", 0, n), c(by, i, e)), (B("I3N"), part("FK", i, e), c(by, i, e))] + [
+                (w, y, c(by, j)) for j in js for w, y in ((B("I3N"), ng), (B("I56N"), na))], True, False), ny, n, n, *[C] * (2 * len(js)))
             for j in reversed(js):
-                compare(1 + j, j, c(by, j), ky(*js, "o"), ny, j == i)
-            act(ky(*js), keys("R1", js), part("R1", i, e), c(by, i, e), F.Copy, n=n, banks=[ny], bias=24.0)
-            tt(ky(*js) + " " + keys("R1", js), keys("M1", js), part("M1", i, e), c(by, i, e), part("R1", i, e), A.subtract, n=n, k=1, banks=[ny])
-            nb, to, a, kb = (ny, by, 0, ky) if i == 0 else (nx, bx, 4, kx)
-            pe(x("ID I512N BK .NG .FAR %s %s" % (keys("M1", js), kb("o"))), kb(*range(a, a + len(js))), group(None, [(B("ID"), part("M1", i, e), c(to, a, a + len(js)))] + [
-                (w, y, c(to, a + j - i)) for j in js for w, y in ((B("I512N"), ng), (B("BK"), far))]), nb, n, *[C] * (2 * len(js)))
-            tt(kb(*range(a, a + len(js))) + " " + keys("CV", js), keys("A2", js), part("A2", i, e), c(to, a, a + len(js)), part("CV", i, e), A.min, n=n, k=1, banks=[nb])
+                compare(1 + j, j, ky(*js, "o"), j == i)
+            act(ky(*js), keys("R1", js), part("R1", i, e), c(by, i, e), F.Copy, n=n, banks=[ny])
+            tt(ky(*js) + " " + keys("R1", js), ky(*js), c(by, i, e), c(by, i, e), part("R1", i, e), A.subtract, n=n, k=1, banks=[ny])
+            tt(ky(*js) + " " + keys("CV", js), ky(*js), c(by, i, e), c(by, i, e), part("CV", i, e), A.min, n=n, k=1, banks=[ny])
+        def other(js, terms, rd, bias):
+            i, e, n, bank = js[0], js[-1] + 1, C * len(js), newbank()
+            op(TE, x(rd), bank, ct(*[C] * (3 * len(js))), mm(lambda: [y for j in js for y in group(c(pool(bank), j), terms(j))]), get=bank)
+            op(S, bank, keys("A2", js), K["fix"] + K["v"] * n, lambda q: q.activation(part("A2", i, e), c(pool(bank), i, e), F.Copy, bias=bias), put=bank)
+        other([0, 1], lambda j: [(B("ID"), part("CV", 2 + j)), (B("I4"), ng), (B("I4"), na)], "ID I4 .NG .CV2_ .CV3_", -8.0)
+        if t == 3:
+            ts(keys("A2", [0, 1]), keys("A2", [0, 1]), part("A2", 0, 2), part("A2", 0, 2), -1.0, None, A.max, n=2 * C, k=.5)
+        other([2], lambda j: [(B("I512N"), ng), (B("IH"), b("YK")), (B("IH"), b("TP", 15, L, 16))], "IH I512N .NG .YK " + need("TP"), ZO - 0.25)
         def finish(js):
             i, e, n = js[0], js[-1] + 1, C * len(js)
             tt(kx(*js) + " " + keys("A2", js), keys("A3", js), part("A3", i, e), c(bx, i, e), part("A2", i, e), A.max, n=n, k=1, banks=[nx])
-            bank = newbank()
-            terms = lambda j: ((B("ID"), part("CV", 2 + j)), (B("I4"), ng), (B("BKN"), far)) if j < 2 else ((B("I512N"), ng), (B("IH"), b("YK")), (B("IH"), b("TP", 15, L, 16)))
-            op(TE, x("ON1 C3 ID I4 BKN IH I512N .NG .FAR " + keys("CV", [2 + j for j in js if j < 2]) + (" .YK " + need("TP") if 2 in js else "")), bank, ct(n, *[C] * (3 * len(js))), mm(lambda: group(None, [
-                (ones, B("C3", C * i, C * e), c(pool(bank), i, e))] + [(w, y, c(pool(bank), j)) for j in js for w, y in terms(j)])), get=bank)
             ko = "o%d%d%d" % (t, h, i)
             out = T["o%d%d" % (t, h)][:, C * i:C * e] if t < 3 else part("FIN", i, e)
-            op(V, x(bank + " " + keys("A3", js)), ko, cv(n), lambda q: q.tensor_tensor(out, c(pool(bank), i, e), part("A3", i, e), A.max), put=bank)
+            tt(ky(*js) + " " + keys("A3", js), ko, out, c(by, i, e), part("A3", i, e), A.max, n=n, k=1, banks=[ny])
             if t < 3:
                 op(G, ko, " ".join("m%d%d%s" % (t + 1, h, "dtz"[j]) for j in js), 1.0, ("send", HOPS[t], T["m%d%d" % (t + 1, h)][:, C * i:C * e], out), lat=K["hop"], sem="a%d%d%d" % (t + 1, h, i), val=NENG)
                 return
             ls = [j for j in js if j < 2]
             if ls:
                 i, e, n = ls[0], ls[-1] + 1, C * len(ls)
-                ts(ko, keys("R0", ls) + x(" .R0"), part("R0", i, e), part("FIN", i, e), -1.0, None, A.max, n=n, k=.5)
-                act(keys("R0", ls), keys("OUT", ls), part("OUT", i, e), part("R0", i, e), F.Copy, n=n, scale=2048.0, bias=2047.0)
+                act(ko, keys("OUT", ls), part("OUT", i, e), part("FIN", i, e), F.Copy, n=n, scale=2048.0, bias=2047.0)
             if 2 in js:
                 ts(ko, keys("OUT", [2]), part("OUT", 2), part("FIN", 2), -ZO, None, A.add)
             for j in js:
@@ -393,24 +410,21 @@ def build(T):
             if js[0] < 2: refill([j for j in js if j < 2])
             finish(js)
 
-    def proofs(t, h):
-        now[0] = h
-        X = lambda n: n + str(h)
-        b = lambda n, *a, **k: B(X(n), *a, **k)
-        x = lambda s: " ".join(X(w[1:]) if w[0] == "." else w for w in s.split())
-        bank = newbank()
-        cp(x(".VI2"), x(".VL"), b("VL"), b("VI2", NC, 2 * NC), n=NC)
-        op(TE, x("LK TRI SEIq0 SEIq1 SEIq2 SEIq3 I2KN .VL .NG"), bank, ct(C, C, *[64] * 16), mm(lambda: group(None, [(B("LK"), B("TRI"), pool(bank)[:, 0:C])] + [
-            (sel(r, "SEI"), b("VL"), pool(bank)[:, r:C:16]) for r in range(16)] + [(B("I2KN"), b("NG", C, 2 * C), pool(bank)[:, 0:C])])), get=bank)
-        op(V, bank + " SP", x(".EP"), cv(C), lambda q: q.tensor_scalar(b("EP"), pool(bank)[:, 0:C], 0.0, B("SP", 0, 1), A.is_equal, A.mult), put=bank)
-        scan(x(".EP RST0"), x(".LS"), b("LS"), B("RST0"), b("EP"), A.mult, A.max, k=.5)
-        tt(x(".LS .VL"), x(".WO"), b("WO"), b("LS", 15, C, 16), b("VL"), A.max, n=NC)
-        cp(x(".WO"), x(".OFW"), b("OFW", 0, 2 * NC, 2), b("WO"), n=NC)
-
-    def writes(t, h):
-        now[0] = h
-        for j in range(NC):
-            ts("OFW%d TN%d scwd" % (h, h), "scw", T.scw[:, 0:528].indirect(B("OFW%d" % h, 2 * j, 2 * j + 1)), B("TN%d" % h, 16 * j, 16 * j + 16), 1.0, -1.0, A.mult, A.add, n=16, k=K["sca"])
+    def proofs(t):
+        hs, bank, n = range(NH_), newbank(), M // 16
+        each = lambda k: " ".join(k + str(h) for h in hs)
+        for h in hs:
+            cp("VI2%d" % h, "VL%d" % h, B("VL", NC * h, NC * h + NC), B("VI2%d" % h, NC, 2 * NC), n=NC)
+        op(TE, "LK TRI SEIq0 SEIq1 SEIq2 SEIq3 I512N ID %s %s %s" % (each("VL"), each("NG"), each("NH")), bank, ct(M, *[C] * (3 * NH_), *[64] * 16), mm(lambda: group(None, [
+            (B("LK"), B("TRI"), pool(bank)[:, 0:M])] + [(sel(r, "SEI"), B("VL"), pool(bank)[:, r:M:16]) for r in range(16)] + [
+            (w, y, pool(bank)[:, C * h:C * h + C]) for h in hs for w, y in ((B("I512N"), B("NG%d" % h, 0, C)), (B("I512N"), B("NG%d" % h, C, 2 * C)), (B("ID"), B("NH%d" % h)))])), get=bank)
+        op(V, bank + " SP", "EP", cv(M), lambda q: q.tensor_scalar(B("EP"), pool(bank)[:, 0:M], 0.0, B("SP", 0, 1), A.is_equal, A.mult), put=bank)
+        scan("EP RST0", "LS", B("LS"), B("RST0"), B("EP"), A.mult, A.max, n=M, k=.5)
+        tt("LS " + each("VL"), "WO", B("WO"), B("LS", 15, M, 16), B("VL"), A.max, n=n)
+        cp("WO", "OFW", B("OFW", 0, 2 * n, 2), B("WO"), n=n)
+        for j in range(n):
+            h, a = divmod(16 * j, C)
+            ts("OFW TN%d scwd" % h, "scw", T.scw[:, 0:528].indirect(B("OFW", 2 * j, 2 * j + 1)), B("TN%d" % h, a, a + 16), 1.0, -1.0, A.mult, A.add, n=16, k=K["sca"])
 
     for t in range(4):
         now[1] = t
@@ -427,9 +441,7 @@ def build(T):
             ts("AI", "AI2", col("AI2", 0), col("AI", 0), 31, None, A.bitwise_and, n=1)
             ts("AI2 NTH", "NLIM", col("NLIM", 0), col("AI2", 0), -0.5, col("NTH", 0), A.mult, A.add, n=1)
             ts("BK NLIM", "CMb%d" % ((t + 1) % 2), B("CM%d" % ((t + 1) % 2), 128, 256), B("BK"), col("NLIM", 0), None, A.mult, n=128)
-        for h in range(NH_):
-            proofs(t, h)
-            writes(t, h)
+        proofs(t)
     op(Y, "scw", "ysd", 0.1, lambda q: q.dma_start(T.ys[:], T.scw[:, 0:512]), lat=2.5, sem="out%d" % (NOUT - 1), val=16)
     return ops
 
@@ -444,6 +456,7 @@ def depend(ops):
             last[k] = o["i"]
             readers[k] = []
         o["d"].discard(o["i"])
+        o["free"] = {j for j in o["d"] if ops[j]["e"] == o["e"] == "t"}
     return ops
 
 
@@ -454,7 +467,7 @@ def schedule(ops, off):
     for o in ops:
         for i in o["d"]:
             succ[i].append(o["i"]); left[o["i"]] += 1
-    gap = lambda i, j: 0.0 if ops[i]["e"] == ops[j]["e"] == "t" else wake
+    gap = lambda i, j: 0.0 if i in ops[j]["free"] else wake
     pri = [0.0] * n
     for o in reversed(ops):
         pri[o["i"]] = o["c"] + o["lat"] + max([pri[j] + gap(o["i"], j) for j in succ[o["i"]]] or [0.0])
@@ -498,36 +511,47 @@ def schedule(ops, off):
 def timer(ops):
     n, wake = len(ops), K["wake"]
     E, cost, lat = [o["e"] for o in ops], [o["c"] for o in ops], [o["lat"] for o in ops]
-    D = [[(j, 0.0 if E[j] == o["e"] == "t" else wake) for j in o["d"]] for o in ops]
-    BK, get, put = [o["b"] for o in ops], [o["get"] for o in ops], [o["put"] for o in ops]
-    def times(order):
-        end, why, res = [0.0] * n, [-1] * n, [False] * n
-        free, bank, given, before = {}, {}, {}, {}
-        banks = [[0.0, -1, j] for j in range(NPOOL)]
-        for i in order:
-            x, w, r = 0.0, -1, False
-            for j, g in D[i]:
-                if end[j] + g > x: x, w = end[j] + g, j
-            e = E[i]
-            f = free.get(e)
-            if f and f[0] > x: x, w, r = f[0], f[1], True
-            for k in BK[i]:
-                for e2, (tm, j) in bank.get(k, {}).items():
-                    if e2 != e and tm + wake > x: x, w, r = tm + wake, j, True
-            if get[i]:
-                q = min(banks)
-                if q[0] > 1e8: return None
-                if q[1] >= 0:
+    anc, D = [0] * n, []
+    for o in ops:
+        far = 0
+        for j in o["d"]: far |= anc[j]
+        D.append([(j, 0.0 if j in o["free"] else wake) for j in o["d"] if not far >> j & 1])
+        for j in o["d"]: far |= 1 << j
+        anc[o["i"]] = far
+    BK, get, put = [o["b"][0] if o["b"] else None for o in ops], [o["get"] for o in ops], [o["put"] for o in ops]
+    def times(order, old=None, same=0):
+        if old is None:
+            end, why, res, given, before, marks, a = [0.0] * n, [-1] * n, [False] * n, {}, {}, [], 0
+            last, banks = {}, [(0.0, -1, j) for j in range(NPOOL)]
+        else:
+            a = same // 32
+            end, why, res, given, before, marks = old[0][:], old[1][:], old[2][:], dict(old[3]), dict(old[4]), old[5][:a]
+            last, banks = dict(old[5][a][0]), old[5][a][1][:]
+        for a in range(32 * a, n, 32):
+            marks.append((dict(last), banks[:]))
+            for i in order[a:a + 32]:
+                x, w, r = 0.0, -1, False
+                for j, g in D[i]:
+                    if end[j] + g > x: x, w = end[j] + g, j
+                e, k = E[i], BK[i]
+                f = last.get(e)
+                if f and f[0] > x: x, w, r = f[0], f[1], True
+                if k:
+                    f = last.get(k)
+                    if f and f[2] != e and f[0] + wake > x: x, w, r = f[0] + wake, f[1], True
+                if get[i]:
+                    q = min(banks)
+                    if q[0] > 1e8: return None
                     before[i] = q[1]
-                    if q[0] + wake > x: x, w, r = q[0] + wake, q[1], True
-                given[get[i]] = q
-                q[0] = 1e9
-            y = x + cost[i]
-            free[e] = (y, i)
-            for k in BK[i]: bank.setdefault(k, {})[e] = (y, i)
-            if put[i]: given[put[i]][0:2] = [y, i]
-            end[i], why[i], res[i] = y + lat[i], w, r
-        return end, why, res, {k: q[2] for k, q in given.items()}, before
+                    if q[1] >= 0 and q[0] + wake > x: x, w, r = q[0] + wake, q[1], True
+                    given[get[i]] = q[2]
+                    banks[q[2]] = (1e9, -1, q[2])
+                y = x + cost[i]
+                last[e] = f = (y, i, e)
+                if k: last[k] = f
+                elif put[i]: banks[given[put[i]]] = (y, i, given[put[i]])
+                end[i], why[i], res[i] = y + lat[i], w, r
+        return end, why, res, given, before, marks
     return times
 
 
@@ -578,7 +602,7 @@ def swap(ops, order, rng, rounds, hot=0.15, cold=0.01):
             if i in S: continue
             new = [x for x in seg if x not in S] + [x for x in seg if x in S]
         p = order[:a] + new + order[a + len(seg):]
-        d = times(p)
+        d = times(p, cur, a)
         if d is None: continue
         y = max(d[0])
         if y <= c or z < math.exp((c - y) / (hot * (cold / hot) ** (it / rounds))):
@@ -593,17 +617,17 @@ def plan(ops):
     depend(ops)
     rng = np.random.default_rng(SEED)
     order = swap(ops, shift(ops, rng, ROUNDS[0]), rng, ROUNDS[1])
-    end, _, _, given, before = timer(ops)(order)
+    end, _, _, given, before, _ = timer(ops)(order)
     deps, prev = [set(o["d"]) for o in ops], {}
     for i in order:
         o = ops[i]
-        if i in before: deps[i].add(before[i])
+        if before.get(i, -1) >= 0: deps[i].add(before[i])
         for k in o["b"]:
             p = prev.setdefault(k, {})
             for e, j in p.items():
                 if e != o["e"]: deps[i].add(j)
             p[o["e"]] = i
-    PLAN.update(order=order, time=max(end), bank=given, d=deps, end=end)
+    PLAN.update(order=order, time=max(end), bank=given, d=deps, end=end, free=[o["free"] for o in ops])
 
 
 def rank_program(g, core, T, topo):
@@ -621,7 +645,7 @@ def rank_program(g, core, T, topo):
         e, q = o["e"], queue[o["e"]]
         kn = know[e]
         for j in sorted(PLAN["d"][i], key=lambda j: -clock[j][2]):
-            if e == ops[j]["e"] == "t":
+            if j in PLAN["free"][i]:
                 continue
             s, v, _, c = clock[j]
             if kn.get(s, 0) < v:

import math
import numpy as np
from concourse.mybir import dt, AluOpType as A, ActivationFunctionType as F

N = 6
HOPS = [1, 2, 3]
M, C = 192, 96
NH_, NC, L = M // C, C // 16, 16 * C
LB = 4
NB = 16 // LB
BIG = 30000.0
ZO = 1536.0
EQ = 3 / 128

H, BF, F4, I4, U2 = "float16", "bfloat16", "float32", "int32", "uint16"
PER = {
    "OFT": (U2, C), "OFX": (U2, C), "OFN": (U2, 8), "OFV": (U2, 2 * NC), "LI": (I4, 2 * C), "VI": (I4, 2 * NC), "VI2": (I4, 2 * NC),
    "ZE": (H, L // 2), "GD": (H, L), "GN": (H, L), "XT": (H, L), "TP": (H, L),
    "EQ0": (BF, L), "EQ1": (BF, L), "EQ2": (BF, L),
    "FL": (H, 2 * C), "FK": (H, 2 * C), "NH": (H, C), "OH": (H, 128), "NF": (H, 128), "FAR": (BF, C), "R0": (H, 2 * C), "R1": (BF, 2 * C),
    "DT1": (H, 2 * C), "SA": (H, 2 * C), "SB": (H, 2 * C),
    "CV": (H, 4 * C), "YK": (H, C), "YM": (H, C), "NG": (H, 2 * C), "A2": (H, 3 * C), "A3": (H, 3 * C), "FIN": (H, 3 * C),
    "MX": (F4, 128), "SM": (F4, 128), "JK": (F4, C), "TN": (F4, C), "OUT": (F4, 3 * C),
}
SCALED = {"IDN": -1, "I3N": -3, "I4": 4, "I56N": -56, "I512": 512, "I512N": -512, "I2K": 2048, "I8K": 8192, "IH": 0.5}
ONE = {
    "SEI": (BF, 2048), "GG": (BF, 2048), "SX": (BF, 1024), "DF": (BF, 1024), "ON1": (BF, 1024),
    "ID": (BF, 128), "BK": (BF, 128), "BKN": (BF, 128), "BKC": (BF, 128), "W16": (BF, 16),
    "RSTB": (BF, L), "RST8": (BF, L // 2), "PQ": (BF, 512), "RST0": (BF, M), "CZ": (BF, 2 * C), "CY": (BF, 2 * C), "LC": (BF, 2 * NC), "TRI": (BF, M), "LK": (BF, 128), "SH": (BF, 256), "ILO": (BF, 128), "IHI": (BF, 128), "Z0": (BF, M), "ZR": (BF, 1024), "IB": (BF, 128),
    "ZSS": (H, L // 2), "CM0": (H, 256), "CM1": (H, 256), "CB": (F4, 8), "IA": (I4, 8), "IC": (I4, 8),
    "THR": (I4, 8), "TH1": (I4, 8), "TH2": (I4, 8), "NTH": (F4, 8), "NLIM": (F4, 8), "ACN": (F4, 16), "AS": (F4, 8), "AI": (I4, 8), "AI2": (I4, 8), "SP": (F4, 8),
    "SI": (I4, 512), "VL": (H, M // 16), "EP": (H, M), "LS": (H, M), "WO": (H, M // 16), "OFW": (U2, M // 8),
}
ONE.update({_n: (BF, 128) for _n in SCALED})
WHERE = {}
_tot = {}
for _n, (_d, _w) in [(n + str(h), x) for n, x in PER.items() for h in range(NH_)] + list(ONE.items()):
    WHERE[_n] = (_d, _tot.get(_d, 0), _w)
    _tot[_d] = _tot.get(_d, 0) + (_w + 15) // 16 * 16

SCRATCH = {"p_" + _d: ("sbuf", [128, _w], _d) for _d, _w in _tot.items()}
SCRATCH["tab"] = ("sbuf", [128, 4112], BF)
SCRATCH["scw"] = ("sbuf", [128, 528], F4)
SCRATCH["stw"] = ("sbuf", [128, 512], I4)
for _h in range(NH_):
    for _t in range(4):
        SCRATCH["m%d%d" % (_t, _h)] = ("sbuf", [128, 4 * C], H)
        if _t < 3:
            SCRATCH["o%d%d" % (_t, _h)] = ("sbuf", [128, 3 * C], H)
SENDS = [[0, 1, 2]]
LAST = [[2], [0, 1]]
NPOOL = 4
for _b in ("cm0", "cm1", "cm2", "cm3", "bx0", "bx1", "by0", "by1"):
    SCRATCH[_b] = ("psum", [128, 512], F4)
NLOAD, NOUT = 2 * NH_ + 14, 3 * NH_ + 1
SEMAPHORES = ["v", "s", "t", "g", "loc"] + ["l%d" % i for i in range(NLOAD)] + ["a%d%d%d" % (t, h, js[0]) for t in (1, 2, 3) for h in range(NH_) for js in SENDS] + ["out%d" % i for i in range(NOUT)]
MAGIC = 1.5 * 2.0 ** 30

K = {"v": 0.87e-3, "t": 0.435e-3, "fix": 0.05, "wake": 0.13, "gat": 1.56, "sca": 3.8, "hop": 4.0, "lag": 8.0}
def cv(n, k=1.0): return K["fix"] + K["v"] * max(64, n * k)
def ct(*ns): return sum(K["t"] * max(64, n) for n in ns) + 0.03

ALL, FIRST, END = "SSSS" "SSSV" "SSSS", "SSSS" "SSSV" "SSSS", "SSSS" "SVSV" "SVSV"
MODES = [[FIRST, FIRST], [ALL, ALL], [ALL, ALL], [ALL, END]]
ON = {"ZSS": "s", "FKD": "s", "FKT": "s"}
SEMAPHORES += ["k%d%d%d" % (t, h, j) for t in range(4) for h in range(NH_) for j in range(4)]
PARTS = {"XT": 2, "TP": 1}
ROUNDS, SEED = (200, 150000), 0
NENG = 8
PLAN = {}


def build(T):
    ops = []
    now = [0, -1]

    def B(name, lo=0, hi=None, step=1, p=None):
        d, a, w = WHERE[name]
        hi = w if hi is None else hi
        t = T["p_" + d]
        rows = slice(0, 128) if p is None else slice(*p)
        return t[rows, a + lo:a + hi] if step == 1 else t[rows, a + lo:a + hi:step]

    def back(name, n, p):
        d, a, w = WHERE[name]
        return T["p_" + d][slice(*p), a + n - 1:(a - 1 if a else None):-1]

    def op(eng, rd, wr, cost, fn, banks=(), lat=0.0, sem=None, val=1, get=None, put=None):
        ops.append(dict(h=now[0], t=now[1], e=eng, r=rd.split(), w=wr.split(), c=cost, f=fn, lat=lat, sem=sem, val=val, b=list(banks), i=len(ops), get=get, put=put))

    def mm(calls):
        def f(q):
            x = None
            for o, a, b, s, e in (calls if isinstance(calls, list) else calls()):
                x = q.matmul(o, a, b, s, e)
            return x
        return f

    def group(out, pairs, start=True, stop=True):
        k = len(pairs)
        return [(out if len(x) == 2 else x[2], x[0], x[1], start and j == 0, stop and j == k - 1) for j, x in enumerate(pairs)]

    pool = lambda k: T["cm%d" % PLAN["bank"][k]]
    sel = lambda l, nm="SEL": B(nm, 128 * l, 128 * l + 128)
    V, S, TE, G, Y = "v", "s", "t", "g", "y"

    def ts(rd, wr, out, i, s1, s2, o0, o1=None, n=C, k=1.0, banks=()):
        op(V, rd, wr, cv(n, k), (lambda q: q.tensor_scalar(out, i, s1, s2, o0, o1)) if o1 is not None else (lambda q: q.tensor_scalar(out, i, s1, None, o0)), banks)
    def tt(rd, wr, out, a, b, o, n=C, k=2.0, banks=()):
        op(V, rd, wr, cv(n, k), lambda q: q.tensor_tensor(out, a, b, o), banks)
    def cp(rd, wr, out, i, n=C, k=1.0, banks=()):
        op(V, rd, wr, cv(n, k), lambda q: q.tensor_copy(out, i), banks)
    def scan(rd, wr, out, a, b, o0, o1, n=C, k=1.0, banks=()):
        op(V, rd, wr, cv(n, k), lambda q: q.tensor_tensor_scan(out, a, b, 0.0, o0, o1), banks)
    def act(rd, wr, out, i, f, n=C, banks=(), k=1.0, **kw):
        op(S, rd, wr, K["fix"] + K["v"] * n * k, lambda q: q.activation(out, i, f, **kw), banks)
    def pe(rd, wr, calls, bank, *ns):
        op(TE, rd, wr, ct(*ns), mm(calls), [bank])

    nl = [0]
    def load(dst, out, src, eng=Y, rd="", kb=100):
        op(eng, rd, dst, 0.1, lambda q: q.dma_start(out, src), lat=2.0 + kb / 250.0, sem="l%d" % nl[0], val=16)
        nl[0] += 1
    for h in range(NH_):
        s = slice(C * h, C * h + C)
        load("LIt%d" % h, B("LI%d" % h, C, 2 * C), T.tl[:, s], kb=50)
        load("LId%d" % h, B("LI%d" % h, 0, C), T.dl[:, s], kb=50)
        if h == 0:
            load("Z0", B("Z0"), T.z0[:], kb=50, eng=S)
            load("taba", T.tab[:, 16:2064], T.clk[:, 0:2048], kb=520)
            load("tabb", T.tab[:, 2064:4112], T.clk[:, 2048:4096], eng=S, kb=520)
            load("THR", B("THR", 0, 1), T.th[:], kb=1)
    load("SIc", B("SI", 0, 512), T.sc[:], kb=260)
    load("stw", T.stw[:], T.st[:], kb=260)
    TAB = "taba tabb tabm"
    tab = T.tab[:, 0:4112]

    def ms(name, c, lo=0, hi=None, step=1, p=None, key=None, eng=S):
        n = len(range(lo, WHERE[name][2] if hi is None else hi, step))
        if eng == V:
            op(V, "", key or name, cv(n, 0.5), lambda q: q.memset(B(name, lo, hi, step, p), c))
        else:
            act("ON1", key or name, B(name, lo, hi, step, p), B("ON1", 0, n, p=p), F.Copy, n=n, scale=float(c))
    def iota(name, n, pat, base, cmul):
        op(G, "", name, 0.13 + 2 * K["v"] * n, lambda q: q.iota(B(name, 0, n), pat, base, cmul, allow_small_or_imprecise_dtypes=True))
    def aff(out, src, n, pat, cmp, base, cmul, fill=0.0, at=0, p=None, key=""):
        a = at if src == out else 0
        op(G, (src + key if src == out else src + " ON2" * (n > 384)), out + key, 0.17 + 2 * K["v"] * n, lambda q: q.affine_select(B(out, at, at + n, p=p), B(src, a, a + n, p=p), pat, cmp, fill, base, cmul))
    LO, HI = (0, 64), (64, 128)
    ms("ON1", 1.0, 0, 384, eng=V)
    ms("ON1", 1.0, 384, 1024, key="ON2", eng=V)
    act("ON1", "tabm", T.tab[:, 0:16], B("ON1", 0, 16), F.Copy, n=16, scale=-1.0)
    for q in (0, 1):
        for a in (0, 1):
            aff("PQ", "ON1", 128, [[-16, 8], [992, 2], [-1, 8]], A.is_equal, -8 * (q - a) - 1000 * a, 1, at=128 * (2 * q + a), key=str(2 * q + a))
    aff("ID", "ON1", 128, [[-1, 128]], A.is_equal, 0, 1)
    aff("BKC", "ON1", 128, [[-16, 8], [0, 16]], A.is_ge, 0, 1)
    aff("BK", "BKC", 128, [[16, 8], [0, 16]], A.is_ge, 15, -1)
    aff("DF", "ON1", 1024, [[-1, 16], [-16, 4], [0, 16]], A.is_equal, -64, 1, key="u")
    aff("SH", "ON1", 256, [[-1, 256]], A.is_equal, 64, 1)
    aff("ILO", "ID", 128, [[0, 128]], A.is_ge, 63, -1)
    aff("IHI", "ID", 128, [[0, 128]], A.is_ge, -64, 1)
    iota("IB", 128, [[0, 8], [-1, 16]], 15, 0)
    iota("IA", 1, [[0, 1]], 0, 1)
    aff("LK", "ON1", 128, [[0, 8], [-1, 16]], A.is_equal, 0, 1)
    iota("TRI", M, [[0, M]], 1024, 0)
    aff("TRI", "TRI", M, [[0, M // 16], [1, 16]], A.is_gt, 0, -1, 2048.0)
    aff("TRI", "TRI", M, [[0, M // 16], [1, 16]], A.not_equal, 0, -1, 512.0)
    act("ID DFu", "DFl", B("DF", 0, 64, p=LO), B("ID", 0, 64, p=LO), F.Copy, n=64, scale=-1.0)
    for w in (64, 128):
        act("DFl", "DFl", B("DF", w, 2 * w, p=LO), B("DF", 0, w, p=LO), F.Copy, n=w)
    for j in (1, 2, 3):
        load("DF%d" % j, B("DF", 256 * j, 256 * j + 256, p=LO), B("DF", 0, 256, p=LO), rd="DFl", kb=30)
    for j in range(4):
        k = "q%d" % j
        aff("SEI", "ON1", 512, [[-1, 4], [-16, 8], [0, 16]], A.is_equal, -4 * j, 1, at=512 * j, key=k)
        aff("SEI", "SEI", 512, [[0, 4], [-1, 128]], A.not_equal, 0, 1, -1.0, at=512 * j, key=k)
        aff("SEI", "SEI", 512, [[-1, 4], [-512, 8], [-31, 16]], A.not_equal, -4 * j, 32, at=512 * j, key=k)
    ms("RST8", BIG, eng=V)
    ms("RST8", -BIG, 0, L // 2, 8, eng=V)
    ms("RSTB", BIG, eng=V)
    ms("RSTB", -BIG, 0, L, 16, eng=V)
    ms("ZSS", 0.0, eng=V)
    ms("ZR", 0.0, eng=V)
    for j in (0, 1):
        load("GG%d" % j, B("GG", 1024 * j, 1024 * j + 1024), B("ZR"), rd="ZR", kb=260)
    ms("SX", 0.0, 64, 128)
    act("ID", "SX", B("SX", 0, 64, p=LO), B("ID", 0, 64, p=LO), F.Copy, n=64, scale=-128.0)
    act("ID", "SX", B("SX", 0, 64, p=HI), B("ID", 64, 128, p=HI), F.Copy, n=64, scale=-128.0)
    act("SX", "SX", B("SX", 128, 256), B("SX", 0, 128), F.Copy, n=128)
    for j in (1, 2, 3):
        load("SX%d" % j, B("SX", 256 * j, 256 * j + 256), B("SX", 0, 256), rd="SX", kb=60)
    for g in range(8):
        a = 64 * (g % 2) + 16 * (g // 2)
        act("BK SX1 SX2 SX3", "SXg%d" % g, B("SX", 64 + 16 * (g // 2) + g % 2, 1024, 130), B("BK", a, a + 8), F.Copy, n=8, scale=-128.0)
        act("BK GG0 GG1", "GGg%d" % g, B("GG", 16 * g, 2048, 129), B("BK", 16 * g, 16 * g + 16), F.Copy, n=16, scale=-128.0)
    GGK = " ".join("GGg%d" % g for g in range(8))
    SXK = " ".join("SXg%d" % g for g in range(8))
    for out, k in SCALED.items():
        act("ID", out, B(out), B("ID"), F.Copy, n=128, scale=float(k))
    act("BK", "BKN", B("BKN"), B("BK"), F.Copy, n=128, scale=-1.0)
    act("BK", "W16a", B("W16", 0, 8), B("BK", 0, 128, 16), F.Copy, n=8)
    act("BK", "W16b", B("W16", 8, 16), B("BK", 0, 128, 16), F.Copy, n=8, scale=-2.0)
    def sums(name, parts):
        a = 0
        for w, hi, lo in parts:
            if lo is None:
                ms(name, hi / 128, a, a + w)
            else:
                ms(name, hi / 64, a, a + w, p=LO)
                ms(name, lo / 64, a, a + w, p=HI)
            a += w
    sums("CZ", [(C, 2 * ZO, None), (C, -512, None)])
    sums("CY", [(2 * C, 24576, 57)])
    ms("LC", 0.0)
    ms("LC", 128.0, NC, 2 * NC)
    ms("RST0", 1.0)
    ms("RST0", 0.0, 0, M, 16)
    ms("CB", 2048.0, 0, 1, key="CB0")
    ms("CB", float(np.log(EQ / (1 - EQ))), 1, 2, key="CB1")
    ms("CB", 4096 * 2047.5, 2, 3, key="CB2")
    ms("CB", -3072.0, 3, 4, key="CB3")
    ms("CB", 512.0, 4, 5, key="CB4")
    for j in (0, 1):
        act("IB", "CMa%d" % j, B("CM%d" % j, 0, 128), B("IB"), F.Copy, n=128, scale=1 / 2048)
    ts("IA", "IC", B("IC", 0, 1), B("IA", 0, 1), 15, None, A.bitwise_and, n=1)
    ts("IC", "SP", B("SP", 0, 1), B("IC", 0, 1), 512.0, None, A.add, n=1)
    ms("AS", 0.0)
    tt("THR IC", "TH1", B("TH1", 0, 1), B("THR", 0, 1), B("IC", 0, 1), A.add, n=1)
    ts("TH1", "TH2", B("TH2", 0, 1), B("TH1", 0, 1), 4, None, A.arith_shift_right, n=1)
    ts("TH2", "NTH", B("NTH", 0, 1), B("TH2", 0, 1), -1.0, ZO - 512, A.mult, A.add, n=1)
    ts("BK NTH", "CMb0", B("CM0", 128, 256), B("BK"), B("NTH", 0, 1), None, A.mult, n=128)

    for h in range(NH_):
        m = T["m0%d" % h]
        ts("LIt%d LId%d" % (h, h), "m0%dd m0%dt" % (h, h), m[:, 0:2 * C], B("LI%d" % h), 1 / 2048, -2047 / 2048, A.mult, A.add, n=2 * C)
        act("Z0", "m0%dz" % h, m[:, 2 * C:3 * C], B("Z0", C * h, C * h + C), F.Copy, bias=ZO)
    act("SIc", "scw", T.scw[:, 0:512], B("SI", 0, 512), F.Copy, n=512)
    act("ON1", "scwd", T.scw[:, 512:528], B("ON1", 0, 16), F.Copy, n=16)

    nblk = [0]
    def newbank():
        nblk[0] += 1
        return "blk%d" % nblk[0]

    def parts(name):
        k = PARTS[name]
        return [(L * i // k, L * (i + 1) // k, (C * i // k, C * (i + 1) // k), "%d_" % i) for i in range(k)]
    def need(name, a=0, e=L):
        return " ".join("." + name + k for a1, e1, o, k in parts(name) if a1 < e and a < e1)

    def chunk(t, h):
        now[0] = h
        m = T["m%d%d" % (t, h)]
        X = lambda n: n + str(h)
        b = lambda n, *a, **k: B(X(n), *a, **k)
        D, TT, Z, DT = m[:, 0:C], m[:, C:2 * C], m[:, 2 * C:3 * C], m[:, 0:2 * C]
        kd, kt, kz = ("m%d%d%s" % (t, h, j) for j in "dtz")
        km = kd + " " + kt
        x = lambda s: " ".join(X(w[1:]) if w[0] == "." else w for w in s.split())
        nx, ny = "bx%d" % (h % 2), "by%d" % (h % 2)
        bx, by = T[nx], T[ny]
        kx = lambda *js: " ".join(nx + str(j) for j in js)
        ky = lambda *js: " ".join(ny + str(j) for j in js)
        c = lambda bank, i, j=None: bank[:, C * i:C * (i + 1 if j is None else j)]
        P = (0, C)
        ones = B("ON1", 0, 128)
        def stack(j, wr, out, src):
            op(Y, km, x(wr), 0.1, lambda q: q.dma_start(out, src), lat=2.1, sem="k%d%d%d" % (t, h, j), val=16)
        stack(0, ".SAd .SAt", b("SA", p=HI), m[0:64, 0:2 * C])
        stack(1, ".SAc", b("SA", 0, C, p=LO), m[0:64, C:2 * C])
        stack(2, ".SBd .SBt", b("SB", p=LO), m[64:128, 0:2 * C])
        stack(3, ".SBc", b("SB", 0, C, p=HI), m[64:128, C:2 * C])
        def compare(j, col, kt=None, last=True):
            for k in range(NB):
                bank, w, up = newbank(), LB * C, k >= NB // 2
                ss = range(LB * k % 8, LB * k % 8 + LB)
                src, ks = b("SB" if up else "SA", C * col, C * col + C), (".SBd .SBc", ".SBt .SB2")[col] if up else (".SAd .SAc", ".SAt .SA2")[col]
                op(TE, x("DFu DFl DF1 DF2 DF3 " + ks), bank, ct(*[C] * LB), mm((lambda bank, ss, src: lambda: [
                    (pool(bank)[:, C * i:C * i + C], sel(s, "DF"), src, True, True) for i, s in enumerate(ss)])(bank, ss, src)), get=bank)
                eq, ke = b("EQ%d" % j, w * k, w * k + w), x(".EQ%d_%d_" % (j, k))
                if MODES[t][h][NB * j + k] == "V":
                    op(V, bank, ke, cv(w), (lambda bank, eq: lambda q: q.tensor_scalar(eq, pool(bank)[:, 0:w], 0.0, EQ, A.is_equal, A.mult))(bank, eq), put=bank)
                else:
                    op(S, bank + " CB1", ke, cv(w), (lambda bank, eq: lambda q: q.activation(eq, pool(bank)[:, 0:w], F.Sigmoid, bias=B("CB", 1, 2), scale=524288.0))(bank, eq), put=bank)
                e = lambda i: b("EQ%d" % j, w * k + C * i, w * k + C * i + C)
                if j == 0:
                    first = k % (NB // 2) == 0
                    calls = [(B("ID"), src)] * first + [(sel(s, "SX"), e(i)) for i, s in enumerate(ss)]
                    pe(x("ID %s %s %s" % (SXK, ke, ks * first)), kx(int(up), "o"), group(c(bx, int(up)), calls, first, k % (NB // 2) == NB // 2 - 1), nx, *[C] * len(calls))
                else:
                    calls = [(B("SX", 128 * s + 64 * up, 128 * s + 64 * up + 64), e(i)) for i, s in enumerate(ss)]
                    pe(SXK + " " + ke, kt, group(by[64 * up:64 * up + 64, C * col:C * col + C], calls, False, last and k % (NB // 2) == NB // 2 - 1), ny, *[C] * len(calls))
        W = L // 2
        pe("PQ0 PQ1 PQ2 PQ3 %s %s" % (kt, kx("o")), kx(2), [y for q in (0, 1) for y in group(bx[:, 2 * C + C // 2 * q:2 * C + C // 2 * (q + 1)], [
            (sel(2 * q + a, "PQ"), m[:, C + a:2 * C:2]) for a in (0, 1)])], nx, *[64] * 4)
        ts(kx(2), x(".OFT"), b("OFT"), c(bx, 2), 2048.0, 2063.0, A.mult, A.add, banks=[nx])
        if ON["ZSS"] == V:
            cp(kz, "ZSS", B("ZSS", 0, W, 8), Z, k=.5)
        else:
            act(kz, "ZSS", B("ZSS", 0, W, 8), Z, F.Copy)
        scan("ZSS RST8", x(".ZE"), b("ZE"), B("RST8"), B("ZSS"), A.min, A.max, n=W, k=.5)
        for q in (0, 1):
            a, e = W * q, W * q + W
            tt(x(TAB + " .OFT .ZE"), x(".GD%d_" % q), b("GD", a, e), tab.indirect(b("OFT", C // 2 * q, C // 2 * (q + 1))), b("ZE"), A.subtract, n=W, k=K["gat"])
            ts(x(".GD%d_" % q), x(".GN%d_" % q), b("GN", a, e), b("GD", a, e), ZO, 0.0, A.add, A.min, n=W, k=.5)
        ts(km, x(".FL"), b("FL"), DT, -1.0, None, A.is_gt, n=2 * C, k=.5)
        pe(x("BK .FL " + kx("o")), kx(4), group(c(bx, 4), [(B("BK"), b("FL", C, 2 * C))]), nx, C)
        act(kx(4) + " CB4", x(".NH"), b("NH"), c(bx, 4), F.Relu, banks=[nx], bias=B("CB", 4, 5), scale=-512.0)
        compare(0, 0)
        cm = "CM%d" % (t % 2)
        calls = [(B("ON1", 0, C), B(cm), by[0:C, 0:256]), (b("FL", C, 2 * C), B("I8K"), by[0:C, 128:256])]
        pe(x("ON1 CMa%d CMb%d I8K .FL" % (t % 2, t % 2)), ky(0, 1, 2, "o"), group(None, calls, True, False), ny, 256, 128)
        for q in (0, 1):
            calls = [(b("GD", W * q + p, W * q + W, 8), B("W16", 0, 8), by[0:C, 128 + 8 * q + p:256:16]) for p in range(8)]
            pe(x("W16a .GD%d_" % q), ky(0, 1, 2, "o"), group(None, calls, False, False), ny, *[64] * 8)
            calls = [(b("GN", W * q + p, W * q + W, 8), B("W16"), by[0:C, 8 * q + p:256:16]) for p in range(8)]
            pe(x("W16a W16b .GN%d_" % q), ky(0, 1, 2, "o"), group(None, calls, False, q == 1), ny, *[64] * 8)
        scan(ky(0, 1) + " RSTB", x(".MX"), b("MX", p=P), B("RSTB", 0, 128, p=P), by[0:C, 0:128], A.min, A.max, n=128, banks=[ny])
        act(ky(1, 2) + " CB0", x(".NF"), b("NF", p=P), by[0:C, 128:256], F.Sigmoid, n=128, banks=[ny], bias=B("CB", 0, 1, p=P), scale=-4096.0)
        scan(ky(0, 1) + " RSTB", ky(3, 4), by[0:C, 415:287:-1], B("RSTB", 0, 128, p=P), by[0:C, 127::-1], A.min, A.max, n=128, banks=[ny])
        tt(x(ky(3, 4) + " .MX"), x(".OH"), b("OH", p=P), by[0:C, 288:416], b("MX", p=P), A.is_equal, n=128, k=1, banks=[ny])
        pe(x(".OH I2K " + kx("o")), kx(2), group(c(bx, 2), [(b("OH", p=P), B("I2K", 0, C, p=P))]), nx, C)
        tt(kx(2) + " " + kt, x(".TH"), m[:, 3 * C:4 * C], c(bx, 2), TT, A.mult, k=1, banks=[nx])
        pl = bx[:, 5 * C:5 * C + 2 * NC]
        pe(x(GGK + " ID LC .TH " + kz + " " + kx("o")), kx(5), group(pl, [(B("ID"), B("LC"))] + [(sel(r, "GG"), m[:, 2 * C + r:4 * C:16]) for r in range(16)]), nx, *[64] * 17)
        ts(kx(5), x(".VI"), b("VI"), pl, -1 / 128, None, A.mult, n=2 * NC, banks=[nx])
        ts(kx(5), x(".OFN"), b("OFN", 0, NC), bx[:, 5 * C + NC:5 * C + 2 * NC], -1 / 128, 2064.0, A.mult, A.add, n=NC, banks=[nx])
        ts(x(".VI"), x(".VI2"), b("VI2"), b("VI"), 511, None, A.bitwise_and, n=2 * NC)
        cp(x(".VI2"), x(".OFV"), b("OFV"), b("VI2"), n=2 * NC)
        for j, (win, kw, a) in enumerate(((T.scw, "scw", NC), (T.stw, "stw", NC), (T.scw, "scw", 0), (T.stw, "stw", 0))):
            act(x(kw + " .OFV"), x(".CV%d_" % j), b("CV", C * j, C * j + C), win[:, 0:512].indirect(b("OFV", a, a + NC)), F.Copy, k=K["gat"], scale=1 / 2048, bias=-2047 / 2048)
        act(x(TAB + " .OFN"), x(".YK"), b("YK"), tab.indirect(b("OFN", 0, NC)), F.Relu, k=K["gat"])
        ts(kx(0, 1), x(".R0"), b("R0"), c(bx, 0, 2), MAGIC, -MAGIC, A.add, A.add, n=2 * C, banks=[nx])
        tt(x(kx(0, 1) + " .R0"), x(".DT1"), b("DT1"), c(bx, 0, 2), b("R0"), A.subtract, n=2 * C, k=1, banks=[nx])
        def home(j, i):
            lo, hi = (B("SH", 128, 256), B("SH", 0, 128)) if j == 0 else (B("ILO"), B("IHI"))
            return [(lo, b("DT1", 0, C), c(bx, i)), (hi, b("DT1", C, 2 * C), c(bx, i))]
        pe(x("SH .DT1 " + kx("o")), kx(4), group(None, home(0, 4)), nx, C, C)
        ts(kx(4), x(".OFX"), b("OFX"), c(bx, 4), 2048.0, 2063.0, A.mult, A.add, banks=[nx])
        def filled(j, key, src, k, banks):
            if ON["FK" + "DT"[j]] == V:
                ts(key, x(".FK%d_" % j), b("FK", C * j, C * j + C), src, -1.0, None, A.is_gt, k=k, banks=banks)
            else:
                act(key + " CB2", x(".FK%d_" % j), b("FK", C * j, C * j + C), src, F.Sigmoid, banks=banks, bias=B("CB", 2, 3), scale=2.0 ** 23)
        filled(0, kx(4), c(bx, 4), 1, [nx])
        for a, e, o, k in parts("XT"):
            act(x(TAB + " .OFX"), x(".XT" + k), b("XT", a, e), tab.indirect(b("OFX", *o)), F.Copy, n=e - a, k=K["gat"])
        for a, e, o, k in parts("TP"):
            scan(x("RSTB " + need("XT", a, e)), x(".TP" + k), b("TP", a, e), B("RSTB", 0, e - a), b("XT", a, e), A.min, A.max, n=e - a, k=.5)
        oh = (b("OH", p=P), B("I3N", 0, C, p=P))
        pe(x(".NF .DT1 I512 ILO IHI " + kx("o")), kx(3), group(c(bx, 3), [(b("NF", p=P), B("I512", 0, C, p=P))] + home(1, 3)), nx, C, C, C)
        act(kx(3) + " CB3", x(".FAR"), b("FAR"), c(bx, 3), F.Relu, banks=[nx], scale=-2048.0, bias=B("CB", 3, 4))
        pe(x(".OH .DT1 I3N ILO IHI " + kx("o")), kx(4), group(c(bx, 4), [oh] + home(1, 4)), nx, C, C, C)
        filled(1, kx(4), c(bx, 4), 1, [nx])
        act(kx(4) + " CB0", x(".TN"), b("TN"), c(bx, 4), F.Relu, banks=[nx], bias=B("CB", 0, 1), scale=2048.0)
        far, left, nh = b("FAR"), b("FK", 0, C), b("NH")
        ng = b("NG", 0, C)
        if t < 3:
            pe(x("BK BKN .FL .FK0_ .FAR " + kx("o")), kx(3), group(c(bx, 3), [(B("BK"), b("FL", 0, C)), (B("BKN"), left), (B("BKN"), far)]), nx, C, C, C)
            act(kx(3), x(".JK ACN%d%d" % (t, h)), b("JK"), c(bx, 3), F.Relu, banks=[nx], accum_out=B("ACN", NH_ * t + h, NH_ * t + h + 1))
        na = b("NG", C, 2 * C)
        pe(x("ID BK BKN .FAR .FK0_ .NH " + ky("o")), ky(3, 4), group(c(by, 3), [(B("BKN"), left), (B("ID"), nh), (B("BK"), far)]) + group(c(by, 4), [(B("BKN"), far)]), ny, *[C] * 4)
        act(ky(3, 4) + " CB0", x(".NG"), b("NG"), c(by, 3, 5), F.Sigmoid, n=2 * C, banks=[ny], bias=B("CB", 0, 1), scale=4096.0)
        pe(x("BK .FAR " + kx("o")), kx(2), group(c(bx, 2), [(B("BK"), far)]), nx, C)
        tt(x(kx(2) + " .YK"), x(".YM"), b("YM"), c(bx, 2), b("YK"), A.min, k=1, banks=[nx])
        pe(x("ON1 CZ ID IDN I512 .YM .NG %s %s" % (kz, ky("o"))), ky(2), group(c(by, 2), [(ones, B("CZ", C, 2 * C)), (B("ID"), Z), (B("I512"), ng), (B("IDN"), b("YM"))]), ny, C, C, C, C)
        pe(x("SH ILO IHI I3N I512N .DT1 .OH .NG " + kx("o")), kx(0, 1), group(c(bx, 0), [(B("I512N"), ng)] + home(0, 0)) +
           group(c(bx, 1), [(B("I512N"), ng), oh] + home(1, 1)), nx, *[C] * 7)
        pe(x("ON1 CZ ID IDN .YM %s %s" % (kz, kx("o"))), kx(2), group(c(bx, 2), [(ones, B("CZ", 0, C)), (B("IDN"), Z), (B("ID"), b("YM"))]), nx, C, C, C)
        cp(x(".CV0_ .CV1_"), x(".SAc .SA2"), b("SA", p=LO), b("CV", 0, 2 * C, p=LO), n=2 * C, k=.5)
        cp(x(".CV0_ .CV1_"), x(".SBc .SB2"), b("SB", p=HI), b("CV", 0, 2 * C, p=HI), n=2 * C, k=.5)
        part = lambda n, i, j=None: b(n, C * i, C * (i + 1 if j is None else j))
        keys = lambda n, js: " ".join(x(".%s%d_" % (n, j)) for j in js)
        def refill(js):
            i, e, n = js[0], js[-1] + 1, C * len(js)
            pe(x("ON1 CY I3N I56N .NG " + keys("FK", js)), ky(*js, "o"), group(None, [(ones, B("CY", 0, n), c(by, i, e)), (B("I3N"), part("FK", i, e), c(by, i, e))] + [
                (w, y, c(by, j)) for j in js for w, y in ((B("I3N"), ng), (B("I56N"), na))], True, False), ny, n, n, *[C] * (2 * len(js)))
            for j in reversed(js):
                compare(1 + j, j, ky(*js, "o"), j == i)
            act(ky(*js), keys("R1", js), part("R1", i, e), c(by, i, e), F.Copy, n=n, banks=[ny])
            tt(ky(*js) + " " + keys("R1", js), ky(*js), c(by, i, e), c(by, i, e), part("R1", i, e), A.subtract, n=n, k=1, banks=[ny])
            tt(ky(*js) + " " + keys("CV", js), ky(*js), c(by, i, e), c(by, i, e), part("CV", i, e), A.min, n=n, k=1, banks=[ny])
        def other(js, terms, rd, bias):
            i, e, n, bank = js[0], js[-1] + 1, C * len(js), newbank()
            op(TE, x(rd), bank, ct(*[C] * (3 * len(js))), mm(lambda: [y for j in js for y in group(c(pool(bank), j), terms(j))]), get=bank)
            op(S, bank, keys("A2", js), K["fix"] + K["v"] * n, lambda q: q.activation(part("A2", i, e), c(pool(bank), i, e), F.Copy, bias=bias), put=bank)
        other([0, 1], lambda j: [(B("ID"), part("CV", 2 + j)), (B("I4"), ng), (B("I4"), na)], "ID I4 .NG .CV2_ .CV3_", -8.0)
        if t == 3:
            ts(keys("A2", [0, 1]), keys("A2", [0, 1]), part("A2", 0, 2), part("A2", 0, 2), -1.0, None, A.max, n=2 * C, k=.5)
        other([2], lambda j: [(B("I512N"), ng), (B("IH"), b("YK")), (B("IH"), b("TP", 15, L, 16))], "IH I512N .NG .YK " + need("TP"), ZO - 0.25)
        def finish(js):
            i, e, n = js[0], js[-1] + 1, C * len(js)
            tt(kx(*js) + " " + keys("A2", js), keys("A3", js), part("A3", i, e), c(bx, i, e), part("A2", i, e), A.max, n=n, k=1, banks=[nx])
            ko = "o%d%d%d" % (t, h, i)
            out = T["o%d%d" % (t, h)][:, C * i:C * e] if t < 3 else part("FIN", i, e)
            tt(ky(*js) + " " + keys("A3", js), ko, out, c(by, i, e), part("A3", i, e), A.max, n=n, k=1, banks=[ny])
            if t < 3:
                op(G, ko, " ".join("m%d%d%s" % (t + 1, h, "dtz"[j]) for j in js), 1.0, ("send", HOPS[t], T["m%d%d" % (t + 1, h)][:, C * i:C * e], out), lat=K["hop"], sem="a%d%d%d" % (t + 1, h, i), val=NENG)
                return
            ls = [j for j in js if j < 2]
            if ls:
                i, e, n = ls[0], ls[-1] + 1, C * len(ls)
                act(ko, keys("OUT", ls), part("OUT", i, e), part("FIN", i, e), F.Copy, n=n, scale=2048.0, bias=2047.0)
            if 2 in js:
                ts(ko, keys("OUT", [2]), part("OUT", 2), part("FIN", 2), -ZO, None, A.add)
            for j in js:
                op(Y, keys("OUT", [j]), "y%d%d" % (j, h), 0.1, (lambda j: lambda q: q.dma_start((T.yd, T.yt, T.yz)[j][:, C * h:C * h + C], part("OUT", j)))(j), lat=2.2, sem="out%d" % (3 * h + j), val=16)
        for js in (SENDS if t < 3 else LAST):
            if js[0] < 2: refill([j for j in js if j < 2])
            finish(js)

    def proofs(t):
        hs, bank, n = range(NH_), newbank(), M // 16
        each = lambda k: " ".join(k + str(h) for h in hs)
        for h in hs:
            cp("VI2%d" % h, "VL%d" % h, B("VL", NC * h, NC * h + NC), B("VI2%d" % h, NC, 2 * NC), n=NC)
        op(TE, "LK TRI SEIq0 SEIq1 SEIq2 SEIq3 I512N ID %s %s %s" % (each("VL"), each("NG"), each("NH")), bank, ct(M, *[C] * (3 * NH_), *[64] * 16), mm(lambda: group(None, [
            (B("LK"), B("TRI"), pool(bank)[:, 0:M])] + [(sel(r, "SEI"), B("VL"), pool(bank)[:, r:M:16]) for r in range(16)] + [
            (w, y, pool(bank)[:, C * h:C * h + C]) for h in hs for w, y in ((B("I512N"), B("NG%d" % h, 0, C)), (B("I512N"), B("NG%d" % h, C, 2 * C)), (B("ID"), B("NH%d" % h)))])), get=bank)
        op(V, bank + " SP", "EP", cv(M), lambda q: q.tensor_scalar(B("EP"), pool(bank)[:, 0:M], 0.0, B("SP", 0, 1), A.is_equal, A.mult), put=bank)
        scan("EP RST0", "LS", B("LS"), B("RST0"), B("EP"), A.mult, A.max, n=M, k=.5)
        tt("LS " + each("VL"), "WO", B("WO"), B("LS", 15, M, 16), B("VL"), A.max, n=n)
        cp("WO", "OFW", B("OFW", 0, 2 * n, 2), B("WO"), n=n)
        for j in range(n):
            h, a = divmod(16 * j, C)
            ts("OFW TN%d scwd" % h, "scw", T.scw[:, 0:528].indirect(B("OFW", 2 * j, 2 * j + 1)), B("TN%d" % h, a, a + 16), 1.0, -1.0, A.mult, A.add, n=16, k=K["sca"])

    for t in range(4):
        now[1] = t
        for h in range(NH_):
            chunk(t, h)
        now[0] = NH_ - 1
        if t < 3:
            col = lambda n, j: B(n, j, j + 1)
            for h in range(0, NH_, 2):
                j = NH_ * t + h
                two = h + 1 < NH_
                ts("AS ACN%d%d" % (t, h) + (" ACN%d%d" % (t, h + 1) if two else ""), "AS", col("AS", 0), col("ACN", j), col("ACN", j + 1) if two else 0.0, col("AS", 0), A.add, A.add, n=1)
            cp("AS", "AI", col("AI", 0), col("AS", 0), n=1)
            ts("AI", "AI2", col("AI2", 0), col("AI", 0), 31, None, A.bitwise_and, n=1)
            ts("AI2 NTH", "NLIM", col("NLIM", 0), col("AI2", 0), -0.5, col("NTH", 0), A.mult, A.add, n=1)
            ts("BK NLIM", "CMb%d" % ((t + 1) % 2), B("CM%d" % ((t + 1) % 2), 128, 256), B("BK"), col("NLIM", 0), None, A.mult, n=128)
        proofs(t)
    op(Y, "scw", "ysd", 0.1, lambda q: q.dma_start(T.ys[:], T.scw[:, 0:512]), lat=2.5, sem="out%d" % (NOUT - 1), val=16)
    return ops


def depend(ops):
    last, readers = {}, {}
    for o in ops:
        o["d"] = {last[k] for k in o["r"] + o["w"] if k in last} | {i for k in o["w"] for i in readers.get(k, ())}
        for k in o["r"]:
            readers.setdefault(k, []).append(o["i"])
        for k in o["w"]:
            last[k] = o["i"]
            readers[k] = []
        o["d"].discard(o["i"])
        o["free"] = {j for j in o["d"] if ops[j]["e"] == o["e"] == "t"}
    return ops


def schedule(ops, off):
    n, wake = len(ops), K["wake"]
    succ = [[] for _ in ops]
    left = [0] * n
    for o in ops:
        for i in o["d"]:
            succ[i].append(o["i"]); left[o["i"]] += 1
    gap = lambda i, j: 0.0 if i in ops[j]["free"] else wake
    pri = [0.0] * n
    for o in reversed(ops):
        pri[o["i"]] = o["c"] + o["lat"] + max([pri[j] + gap(o["i"], j) for j in succ[o["i"]]] or [0.0])
    pri = [a + b for a, b in zip(pri, off)]
    free, bank, end, base, order = {}, {}, [0.0] * n, {}, []
    banks, given = [[0.0, None] for _ in range(NPOOL)], {}
    ready = [o["i"] for o in ops if not left[o["i"]]]
    def est(i):
        o = ops[i]
        x = max(free.get(o["e"], 0.0), base.get(i, 0.0))
        for k in o["b"]:
            e, tm = bank.get(k, ("", 0.0))
            if e != o["e"]: x = max(x, tm + wake)
        if o["get"]: x = max(x, min(p[0] for p in banks) + wake)
        return x
    while ready:
        ests = [(est(i), i) for i in ready]
        t0 = min(ests)[0]
        best = None
        for x, i in ests:
            if x <= t0 + 0.02 and (best is None or pri[i] > pri[best[1]]): best = (x, i)
        x, i = best
        o = ops[i]
        ready.remove(i)
        free[o["e"]] = x + o["c"]
        end[i] = x + o["c"] + o["lat"]
        for k in o["b"]: bank[k] = (o["e"], x + o["c"])
        if o["get"]:
            j = min(range(NPOOL), key=lambda j: banks[j][0])
            given[o["get"]] = j
            banks[j][0] = 1e9
        if o["put"]: banks[given[o["put"]]] = [x + o["c"], i]
        order.append(i)
        for j in succ[i]:
            base[j] = max(base.get(j, 0.0), end[i] + gap(i, j))
            left[j] -= 1
            if not left[j]: ready.append(j)
    return order, max(end)


def timer(ops):
    n, wake = len(ops), K["wake"]
    E, cost, lat = [o["e"] for o in ops], [o["c"] for o in ops], [o["lat"] for o in ops]
    anc, D = [0] * n, []
    for o in ops:
        far = 0
        for j in o["d"]: far |= anc[j]
        D.append([(j, 0.0 if j in o["free"] else wake) for j in o["d"] if not far >> j & 1])
        for j in o["d"]: far |= 1 << j
        anc[o["i"]] = far
    BK, get, put = [o["b"][0] if o["b"] else None for o in ops], [o["get"] for o in ops], [o["put"] for o in ops]
    def times(order, old=None, same=0):
        if old is None:
            end, why, res, given, before, marks, a = [0.0] * n, [-1] * n, [False] * n, {}, {}, [], 0
            last, banks = {}, [(0.0, -1, j) for j in range(NPOOL)]
        else:
            a = same // 32
            end, why, res, given, before, marks = old[0][:], old[1][:], old[2][:], dict(old[3]), dict(old[4]), old[5][:a]
            last, banks = dict(old[5][a][0]), old[5][a][1][:]
        for a in range(32 * a, n, 32):
            marks.append((dict(last), banks[:]))
            for i in order[a:a + 32]:
                x, w, r = 0.0, -1, False
                for j, g in D[i]:
                    if end[j] + g > x: x, w = end[j] + g, j
                e, k = E[i], BK[i]
                f = last.get(e)
                if f and f[0] > x: x, w, r = f[0], f[1], True
                if k:
                    f = last.get(k)
                    if f and f[2] != e and f[0] + wake > x: x, w, r = f[0] + wake, f[1], True
                if get[i]:
                    q = min(banks)
                    if q[0] > 1e8: return None
                    before[i] = q[1]
                    if q[1] >= 0 and q[0] + wake > x: x, w, r = q[0] + wake, q[1], True
                    given[get[i]] = q[2]
                    banks[q[2]] = (1e9, -1, q[2])
                y = x + cost[i]
                last[e] = f = (y, i, e)
                if k: last[k] = f
                elif put[i]: banks[given[put[i]]] = (y, i, given[put[i]])
                end[i], why[i], res[i] = y + lat[i], w, r
        return end, why, res, given, before, marks
    return times


def shift(ops, rng, rounds):
    kind = [(o["e"] + o["w"][0].rstrip("0123456789_") + str(round(o["c"], 2)), o["h"]) for o in ops]
    same = [[j for j, x in enumerate(kind) if x == k] for k in sorted(set(kind))]
    off = np.array([-K["lag"] * o["h"] for o in ops])
    order, cur = schedule(ops, list(off))
    for it in range(rounds):
        new = off.copy()
        if rng.random() < .5:
            new[same[rng.integers(len(same))]] += 3 * rng.normal()
        else:
            a = rng.integers(len(ops))
            new[a:a + (1, 5, 20, 60)[rng.integers(4)]] += 3 * rng.normal()
        p, x = schedule(ops, list(new))
        if x <= cur: off, cur, order = new, x, p
    return order


def swap(ops, order, rng, rounds, hot=0.15, cold=0.01):
    n, times = len(ops), timer(ops)
    pre, suc = [o["d"] for o in ops], [set() for _ in ops]
    for o in ops:
        for j in o["d"]: suc[j].add(o["i"])
    cur = times(order)
    c = best = max(cur[0])
    keep = order
    for it, (u, v, w, z) in enumerate(rng.random((rounds, 4)).tolist()):
        end, why, res = cur[:3]
        i, arcs = end.index(c), []
        while why[i] >= 0:
            if res[i]: arcs.append((why[i], i))
            i = why[i]
        j, i = arcs[int(u * len(arcs))]
        a, b, more = order.index(j), order.index(i), (0, 0, 0, 3, 10)[int(5 * w)]
        if v < .5:
            a = max(0, a - more)
            seg, S = order[a:b + 1], {i}
            for x in reversed(seg[:-1]):
                if suc[x] & S: S.add(x)
            if j in S: continue
            new = [x for x in seg if x in S] + [x for x in seg if x not in S]
        else:
            seg, S = order[a:b + 1 + more], {j}
            for x in seg[1:]:
                if pre[x] & S: S.add(x)
            if i in S: continue
            new = [x for x in seg if x not in S] + [x for x in seg if x in S]
        p = order[:a] + new + order[a + len(seg):]
        d = times(p, cur, a)
        if d is None: continue
        y = max(d[0])
        if y <= c or z < math.exp((c - y) / (hot * (cold / hot) ** (it / rounds))):
            order, cur, c = p, d, y
            if y < best: best, keep = y, p
    return keep


def plan(ops):
    if "order" in PLAN:
        return
    depend(ops)
    rng = np.random.default_rng(SEED)
    order = swap(ops, shift(ops, rng, ROUNDS[0]), rng, ROUNDS[1])
    end, _, _, given, before, _ = timer(ops)(order)
    deps, prev = [set(o["d"]) for o in ops], {}
    for i in order:
        o = ops[i]
        if before.get(i, -1) >= 0: deps[i].add(before[i])
        for k in o["b"]:
            p = prev.setdefault(k, {})
            for e, j in p.items():
                if e != o["e"]: deps[i].add(j)
            p[o["e"]] = i
    PLAN.update(order=order, time=max(end), bank=given, d=deps, end=end, free=[o["free"] for o in ops])


def rank_program(g, core, T, topo):
    rank = T.rank_of(core)
    if rank is None:
        return
    ops = build(T)
    plan(ops)
    queue = {"v": g.vector, "s": g.scalar, "t": g.tensor, "g": g, "y": g.sync}
    know = {e: {} for e in queue}
    count, clock = {}, {}
    sends = 0
    for i in PLAN["order"]:
        o = ops[i]
        e, q = o["e"], queue[o["e"]]
        kn = know[e]
        for j in sorted(PLAN["d"][i], key=lambda j: -clock[j][2]):
            if j in PLAN["free"][i]:
                continue
            s, v, _, c = clock[j]
            if kn.get(s, 0) < v:
                q.wait_ge(T.sem[s], v)
                for k, w in c.items():
                    if kn.get(k, 0) < w: kn[k] = w
                kn[s] = max(kn.get(s, 0), v)
        if isinstance(o["f"], tuple):
            _, hop, out, src = o["f"]
            dst = T.cores[(rank + hop) % N]
            rid, pid, _ = topo.addr(dst)
            mask = sum(1 << x for x in topo.engines(core, dst)[:NENG])
            g.remote_dma(out, src, T.sem[o["sem"]], T.sem.loc, pid, rid, mask)
            sends += NENG
            clock[i] = (o["sem"], o["val"], len(clock), {})
            continue
        x = o["f"](q)
        if o["sem"]:
            x.then_inc(T.sem[o["sem"]], o["val"])
            clock[i] = (o["sem"], o["val"], len(clock), dict(kn))
        else:
            count[e] = count.get(e, 0) + 1
            x.then_inc(T.sem[e], 1)
            clock[i] = (e, count[e], len(clock), dict(kn))
    for e, c in count.items():
        g.wait_ge(T.sem[e], c)
    for i in range(NLOAD):
        g.wait_ge(T.sem["l%d" % i], 16)
    for i in range(NOUT):
        g.wait_ge(T.sem["out%d" % i], 16)
    g.wait_ge(T.sem.loc, sends)
    for s in SEMAPHORES:
        if s[0] == "k": g.wait_ge(T.sem[s], 16)
    for s in SEMAPHORES:
        if s[0] == "a": g.wait_ge(T.sem[s], NENG)
